import numpy as np
import ml_dtypes


def mxq(x, axis, fmt="e4m3"):
    dtype, down = {"e4m3": (ml_dtypes.float8_e4m3fn, 7), "e5m2": (ml_dtypes.float8_e5m2, 14)}[fmt]
    v = np.moveaxis(np.asarray(x, np.float32).astype(ml_dtypes.bfloat16).astype(np.float64), axis, -1)
    blocks = v.reshape(v.shape[:-1] + (-1, 32))
    amax = np.abs(blocks).max(-1, keepdims=True)
    byte = np.maximum(np.where(amax > 0, np.frexp(amax)[1] - 1 + 127, 0) - down, 1)
    scale = np.exp2(byte - 127.0)
    codes = (blocks / scale).astype(np.float32).astype(dtype).astype(np.float64)
    return np.moveaxis((codes * scale).reshape(v.shape), -1, axis)


WIDE = False


def mx_kscale(k):
    if not WIDE:
        return np.ones(k)
    levels = np.array([10, -10, 5, -5, 0])
    if k % 512:
        return np.exp2(np.random.permutation(np.resize(levels, k // 32))).repeat(32)
    a = np.empty((k // 512, 16))
    for p in range(k // 512):
        a[p, :8] = np.random.permutation(np.resize(levels, 8))
        for g in range(8):
            far = levels[np.abs(levels - a[p, g]) >= 10]
            a[p, g + 8] = far[np.random.randint(len(far))]
    return np.exp2(a.ravel()).repeat(32)


def f64(x):
    return np.asarray(x).astype(np.float64)


def striped(idx):
    return np.tile(idx.reshape(-1, 16).T, (8, 1)).astype(np.uint16)


def unstriped(offs):
    return offs[:16].T.reshape(-1).astype(np.int64)


def striped8(idx):
    return np.concatenate([x.reshape(-1, 16).T for x in idx]).astype(np.uint16)


def runs(offs, k):
    lists = np.stack([offs[16 * r : 16 * r + 16].T.reshape(-1) for r in range(8)]).astype(np.int64)
    return lists[np.arange(k) % 512 // 64]


def pack_weight(w):
    k, n = w.shape
    w = f64(np.asarray(w, np.float32).astype(ml_dtypes.bfloat16)).reshape(k // 32, 32, n)
    amax = np.abs(w).max(1)
    byte = np.clip(np.where(amax > 0, np.frexp(amax)[1] - 1 + 127 - 7, 1), 1, 254)
    scaled = (w * np.exp2(127.0 - byte)[:, None, :]).reshape(k, n).astype(np.float32)
    words = np.ascontiguousarray(scaled.reshape(k // 512, 128, 4, n).transpose(0, 1, 3, 2)).astype(ml_dtypes.float8_e4m3fn).view(np.uint8)
    return words, np.ascontiguousarray(byte.astype(np.uint8).reshape(k // 512, 16, n))


def unpack_weight(words, scales):
    g, p, n, _ = words.shape
    vals = np.ascontiguousarray(words).view(ml_dtypes.float8_e4m3fn).astype(np.float64) * np.repeat(np.exp2(scales.astype(np.float64) - 127.0), 8, axis=1)[..., None]
    return vals.transpose(0, 1, 3, 2).reshape(g * 512, n)


def sigmoid(v):
    return 1.0 / (1.0 + np.exp(-np.maximum(v, -700.0)))

def planes(y):
    n, m = y.shape
    v = y.astype(np.float32).astype(ml_dtypes.bfloat16).astype(np.float64).reshape(n // 32, 32, m)
    top = np.abs(v).max(1)
    byte = np.clip(np.where(top > 0, np.frexp(top)[1] - 1 + 127 - 7, 1), 1, 254)
    codes = (v * np.exp2(127.0 - byte)[:, None, :]).reshape(n, m).astype(np.float32).astype(ml_dtypes.float8_e4m3fn).view(np.uint8)
    words = codes.reshape(n // 512, 128, 4, m).transpose(0, 1, 3, 2)
    return np.ascontiguousarray(words), np.ascontiguousarray(byte.astype(np.uint8).reshape(n // 512, 16, m))


K, T, S, N, H = 512, 2048, 512, 512, 512


def setup_inputs():
    n = np.random.standard_normal
    s = mx_kscale(K)[:, None]
    u = mx_kscale(H)
    packed_xT = pack_weight(n((K, T)) * s)
    packed_w1 = pack_weight(n((K, H)) / np.sqrt(K) / s)
    packed_w2 = pack_weight(n((K, H)) / np.sqrt(K) / s)
    packed_w3 = pack_weight(n((H, N)) / np.sqrt(2 * H) / u[:, None])
    packed_w4 = pack_weight(n((H, N)) / np.sqrt(2 * H) / u[:, None])
    return {
        "x_words": packed_xT[0],
        "x_scales": packed_xT[1],
        "w1_words": packed_w1[0],
        "w1_scales": packed_w1[1],
        "w2_words": packed_w2[0],
        "w2_scales": packed_w2[1],
        "g1": (np.random.uniform(0.5, 1.5, (H, 1)) * u[:, None]).astype(np.float32),
        "g2": (np.random.uniform(0.5, 1.5, (H, 1)) * u[:, None]).astype(np.float32),
        "w3_words": packed_w3[0],
        "w3_scales": packed_w3[1],
        "w4_words": packed_w4[0],
        "w4_scales": packed_w4[1],
        "offs": striped(np.random.permutation(T)[:S]),
        "west": striped8(np.stack([np.random.permutation(S) for _ in range(8)])),
        "east": striped8(np.stack([np.random.permutation(S) for _ in range(8)])),
    }


def reference(x_words, x_scales, w1_words, w1_scales, w2_words, w2_scales, g1, g2, w3_words, w3_scales, w4_words, w4_scales, offs, west, east):
    xq = unpack_weight(x_words, x_scales)[:, unstriped(offs)]
    y = sigmoid(unpack_weight(w1_words, w1_scales).T @ xq)
    e = sigmoid(unpack_weight(w2_words, w2_scales).T @ xq)
    re = y * ((e) ** 2)
    z = f64(g1) * (y + 0.25 * (y[np.arange(H)[:, None], runs(west, H)] + y[np.arange(H)[:, None], runs(east, H)] - (2.0 * y)) - re + 0.125 * (-1.0 * y + 1))
    z2 = f64(g2) * (e + 0.125 * (e[np.arange(H)[:, None], runs(west, H)] + e[np.arange(H)[:, None], runs(east, H)] - (2.0 * e)) + re - (0.25 * e))
    out_0 = unpack_weight(w3_words, w3_scales).T @ mxq(z, 0, "e4m3") + unpack_weight(w4_words, w4_scales).T @ mxq(z2, 0, "e4m3")
    return (out_0,) + planes(out_0)

@@ -1,0 +1,241 @@
+from contextlib import ExitStack
+
+import concourse.mybir as mybir
+from concourse.masks import make_identity
+
+K, T, S, N, H = 512, 2048, 512, 512, 512
+FLOPS = 4 * 2 * 512 * 512 * 512
+
+F32 = mybir.dt.float32
+BF16 = mybir.dt.bfloat16
+I32 = mybir.dt.int32
+U32 = mybir.dt.uint32
+U16 = mybir.dt.uint16
+U8 = mybir.dt.uint8
+FP8X4 = mybir.dt.float8_e4m3fn_x4
+ALU = mybir.AluOpType
+ACT = mybir.ActivationFunctionType
+
+P = 128
+PACK = 4
+HALF = 256
+LOGIT_V = 2
+OW_S = 0
+ZW_S = 0
+
+
+def tile_picked_grayscott_none_po_kernel(
+    tc, x_words, x_scales, w1_words, w1_scales, w2_words, w2_scales, g1, g2,
+    w3_words, w3_scales, w4_words, w4_scales, offs, west, east, out_0, out_1, out_2,
+):
+    nc = tc.nc
+
+    def words_of(dram):
+        return dram[0].rearrange("p n t -> p (n t)").bitcast(I32)
+
+    def load_scale_rows(queues, plane, first_row, dram):
+        for q in range(4):
+            r = 32 * q + first_row
+            queues[q].dma_start(out=plane[r : r + 4, :].bitcast(I32), in_=dram[0, 4 * q : 4 * q + 4, :].bitcast(I32))
+
+    with ExitStack() as ctx:
+        keep = ctx.enter_context(tc.tile_pool(name="keep", bufs=1))
+        ring = ctx.enter_context(tc.tile_pool(name="ring", bufs=2))
+        psum = ctx.enter_context(tc.psum_pool(name="psum", bufs=8))
+
+        offs_t = keep.tile([P, S // 16], U16, name="offs_t")
+        west_t = keep.tile([P, S // 16], U16, name="west_t")
+        east_t = keep.tile([P, S // 16], U16, name="east_t")
+        xw = keep.tile([P, T], I32, name="xw", align_bytes=64)
+        xs = keep.tile([P, T], U8, name="xs", align_bytes=64)
+        s12_raw = keep.tile([P, H], U8, name="s12_raw", align_bytes=64)
+        s34_raw = keep.tile([P, N], U8, name="s34_raw", align_bytes=64)
+        g1_t = keep.tile([P, PACK], F32, name="g1_t")
+        g2_t = keep.tile([P, PACK], F32, name="g2_t")
+
+        xs_rows = keep.tile([P, T], U8, name="xs_rows", align_bytes=64)
+        ident = keep.tile([P, P], F32, name="ident")
+        make_identity(nc, ident[:])
+        nc.vector.memset(s12_raw[:].bitcast(I32), 0)
+        nc.vector.memset(xs[:].bitcast(I32), 0)
+
+        nc.sync.dma_start(offs_t[:], offs)
+        load_scale_rows([nc.sync] * 4, xs_rows, 0, x_scales)
+        nc.sync.dma_start(out=xw[:], in_=words_of(x_words))
+        w1_raw = ring.tile([P, H], I32, name="w_raw", align_bytes=64)
+        nc.sync.dma_start(out=w1_raw[:], in_=words_of(w1_words))
+        w2_raw = ring.tile([P, H], I32, name="w_raw", align_bytes=64)
+        nc.sync.dma_start(out=w2_raw[:], in_=words_of(w2_words))
+        load_scale_rows([nc.sync] * 4, s12_raw, 0, w1_scales)
+        load_scale_rows([nc.sync] + [nc.gpsimd] * 3, s12_raw, 4, w2_scales)
+        nc.sync.dma_start(west_t[:], west)
+        nc.sync.dma_start(east_t[:], east)
+        nc.gpsimd.dma_start(out=g2_t[:], in_=g2.rearrange("(p t) o -> p (t o)", t=PACK))
+        nc.gpsimd.dma_start(out=g1_t[:], in_=g1.rearrange("(p t) o -> p (t o)", t=PACK))
+        nc.gpsimd.memset(s34_raw[:].bitcast(I32), 0)
+        for q in range(4):
+            rows = slice(32 * q, 32 * q + 4)
+            nc.vector.tensor_copy(out=xs[rows, :].bitcast(I32), in_=xs_rows[rows, :].bitcast(I32))
+
+        def deal(engine, raw, dtype, name):
+            dealt = keep.tile([P, H], dtype, name=name, align_bytes=64)
+            engine.tensor_copy(
+                out=dealt[:].rearrange("p (t m) -> p m t", t=PACK), in_=raw[:].rearrange("p (m t) -> p m t", t=PACK)
+            )
+            return dealt
+
+        xs_g = keep.tile([P, S], U8, name="xs_g", align_bytes=64)
+        nc.vector.tensor_copy(out=xs_g[:], in_=xs[:].indirect(offs_t[:]))
+        xw_g = keep.tile([P, S], U32, name="xw_g", align_bytes=64)
+        nc.vector.tensor_copy(out=xw_g[:], in_=xw[:].bitcast(U32).indirect(offs_t[:]))
+
+        w1 = deal(nc.vector, w1_raw, I32, "w1")
+        w2 = deal(nc.vector, w2_raw, I32, "w2")
+        s12 = deal(nc.vector, s12_raw, U8, "s12")
+        w3_raw = ring.tile([P, H], I32, name="w_raw", align_bytes=64)
+        nc.sync.dma_start(out=w3_raw[:], in_=words_of(w3_words))
+        w4_raw = ring.tile([P, H], I32, name="w_raw", align_bytes=64)
+        nc.sync.dma_start(out=w4_raw[:], in_=words_of(w4_words))
+        load_scale_rows([nc.sync] * 4, s34_raw, 0, w3_scales)
+        load_scale_rows([nc.sync] * 4, s34_raw, 4, w4_scales)
+        w3 = deal(nc.gpsimd, w3_raw, I32, "w3")
+        w4 = deal(nc.gpsimd, w4_raw, I32, "w4")
+        s34 = deal(nc.gpsimd, s34_raw, U8, "s34")
+
+        g2_8 = keep.tile([P, PACK], F32, name="g2_8")
+        nc.scalar.activation(out=g2_8[:], in_=g2_t[:], func=ACT.Copy, scale=0.125)
+        logits, ews, a_negs, bs = [], [], [], []
+
+        def react(t):
+            cols = slice(P * t, P * (t + 1))
+            acc_y = psum.tile([P, S], F32, name="bank")
+            nc.tensor.matmul_mx(out=acc_y[:], lhsT=w1[:, cols].bitcast(FP8X4), lhsT_scale=s12[:, cols],
+                                rhs=xw_g[:].bitcast(FP8X4), rhs_scale=xs_g[:], start=True, stop=True)
+            acc_e = psum.tile([P, S], F32, name="bank")
+            nc.tensor.matmul_mx(out=acc_e[:], lhsT=w2[:, cols].bitcast(FP8X4), lhsT_scale=s12[4:P, cols],
+                                rhs=xw_g[:].bitcast(FP8X4), rhs_scale=xs_g[:], start=True, stop=True)
+            logit = keep.tile([P, S], F32, name="logit%d" % t)
+            y = ring.tile([P, S], F32, name="y")
+            e = ring.tile([P, S], F32, name="e")
+            q4 = ring.tile([P, S], F32, name="q4")
+            u8 = ring.tile([P, S], F32, name="u8")
+            ew = keep.tile([P, S], F32, name="ew%d" % t)
+            a_neg = keep.tile([P, S], F32, name="a_neg%d" % t)
+            b = keep.tile([P, S], F32, name="b%d" % t)
+            nc.scalar.activation(out=y[:], in_=acc_y[:], func=ACT.Sigmoid)
+            nc.scalar.activation(out=e[:], in_=acc_e[:], func=ACT.Sigmoid)
+            if t < LOGIT_V:
+                nc.vector.tensor_copy(out=logit[:], in_=acc_y[:])
+            nc.scalar.activation(out=ew[:], in_=e[:], func=ACT.Copy, scale=g2_8[:, t : t + 1])
+            nc.scalar.activation(out=q4[:], in_=e[:], func=ACT.Square, scale=2.0)
+            if t >= LOGIT_V:
+                nc.scalar.copy(out=logit[:], in_=acc_y[:])
+            nc.vector.scalar_tensor_tensor(out=u8[:], in0=y[:], scalar=8.0, in1=e[:], op0=ALU.mult, op1=ALU.mult)
+            nc.vector.scalar_tensor_tensor(out=b[:], in0=u8[:], scalar=4.0, in1=ew[:], op0=ALU.add, op1=ALU.mult)
+            nc.vector.scalar_tensor_tensor(out=a_neg[:], in0=q4[:], scalar=1.5, in1=y[:], op0=ALU.subtract, op1=ALU.mult)
+            logits.append(logit)
+            ews.append(ew)
+            a_negs.append(a_neg)
+            bs.append(b)
+
+        z2_rows = [keep.tile([P, PACK, HALF], F32, name="z2_rows%d" % h) for h in range(2)]
+
+        def diffuse_e(t, h):
+            js = slice(HALF * h, HALF * (h + 1))
+            ls = slice(HALF * h // 16, HALF * (h + 1) // 16)
+            e1 = ring.tile([P, HALF], F32, name="e1")
+            nc.vector.tensor_tensor(e1[:], ews[t][:].indirect(west_t[:, ls]), bs[t][:, js], ALU.add)
+            nc.vector.tensor_tensor(z2_rows[h][:, t, :], ews[t][:].indirect(east_t[:, ls]), e1[:], ALU.add)
+
+        word_banks = {}
+
+        def diffuse_y(u, h):
+            ls = slice(HALF * h // 16, HALF * (h + 1) // 16)
+            sums = psum.tile([P, 2, 2, P], F32, name="bank")
+            for r in range(2):
+                t = 2 * u + r
+                n_w = ring.tile([P, HALF], F32, name="n_w", bufs=3)
+                n_e = ring.tile([P, HALF], F32, name="n_e", bufs=3)
+                nc.scalar.activation(out=n_w[:], in_=logits[t][:].indirect(west_t[:, ls]), func=ACT.Sigmoid, scale=-1.0)
+                nc.scalar.activation(out=n_e[:], in_=logits[t][:].indirect(east_t[:, ls]), func=ACT.Sigmoid, scale=-1.0)
+                for q in range(2):
+                    j0 = HALF * h + P * q
+                    terms = (a_negs[t][:, j0 : j0 + P], n_w[:, P * q : P * (q + 1)], n_e[:, P * q : P * (q + 1)])
+                    for i, term in enumerate(terms):
+                        nc.tensor.matmul(sums[:, q, r, :], term, ident[:], is_transpose=True, start=(i == 0), stop=(i == 2))
+            for q in range(2):
+                pairs = ring.tile([P, P, 2], BF16, name="pairs", bufs=4)
+                nc.vector.scalar_tensor_tensor(out=pairs[:], in0=sums[:, q].rearrange("j e p -> j p e"), scalar=2.5,
+                                               in1=g1_row[:, u], op0=ALU.subtract, op1=ALU.mult)
+                if u == 0:
+                    word_banks[(h, q)] = psum.tile([P, 2, P], F32, name="bank")
+                nc.tensor.transpose(word_banks[(h, q)][:, u, :], pairs[:].rearrange("j p e -> j (p e)").bitcast(F32), ident[:])
+
+        out_rows = out_0.rearrange("(p t) j -> p t j", t=PACK)
+        o_words = keep.tile([P, S], I32, name="o_words", align_bytes=64)
+        o_scales = keep.tile([P, S], U8, name="o_scales", align_bytes=64)
+
+        def quantise(woven, w, nm):
+            c = ring.tile([P, w], U32, name=nm + "_codes", align_bytes=64)
+            s = ring.tile([P, w], U8, name=nm + "_scales", align_bytes=64)
+            nc.vector.quantize_mx(out=c[:].bitcast(FP8X4), scales=s[:], in_=woven)
+            return c, s
+
+        def project(h, qs):
+            w = P * len(qs)
+            j0 = HALF * h + P * qs[0]
+            js = slice(j0, j0 + w)
+            z2_woven = ring.tile([P, w, PACK], BF16, name="z2_woven", align_bytes=64)
+            if h < ZW_S:
+                nc.scalar.copy(out=z2_woven[:], in_=z2_rows[h][:, :, P * qs[0] : P * qs[0] + w].rearrange("p t j -> p j t"))
+            else:
+                nc.vector.tensor_copy(out=z2_woven[:], in_=z2_rows[h][:, :, P * qs[0] : P * qs[0] + w].rearrange("p t j -> p j t"))
+            z_woven = ring.tile([P, w * PACK], BF16, name="z_woven", align_bytes=64)
+            z_words = z_woven[:].bitcast(F32).rearrange("p (j u) -> p j u", u=2)
+            for i, q in enumerate(qs):
+                nc.scalar.copy(out=z_words[:, P * i : P * (i + 1), :], in_=word_banks[(h, q)][:].rearrange("p u j -> p j u"))
+            z2_c, z2_s = quantise(z2_woven[:].rearrange("p j t -> p (j t)"), w, "z2")
+            z_c, z_s = quantise(z_woven[:], w, "z")
+            o_f32 = ring.tile([P, PACK, w], F32, name="o_f32", bufs=3)
+            per_bank = S // w
+            for b0 in range(0, PACK, per_bank):
+                acc = psum.tile([P, per_bank, w], F32, name="bank")
+                for r in range(per_bank):
+                    cols = slice(P * (b0 + r), P * (b0 + r + 1))
+                    nc.tensor.matmul_mx(out=acc[:, r, :], lhsT=w4[:, cols].bitcast(FP8X4), lhsT_scale=s34[4:P, cols],
+                                        rhs=z2_c[:].bitcast(FP8X4), rhs_scale=z2_s[:], start=True, stop=False)
+                    nc.tensor.matmul_mx(out=acc[:, r, :], lhsT=w3[:, cols].bitcast(FP8X4), lhsT_scale=s34[:, cols],
+                                        rhs=z_c[:].bitcast(FP8X4), rhs_scale=z_s[:], start=False, stop=True)
+                nc.scalar.copy(out=o_f32[:, b0 : b0 + per_bank, :], in_=acc[:])
+            nc.sync.dma_start(out=out_rows[:, :, js], in_=o_f32[:])
+            o_woven = ring.tile([P, w, PACK], BF16, name="o_woven", align_bytes=64)
+            if h < OW_S:
+                nc.scalar.copy(out=o_woven[:], in_=o_f32[:].rearrange("p t j -> p j t"))
+            else:
+                nc.vector.tensor_copy(out=o_woven[:], in_=o_f32[:].rearrange("p t j -> p j t"))
+            nc.vector.quantize_mx(out=o_words[:, js].bitcast(FP8X4), scales=o_scales[:, js],
+                                  in_=o_woven[:].rearrange("p j t -> p (j t)"))
+            nc.sync.dma_start(out=words_of(out_1)[:, js], in_=o_words[:, js])
+
+        for t in range(PACK):
+            react(t)
+            diffuse_e(t, 0)
+        g_bank = psum.tile([P, 2, 2, P], F32, name="bank")
+        for t in range(PACK):
+            nc.tensor.transpose(g_bank[:, t // 2, t % 2, :], g1_t[:, t : t + 1].to_broadcast([P, P]), ident[:])
+        g1_row = keep.tile([P, 2, P, 2], F32, name="g1_row")
+        nc.scalar.activation(out=g1_row[:], in_=g_bank[:].rearrange("j u e p -> j u p e"), func=ACT.Copy, scale=-0.25)
+
+        diffuse_y(0, 0)
+        diffuse_y(1, 0)
+        diffuse_e(0, 1)
+        diffuse_y(0, 1)
+        diffuse_e(1, 1)
+        project(0, [0, 1])
+        diffuse_e(2, 1)
+        diffuse_y(1, 1)
+        diffuse_e(3, 1)
+        project(1, [0])
+        project(1, [1])
+        for q in range(4):
+            nc.sync.dma_start(out=out_2[0, 4 * q : 4 * q + 4, :].bitcast(I32), in_=o_scales[32 * q : 32 * q + 4, :].bitcast(I32))

@@ -20,8 +20,16 @@ P = 128
 PACK = 4
 HALF = 256
 LOGIT_V = 2
-OW_S = 0
-ZW_S = 0
+OW_S = []
+ZW_S = []
+DEALS = [(0, 1), (1, 4)]
+N_BUFS = 3
+ZC_V = []
+WHOLE = [(0, 512)]
+THIRDS = [(0, 256), (256, 128), (384, 128)]
+HALVES = [(0, 256), (256, 256)]
+Y_PIECES = [WHOLE, WHOLE, WHOLE, HALVES]
+E_PIECES = [WHOLE, WHOLE, WHOLE, HALVES]
 
 
 def tile_picked_grayscott_none_po_kernel(
@@ -33,8 +41,8 @@ def tile_picked_grayscott_none_po_kernel(
     def words_of(dram):
         return dram[0].rearrange("p n t -> p (n t)").bitcast(I32)
 
-    def load_scale_rows(queues, plane, first_row, dram):
-        for q in range(4):
+    def load_scale_rows(queues, plane, first_row, dram, quadrants=range(4)):
+        for q in quadrants:
             r = 32 * q + first_row
             queues[q].dma_start(out=plane[r : r + 4, :].bitcast(I32), in_=dram[0, 4 * q : 4 * q + 4, :].bitcast(I32))
 
@@ -48,31 +56,31 @@ def tile_picked_grayscott_none_po_kernel(
         east_t = keep.tile([P, S // 16], U16, name="east_t")
         xw = keep.tile([P, T], I32, name="xw", align_bytes=64)
         xs = keep.tile([P, T], U8, name="xs", align_bytes=64)
-        s12_raw = keep.tile([P, H], U8, name="s12_raw", align_bytes=64)
-        s34_raw = keep.tile([P, N], U8, name="s34_raw", align_bytes=64)
+        s_raw = keep.tile([P, H], U8, name="s_raw", align_bytes=64)
         g1_t = keep.tile([P, PACK], F32, name="g1_t")
         g2_t = keep.tile([P, PACK], F32, name="g2_t")
-
         xs_rows = keep.tile([P, T], U8, name="xs_rows", align_bytes=64)
+        w_raw = [keep.tile([P, H], I32, name="w_raw%d" % i, align_bytes=64) for i in range(4)]
         ident = keep.tile([P, P], F32, name="ident")
-        make_identity(nc, ident[:])
-        nc.vector.memset(s12_raw[:].bitcast(I32), 0)
+
+        nc.gpsimd.memset(s_raw[:].bitcast(I32), 0)
         nc.vector.memset(xs[:].bitcast(I32), 0)
 
         nc.sync.dma_start(offs_t[:], offs)
         load_scale_rows([nc.sync] * 4, xs_rows, 0, x_scales)
+        load_scale_rows([nc.sync] * 2, s_raw, 0, w1_scales, [0, 1])
         nc.sync.dma_start(out=xw[:], in_=words_of(x_words))
-        w1_raw = ring.tile([P, H], I32, name="w_raw", align_bytes=64)
-        nc.sync.dma_start(out=w1_raw[:], in_=words_of(w1_words))
-        w2_raw = ring.tile([P, H], I32, name="w_raw", align_bytes=64)
-        nc.sync.dma_start(out=w2_raw[:], in_=words_of(w2_words))
-        load_scale_rows([nc.sync] * 4, s12_raw, 0, w1_scales)
-        load_scale_rows([nc.sync] + [nc.gpsimd] * 3, s12_raw, 4, w2_scales)
+        nc.sync.dma_start(out=w_raw[0][:], in_=words_of(w1_words))
+        nc.sync.dma_start(out=w_raw[1][:], in_=words_of(w2_words))
+        load_scale_rows([nc.sync] * 4, s_raw, 0, w1_scales, [2, 3])
+        load_scale_rows([nc.sync] * 3 + [nc.gpsimd], s_raw, 4, w2_scales)
+        make_identity(nc, ident[:])
+        nc.gpsimd.dma_start(out=g1_t[:], in_=g1.rearrange("(p t) o -> p (t o)", t=PACK))
+        nc.sync.dma_start(out=w_raw[2][:], in_=words_of(w3_words))
+        nc.sync.dma_start(out=w_raw[3][:], in_=words_of(w4_words))
+        nc.sync.dma_start(out=g2_t[:], in_=g2.rearrange("(p t) o -> p (t o)", t=PACK))
         nc.sync.dma_start(west_t[:], west)
         nc.sync.dma_start(east_t[:], east)
-        nc.gpsimd.dma_start(out=g2_t[:], in_=g2.rearrange("(p t) o -> p (t o)", t=PACK))
-        nc.gpsimd.dma_start(out=g1_t[:], in_=g1.rearrange("(p t) o -> p (t o)", t=PACK))
-        nc.gpsimd.memset(s34_raw[:].bitcast(I32), 0)
         for q in range(4):
             rows = slice(32 * q, 32 * q + 4)
             nc.vector.tensor_copy(out=xs[rows, :].bitcast(I32), in_=xs_rows[rows, :].bitcast(I32))
@@ -89,22 +97,27 @@ def tile_picked_grayscott_none_po_kernel(
         xw_g = keep.tile([P, S], U32, name="xw_g", align_bytes=64)
         nc.vector.tensor_copy(out=xw_g[:], in_=xw[:].bitcast(U32).indirect(offs_t[:]))
 
-        w1 = deal(nc.vector, w1_raw, I32, "w1")
-        w2 = deal(nc.vector, w2_raw, I32, "w2")
-        s12 = deal(nc.vector, s12_raw, U8, "s12")
-        w3_raw = ring.tile([P, H], I32, name="w_raw", align_bytes=64)
-        nc.sync.dma_start(out=w3_raw[:], in_=words_of(w3_words))
-        w4_raw = ring.tile([P, H], I32, name="w_raw", align_bytes=64)
-        nc.sync.dma_start(out=w4_raw[:], in_=words_of(w4_words))
-        load_scale_rows([nc.sync] * 4, s34_raw, 0, w3_scales)
-        load_scale_rows([nc.sync] * 4, s34_raw, 4, w4_scales)
-        w3 = deal(nc.gpsimd, w3_raw, I32, "w3")
-        w4 = deal(nc.gpsimd, w4_raw, I32, "w4")
-        s34 = deal(nc.gpsimd, s34_raw, U8, "s34")
+        s12 = keep.tile([P, H], U8, name="s_dealt", align_bytes=64)
+        w1 = keep.tile([P, H], I32, name="w1", align_bytes=64)
+        w2 = keep.tile([P, H], I32, name="w2", align_bytes=64)
+        for t0, t1 in DEALS:
+            for raw, dealt in ((s_raw, s12), (w_raw[0], w1), (w_raw[1], w2)):
+                nc.vector.tensor_copy(out=dealt[:].rearrange("p (t m) -> p m t", t=PACK)[:, :, t0:t1],
+                                      in_=raw[:].rearrange("p (m t) -> p m t", t=PACK)[:, :, t0:t1])
+        w3 = deal(nc.vector, w_raw[2], I32, "w3")
+        w4 = deal(nc.vector, w_raw[3], I32, "w4")
+        load_scale_rows([nc.sync] * 4, s_raw, 8, w3_scales)
+        load_scale_rows([nc.sync] * 4, s_raw, 12, w4_scales)
 
         g2_8 = keep.tile([P, PACK], F32, name="g2_8")
         nc.scalar.activation(out=g2_8[:], in_=g2_t[:], func=ACT.Copy, scale=0.125)
-        logits, ews, a_negs, bs = [], [], [], []
+        g_bank = psum.tile([P, 2, 2, P], F32, name="bank")
+        for t in range(PACK):
+            nc.tensor.transpose(g_bank[:, t // 2, t % 2, :], g1_t[:, t : t + 1].to_broadcast([P, P]), ident[:])
+        g1_row = keep.tile([P, 2, P, 2], F32, name="g1_row")
+        nc.scalar.activation(out=g1_row[:], in_=g_bank[:].rearrange("j u e p -> j u p e"), func=ACT.Copy, scale=-0.25)
+
+        y_wins, e_wins, a_negs, bs = [], [], [], []
 
         def react(t):
             cols = slice(P * t, P * (t + 1))
@@ -114,62 +127,79 @@ def tile_picked_grayscott_none_po_kernel(
             acc_e = psum.tile([P, S], F32, name="bank")
             nc.tensor.matmul_mx(out=acc_e[:], lhsT=w2[:, cols].bitcast(FP8X4), lhsT_scale=s12[4:P, cols],
                                 rhs=xw_g[:].bitcast(FP8X4), rhs_scale=xs_g[:], start=True, stop=True)
-            logit = keep.tile([P, S], F32, name="logit%d" % t)
-            y = ring.tile([P, S], F32, name="y")
-            e = ring.tile([P, S], F32, name="e")
+            if min(w for j0, w in Y_PIECES[t]) >= HALF:
+                y_win = keep.tile([P, 2 * S], F32, name="y_win%d" % t)
+                logit, y = y_win[:, 0:S], y_win[:, S : 2 * S]
+            else:
+                y_win = keep.tile([P, S], F32, name="y_win%d" % t)
+                y_own = keep.tile([P, S], F32, name="y_own%d" % t)
+                logit, y = y_win[:], y_own[:]
+            if min(w for j0, w in E_PIECES[t]) >= HALF:
+                e_win = keep.tile([P, 2 * S], F32, name="e_win%d" % t)
+                ew, e = e_win[:, 0:S], e_win[:, S : 2 * S]
+            else:
+                e_win = keep.tile([P, S], F32, name="e_win%d" % t)
+                e_own = keep.tile([P, S], F32, name="e_own%d" % t)
+                ew, e = e_win[:], e_own[:]
             q4 = ring.tile([P, S], F32, name="q4")
             u8 = ring.tile([P, S], F32, name="u8")
-            ew = keep.tile([P, S], F32, name="ew%d" % t)
             a_neg = keep.tile([P, S], F32, name="a_neg%d" % t)
             b = keep.tile([P, S], F32, name="b%d" % t)
-            nc.scalar.activation(out=y[:], in_=acc_y[:], func=ACT.Sigmoid)
-            nc.scalar.activation(out=e[:], in_=acc_e[:], func=ACT.Sigmoid)
+            nc.scalar.activation(out=y, in_=acc_y[:], func=ACT.Sigmoid)
+            nc.scalar.activation(out=e, in_=acc_e[:], func=ACT.Sigmoid)
             if t < LOGIT_V:
-                nc.vector.tensor_copy(out=logit[:], in_=acc_y[:])
-            nc.scalar.activation(out=ew[:], in_=e[:], func=ACT.Copy, scale=g2_8[:, t : t + 1])
-            nc.scalar.activation(out=q4[:], in_=e[:], func=ACT.Square, scale=2.0)
+                nc.vector.tensor_copy(out=logit, in_=acc_y[:])
+            nc.scalar.activation(out=ew, in_=e, func=ACT.Copy, scale=g2_8[:, t : t + 1])
+            nc.scalar.activation(out=q4[:], in_=e, func=ACT.Square, scale=2.0)
             if t >= LOGIT_V:
-                nc.scalar.copy(out=logit[:], in_=acc_y[:])
-            nc.vector.scalar_tensor_tensor(out=u8[:], in0=y[:], scalar=8.0, in1=e[:], op0=ALU.mult, op1=ALU.mult)
-            nc.vector.scalar_tensor_tensor(out=b[:], in0=u8[:], scalar=4.0, in1=ew[:], op0=ALU.add, op1=ALU.mult)
-            nc.vector.scalar_tensor_tensor(out=a_neg[:], in0=q4[:], scalar=1.5, in1=y[:], op0=ALU.subtract, op1=ALU.mult)
-            logits.append(logit)
-            ews.append(ew)
+                nc.scalar.copy(out=logit, in_=acc_y[:])
+            nc.vector.scalar_tensor_tensor(out=u8[:], in0=y, scalar=8.0, in1=e, op0=ALU.mult, op1=ALU.mult)
+            nc.vector.scalar_tensor_tensor(out=b[:], in0=u8[:], scalar=4.0, in1=ew, op0=ALU.add, op1=ALU.mult)
+            nc.vector.scalar_tensor_tensor(out=a_neg[:], in0=q4[:], scalar=1.5, in1=y, op0=ALU.subtract, op1=ALU.mult)
+            y_wins.append(y_win)
+            e_wins.append(e_win)
             a_negs.append(a_neg)
             bs.append(b)
 
-        z2_rows = [keep.tile([P, PACK, HALF], F32, name="z2_rows%d" % h) for h in range(2)]
+        z2_rows = keep.tile([P, PACK * S], F32, name="z2_all")
 
-        def diffuse_e(t, h):
-            js = slice(HALF * h, HALF * (h + 1))
-            ls = slice(HALF * h // 16, HALF * (h + 1) // 16)
-            e1 = ring.tile([P, HALF], F32, name="e1")
-            nc.vector.tensor_tensor(e1[:], ews[t][:].indirect(west_t[:, ls]), bs[t][:, js], ALU.add)
-            nc.vector.tensor_tensor(z2_rows[h][:, t, :], ews[t][:].indirect(east_t[:, ls]), e1[:], ALU.add)
+        def diffuse_e(t, k):
+            j0, w = E_PIECES[t][k]
+            js = slice(j0, j0 + w)
+            ls = slice(j0 // 16, (j0 + w) // 16)
+            e1 = ring.tile([P, w], F32, name="e1")
+            nc.vector.tensor_tensor(e1[:], e_wins[t][:].indirect(west_t[:, ls]), bs[t][:, js], ALU.add)
+            nc.vector.tensor_tensor(z2_rows[:, S * t + j0 : S * t + j0 + w], e_wins[t][:].indirect(east_t[:, ls]), e1[:], ALU.add)
 
         word_banks = {}
+        sum_banks = {}
 
-        def diffuse_y(u, h):
-            ls = slice(HALF * h // 16, HALF * (h + 1) // 16)
-            sums = psum.tile([P, 2, 2, P], F32, name="bank")
-            for r in range(2):
-                t = 2 * u + r
-                n_w = ring.tile([P, HALF], F32, name="n_w", bufs=3)
-                n_e = ring.tile([P, HALF], F32, name="n_e", bufs=3)
-                nc.scalar.activation(out=n_w[:], in_=logits[t][:].indirect(west_t[:, ls]), func=ACT.Sigmoid, scale=-1.0)
-                nc.scalar.activation(out=n_e[:], in_=logits[t][:].indirect(east_t[:, ls]), func=ACT.Sigmoid, scale=-1.0)
-                for q in range(2):
-                    j0 = HALF * h + P * q
-                    terms = (a_negs[t][:, j0 : j0 + P], n_w[:, P * q : P * (q + 1)], n_e[:, P * q : P * (q + 1)])
-                    for i, term in enumerate(terms):
-                        nc.tensor.matmul(sums[:, q, r, :], term, ident[:], is_transpose=True, start=(i == 0), stop=(i == 2))
-            for q in range(2):
-                pairs = ring.tile([P, P, 2], BF16, name="pairs", bufs=4)
-                nc.vector.scalar_tensor_tensor(out=pairs[:], in0=sums[:, q].rearrange("j e p -> j p e"), scalar=2.5,
-                                               in1=g1_row[:, u], op0=ALU.subtract, op1=ALU.mult)
-                if u == 0:
-                    word_banks[(h, q)] = psum.tile([P, 2, P], F32, name="bank")
-                nc.tensor.transpose(word_banks[(h, q)][:, u, :], pairs[:].rearrange("j p e -> j (p e)").bitcast(F32), ident[:])
+        def diffuse_y(t, k):
+            j0, w = Y_PIECES[t][k]
+            u, r = t // 2, t % 2
+            ls = slice(j0 // 16, (j0 + w) // 16)
+            n_w = ring.tile([P, w], F32, name="n_w", bufs=N_BUFS)
+            n_e = ring.tile([P, w], F32, name="n_e", bufs=N_BUFS)
+            nc.scalar.activation(out=n_w[:], in_=y_wins[t][:].indirect(west_t[:, ls]), func=ACT.Sigmoid, scale=-1.0)
+            nc.scalar.activation(out=n_e[:], in_=y_wins[t][:].indirect(east_t[:, ls]), func=ACT.Sigmoid, scale=-1.0)
+            for c0 in range(0, w, P):
+                h, q = divmod((j0 + c0) // P, 2)
+                if (u, h) not in sum_banks:
+                    sum_banks[(u, h)] = psum.tile([P, 2, 2, P], F32, name="bank")
+                terms = (a_negs[t][:, j0 + c0 : j0 + c0 + P], n_w[:, c0 : c0 + P], n_e[:, c0 : c0 + P])
+                for i, term in enumerate(terms):
+                    nc.tensor.matmul(sum_banks[(u, h)][:, q, r, :], term, ident[:], is_transpose=True, start=(i == 0), stop=(i == 2))
+
+        def turn_back(u, h, q):
+            pairs = ring.tile([P, P], F32, name="pairs", bufs=4)
+            words = pairs[:]
+            nc.vector.scalar_tensor_tensor(out=words.bitcast(BF16).rearrange("j (p e) -> j p e", e=2), in0=sum_banks[(u, h)][:, q].rearrange("j e p -> j p e"), scalar=2.5,
+                                           in1=g1_row[:, u], op0=ALU.subtract, op1=ALU.mult)
+            if u == 0 and (h == 1 or q == 0):
+                word_banks[(h, q)] = psum.tile([P, 2, 2, P], F32, name="bank")
+            if u == 0 and h == 0 and q == 1:
+                word_banks[(h, q)] = word_banks[(h, 0)]
+            nc.tensor.transpose(word_banks[(h, q)][:, q, u, :], words, ident[:])
 
         out_rows = out_0.rearrange("(p t) j -> p t j", t=PACK)
         o_words = keep.tile([P, S], I32, name="o_words", align_bytes=64)
@@ -181,35 +211,56 @@ def tile_picked_grayscott_none_po_kernel(
             nc.vector.quantize_mx(out=c[:].bitcast(FP8X4), scales=s[:], in_=woven)
             return c, s
 
+        made = {}
+
+        def weave2(h, qs):
+            w = P * len(qs)
+            z2_src = z2_rows[:].rearrange("p (t j) -> p j t", t=PACK)[:, HALF * h + P * qs[0] : HALF * h + P * qs[0] + w, :]
+            z2_woven = ring.tile([P, w, PACK], BF16, name="z2_woven", align_bytes=64)
+            if (h, qs[0]) in ZW_S:
+                nc.scalar.copy(out=z2_woven[:], in_=z2_src)
+            else:
+                nc.vector.tensor_copy(out=z2_woven[:], in_=z2_src)
+            made[("z2", h, qs[0])] = quantise(z2_woven[:].rearrange("p j t -> p (j t)"), w, "z2")
+
+        def weave1(h, qs):
+            w = P * len(qs)
+            z_woven = ring.tile([P, w * PACK], BF16, name="z_woven", align_bytes=64)
+            z_words = z_woven[:].bitcast(F32).rearrange("p (q j u) -> p q j u", u=2, j=P)
+            turned = word_banks[(h, qs[0])][:, qs[0] : qs[0] + len(qs)].rearrange("p q u j -> p q j u")
+            if (h, qs[0]) in ZC_V:
+                nc.vector.tensor_copy(out=z_words, in_=turned)
+            else:
+                nc.scalar.copy(out=z_words, in_=turned)
+            made[("z", h, qs[0])] = quantise(z_woven[:], w, "z")
+
         def project(h, qs):
             w = P * len(qs)
             j0 = HALF * h + P * qs[0]
             js = slice(j0, j0 + w)
-            z2_woven = ring.tile([P, w, PACK], BF16, name="z2_woven", align_bytes=64)
-            if h < ZW_S:
-                nc.scalar.copy(out=z2_woven[:], in_=z2_rows[h][:, :, P * qs[0] : P * qs[0] + w].rearrange("p t j -> p j t"))
-            else:
-                nc.vector.tensor_copy(out=z2_woven[:], in_=z2_rows[h][:, :, P * qs[0] : P * qs[0] + w].rearrange("p t j -> p j t"))
-            z_woven = ring.tile([P, w * PACK], BF16, name="z_woven", align_bytes=64)
-            z_words = z_woven[:].bitcast(F32).rearrange("p (j u) -> p j u", u=2)
-            for i, q in enumerate(qs):
-                nc.scalar.copy(out=z_words[:, P * i : P * (i + 1), :], in_=word_banks[(h, q)][:].rearrange("p u j -> p j u"))
-            z2_c, z2_s = quantise(z2_woven[:].rearrange("p j t -> p (j t)"), w, "z2")
-            z_c, z_s = quantise(z_woven[:], w, "z")
+            z_c, z_s = made[("z", h, qs[0])]
+            z2_c, z2_s = made[("z2", h, qs[0])]
             o_f32 = ring.tile([P, PACK, w], F32, name="o_f32", bufs=3)
             per_bank = S // w
             for b0 in range(0, PACK, per_bank):
                 acc = psum.tile([P, per_bank, w], F32, name="bank")
                 for r in range(per_bank):
                     cols = slice(P * (b0 + r), P * (b0 + r + 1))
-                    nc.tensor.matmul_mx(out=acc[:, r, :], lhsT=w4[:, cols].bitcast(FP8X4), lhsT_scale=s34[4:P, cols],
-                                        rhs=z2_c[:].bitcast(FP8X4), rhs_scale=z2_s[:], start=True, stop=False)
-                    nc.tensor.matmul_mx(out=acc[:, r, :], lhsT=w3[:, cols].bitcast(FP8X4), lhsT_scale=s34[:, cols],
-                                        rhs=z_c[:].bitcast(FP8X4), rhs_scale=z_s[:], start=False, stop=True)
+                    nc.tensor.matmul_mx(out=acc[:, r, :], lhsT=w3[:, cols].bitcast(FP8X4), lhsT_scale=s34[8:P, cols],
+                                        rhs=z_c[:].bitcast(FP8X4), rhs_scale=z_s[:], start=True, stop=False)
+                    nc.tensor.matmul_mx(out=acc[:, r, :], lhsT=w4[:, cols].bitcast(FP8X4), lhsT_scale=s34[12:P, cols],
+                                        rhs=z2_c[:].bitcast(FP8X4), rhs_scale=z2_s[:], start=False, stop=True)
                 nc.scalar.copy(out=o_f32[:, b0 : b0 + per_bank, :], in_=acc[:])
             nc.sync.dma_start(out=out_rows[:, :, js], in_=o_f32[:])
+            made[("o", h, qs[0])] = o_f32
+
+        def planes(h, qs):
+            w = P * len(qs)
+            j0 = HALF * h + P * qs[0]
+            js = slice(j0, j0 + w)
+            o_f32 = made[("o", h, qs[0])]
             o_woven = ring.tile([P, w, PACK], BF16, name="o_woven", align_bytes=64)
-            if h < OW_S:
+            if (h, qs[0]) in OW_S:
                 nc.scalar.copy(out=o_woven[:], in_=o_f32[:].rearrange("p t j -> p j t"))
             else:
                 nc.vector.tensor_copy(out=o_woven[:], in_=o_f32[:].rearrange("p t j -> p j t"))
@@ -217,25 +268,40 @@ def tile_picked_grayscott_none_po_kernel(
                                   in_=o_woven[:].rearrange("p j t -> p (j t)"))
             nc.sync.dma_start(out=words_of(out_1)[:, js], in_=o_words[:, js])
 
-        for t in range(PACK):
-            react(t)
-            diffuse_e(t, 0)
-        g_bank = psum.tile([P, 2, 2, P], F32, name="bank")
-        for t in range(PACK):
-            nc.tensor.transpose(g_bank[:, t // 2, t % 2, :], g1_t[:, t : t + 1].to_broadcast([P, P]), ident[:])
-        g1_row = keep.tile([P, 2, P, 2], F32, name="g1_row")
-        nc.scalar.activation(out=g1_row[:], in_=g_bank[:].rearrange("j u e p -> j u p e"), func=ACT.Copy, scale=-0.25)
-
+        react(0)
+        diffuse_e(0, 0)
+        react(1)
         diffuse_y(0, 0)
+        diffuse_e(1, 0)
+        react(2)
+        s34 = deal(nc.vector, s_raw, U8, "s_dealt")
         diffuse_y(1, 0)
-        diffuse_e(0, 1)
-        diffuse_y(0, 1)
-        diffuse_e(1, 1)
-        project(0, [0, 1])
-        diffuse_e(2, 1)
-        diffuse_y(1, 1)
+        diffuse_e(2, 0)
+        react(3)
+        diffuse_y(2, 0)
+        turn_back(0, 0, 0)
+        turn_back(0, 0, 1)
+        turn_back(0, 1, 0)
+        turn_back(0, 1, 1)
+        diffuse_y(3, 0)
+        diffuse_y(3, 1)
+        diffuse_e(3, 0)
+        turn_back(1, 0, 0)
+        turn_back(1, 0, 1)
+        weave2(0, [0, 1])
+        weave1(0, [0, 1])
         diffuse_e(3, 1)
+        turn_back(1, 1, 0)
+        turn_back(1, 1, 1)
+        project(0, [0, 1])
+        weave2(1, [0])
+        weave1(1, [0])
+        weave2(1, [1])
+        weave1(1, [1])
         project(1, [0])
         project(1, [1])
+        planes(0, [0, 1])
+        planes(1, [0])
+        planes(1, [1])
         for q in range(4):
             nc.sync.dma_start(out=out_2[0, 4 * q : 4 * q + 4, :].bitcast(I32), in_=o_scales[32 * q : 32 * q + 4, :].bitcast(I32))

@@ -19,9 +19,9 @@ ACT = mybir.ActivationFunctionType
 P = 128
 PACK = 4
 HALF = 256
-LOGIT_V = 2
+LOGIT_V = 4
 OW_S = []
-ZW_S = []
+ZW_S = [(0, 0)]
 DEALS = [(0, 1), (1, 4)]
 N_BUFS = 3
 ZC_V = []
@@ -109,8 +109,6 @@ def tile_picked_grayscott_none_po_kernel(
         load_scale_rows([nc.sync] * 4, s_raw, 8, w3_scales)
         load_scale_rows([nc.sync] * 4, s_raw, 12, w4_scales)
 
-        g2_8 = keep.tile([P, PACK], F32, name="g2_8")
-        nc.scalar.activation(out=g2_8[:], in_=g2_t[:], func=ACT.Copy, scale=0.125)
         g_bank = psum.tile([P, 2, 2, P], F32, name="bank")
         for t in range(PACK):
             nc.tensor.transpose(g_bank[:, t // 2, t % 2, :], g1_t[:, t : t + 1].to_broadcast([P, P]), ident[:])
@@ -149,7 +147,7 @@ def tile_picked_grayscott_none_po_kernel(
             nc.scalar.activation(out=e, in_=acc_e[:], func=ACT.Sigmoid)
             if t < LOGIT_V:
                 nc.vector.tensor_copy(out=logit, in_=acc_y[:])
-            nc.scalar.activation(out=ew, in_=e, func=ACT.Copy, scale=g2_8[:, t : t + 1])
+            nc.scalar.activation(out=ew, in_=e, func=ACT.Copy, scale=g2_t[:, t : t + 1])
             nc.scalar.activation(out=q4[:], in_=e, func=ACT.Square, scale=2.0)
             if t >= LOGIT_V:
                 nc.scalar.copy(out=logit, in_=acc_y[:])
@@ -191,7 +189,7 @@ def tile_picked_grayscott_none_po_kernel(
                     nc.tensor.matmul(sum_banks[(u, h)][:, q, r, :], term, ident[:], is_transpose=True, start=(i == 0), stop=(i == 2))
 
         def turn_back(u, h, q):
-            pairs = ring.tile([P, P], F32, name="pairs", bufs=4)
+            pairs = ring.tile([P, P], F32, name="pairs", bufs=8)
             words = pairs[:]
             nc.vector.scalar_tensor_tensor(out=words.bitcast(BF16).rearrange("j (p e) -> j p e", e=2), in0=sum_banks[(u, h)][:, q].rearrange("j e p -> j p e"), scalar=2.5,
                                            in1=g1_row[:, u], op0=ALU.subtract, op1=ALU.mult)
@@ -217,10 +215,12 @@ def tile_picked_grayscott_none_po_kernel(
             w = P * len(qs)
             z2_src = z2_rows[:].rearrange("p (t j) -> p j t", t=PACK)[:, HALF * h + P * qs[0] : HALF * h + P * qs[0] + w, :]
             z2_woven = ring.tile([P, w, PACK], BF16, name="z2_woven", align_bytes=64)
+            dst = z2_woven[:].rearrange("p (c i) t -> p c t i", i=4)
+            src = z2_src.rearrange("p (c i) t -> p c t i", i=4)
             if (h, qs[0]) in ZW_S:
-                nc.scalar.copy(out=z2_woven[:], in_=z2_src)
+                nc.scalar.activation(out=dst, in_=src, func=ACT.Copy, scale=0.125)
             else:
-                nc.vector.tensor_copy(out=z2_woven[:], in_=z2_src)
+                nc.vector.tensor_scalar_mul(out=dst, in0=src, scalar1=0.125)
             made[("z2", h, qs[0])] = quantise(z2_woven[:].rearrange("p j t -> p (j t)"), w, "z2")
 
         def weave1(h, qs):
@@ -260,13 +260,17 @@ def tile_picked_grayscott_none_po_kernel(
             js = slice(j0, j0 + w)
             o_f32 = made[("o", h, qs[0])]
             o_woven = ring.tile([P, w, PACK], BF16, name="o_woven", align_bytes=64)
+            dst = o_woven[:].rearrange("p (c i) t -> p c t i", i=4)
+            src = o_f32[:].rearrange("p t (c i) -> p c t i", i=4)
             if (h, qs[0]) in OW_S:
-                nc.scalar.copy(out=o_woven[:], in_=o_f32[:].rearrange("p t j -> p j t"))
+                nc.scalar.copy(out=dst, in_=src)
             else:
-                nc.vector.tensor_copy(out=o_woven[:], in_=o_f32[:].rearrange("p t j -> p j t"))
+                nc.vector.tensor_copy(out=dst, in_=src)
             nc.vector.quantize_mx(out=o_words[:, js].bitcast(FP8X4), scales=o_scales[:, js],
                                   in_=o_woven[:].rearrange("p j t -> p (j t)"))
-            nc.sync.dma_start(out=words_of(out_1)[:, js], in_=o_words[:, js])
+            if j0 + w in (HALF, S):
+                done = slice(HALF * h, HALF * (h + 1))
+                nc.sync.dma_start(out=words_of(out_1)[:, done], in_=o_words[:, done])
 
         react(0)
         diffuse_e(0, 0)
@@ -303,5 +307,5 @@ def tile_picked_grayscott_none_po_kernel(
         planes(0, [0, 1])
         planes(1, [0])
         planes(1, [1])
-        for q in range(4):
-            nc.sync.dma_start(out=out_2[0, 4 * q : 4 * q + 4, :].bitcast(I32), in_=o_scales[32 * q : 32 * q + 4, :].bitcast(I32))
+        for q, queue in enumerate((nc.scalar, nc.scalar, nc.sync, nc.sync)):
+            queue.dma_start(out=out_2[0, 4 * q : 4 * q + 4, :].bitcast(I32), in_=o_scales[32 * q : 32 * q + 4, :].bitcast(I32))

@@ -19,11 +19,17 @@ ACT = mybir.ActivationFunctionType
 P = 128
 PACK = 4
 HALF = 256
-LOGIT_V = 4
+LOGIT_V = 1
 OW_S = []
 ZW_S = [(0, 0)]
 DEALS = [(0, 1), (1, 4)]
 N_BUFS = 3
+EW_S = 0
+SPLIT0 = True
+FORCE = False
+REUSE = {(1, 0): (3, 0)}
+SHARE0 = True
+QUARTERS = [(0, 128), (128, 128), (256, 128), (384, 128)]
 ZC_V = []
 WHOLE = [(0, 512)]
 THIRDS = [(0, 256), (256, 128), (384, 128)]
@@ -133,7 +139,7 @@ def tile_picked_grayscott_none_po_kernel(
                 y_own = keep.tile([P, S], F32, name="y_own%d" % t)
                 logit, y = y_win[:], y_own[:]
             if min(w for j0, w in E_PIECES[t]) >= HALF:
-                e_win = keep.tile([P, 2 * S], F32, name="e_win%d" % t)
+                e_win = keep.tile([P, 2 * S], F32, name="e_win%d" % t, align_bytes=64)
                 ew, e = e_win[:, 0:S], e_win[:, S : 2 * S]
             else:
                 e_win = keep.tile([P, S], F32, name="e_win%d" % t)
@@ -147,7 +153,10 @@ def tile_picked_grayscott_none_po_kernel(
             nc.scalar.activation(out=e, in_=acc_e[:], func=ACT.Sigmoid)
             if t < LOGIT_V:
                 nc.vector.tensor_copy(out=logit, in_=acc_y[:])
-            nc.scalar.activation(out=ew, in_=e, func=ACT.Copy, scale=g2_t[:, t : t + 1])
+            if t < EW_S:
+                nc.scalar.activation(out=ew, in_=e, func=ACT.Copy, scale=g2_t[:, t : t + 1])
+            else:
+                nc.vector.tensor_scalar_mul(out=ew, in0=e, scalar1=g2_t[:, t : t + 1])
             nc.scalar.activation(out=q4[:], in_=e, func=ACT.Square, scale=2.0)
             if t >= LOGIT_V:
                 nc.scalar.copy(out=logit, in_=acc_y[:])
@@ -159,15 +168,21 @@ def tile_picked_grayscott_none_po_kernel(
             a_negs.append(a_neg)
             bs.append(b)
 
+        scratch = {}
         z2_rows = keep.tile([P, PACK * S], F32, name="z2_all")
 
         def diffuse_e(t, k):
             j0, w = E_PIECES[t][k]
             js = slice(j0, j0 + w)
             ls = slice(j0 // 16, (j0 + w) // 16)
-            e1 = ring.tile([P, w], F32, name="e1")
-            nc.vector.tensor_tensor(e1[:], e_wins[t][:].indirect(west_t[:, ls]), bs[t][:, js], ALU.add)
-            nc.vector.tensor_tensor(z2_rows[:, S * t + j0 : S * t + j0 + w], e_wins[t][:].indirect(east_t[:, ls]), e1[:], ALU.add)
+            if j0 >= HALF and FORCE:
+                e1 = scratch[(t, 0)][:, j0 - HALF : j0 - HALF + w]
+            else:
+                e1_tile = ring.tile([P, w], F32, name="e1", bufs=3)
+                e1 = e1_tile[:]
+            scratch[(t, k)] = e1
+            nc.vector.tensor_tensor(e1, e_wins[t][:].indirect(west_t[:, ls]), bs[t][:, js], ALU.add)
+            nc.vector.tensor_tensor(z2_rows[:, S * t + j0 : S * t + j0 + w], e_wins[t][:].indirect(east_t[:, ls]), e1, ALU.add)
 
         word_banks = {}
         sum_banks = {}
@@ -189,13 +204,16 @@ def tile_picked_grayscott_none_po_kernel(
                     nc.tensor.matmul(sum_banks[(u, h)][:, q, r, :], term, ident[:], is_transpose=True, start=(i == 0), stop=(i == 2))
 
         def turn_back(u, h, q):
-            pairs = ring.tile([P, P], F32, name="pairs", bufs=8)
-            words = pairs[:]
+            if (u, h) in REUSE:
+                words = bs[3][:, HALF + P * q : HALF + P * (q + 1)] if FORCE else scratch[REUSE[(u, h)]][:, P * q : P * (q + 1)]
+            else:
+                pairs = ring.tile([P, P], F32, name="pairs", bufs=8)
+                words = pairs[:]
             nc.vector.scalar_tensor_tensor(out=words.bitcast(BF16).rearrange("j (p e) -> j p e", e=2), in0=sum_banks[(u, h)][:, q].rearrange("j e p -> j p e"), scalar=2.5,
                                            in1=g1_row[:, u], op0=ALU.subtract, op1=ALU.mult)
-            if u == 0 and (h == 1 or q == 0):
+            if u == 0 and (h == 1 or q == 0 or not SHARE0):
                 word_banks[(h, q)] = psum.tile([P, 2, 2, P], F32, name="bank")
-            if u == 0 and h == 0 and q == 1:
+            if u == 0 and h == 0 and q == 1 and SHARE0:
                 word_banks[(h, q)] = word_banks[(h, 0)]
             nc.tensor.transpose(word_banks[(h, q)][:, q, u, :], words, ident[:])
 
@@ -204,8 +222,8 @@ def tile_picked_grayscott_none_po_kernel(
         o_scales = keep.tile([P, S], U8, name="o_scales", align_bytes=64)
 
         def quantise(woven, w, nm):
-            c = ring.tile([P, w], U32, name=nm + "_codes", align_bytes=64)
-            s = ring.tile([P, w], U8, name=nm + "_scales", align_bytes=64)
+            c = ring.tile([P, w], U32, name=nm + "_codes", align_bytes=64, bufs=3)
+            s = ring.tile([P, w], U8, name=nm + "_scales", align_bytes=64, bufs=3)
             nc.vector.quantize_mx(out=c[:].bitcast(FP8X4), scales=s[:], in_=woven)
             return c, s
 
@@ -214,7 +232,7 @@ def tile_picked_grayscott_none_po_kernel(
         def weave2(h, qs):
             w = P * len(qs)
             z2_src = z2_rows[:].rearrange("p (t j) -> p j t", t=PACK)[:, HALF * h + P * qs[0] : HALF * h + P * qs[0] + w, :]
-            z2_woven = ring.tile([P, w, PACK], BF16, name="z2_woven", align_bytes=64)
+            z2_woven = ring.tile([P, w, PACK], BF16, name="z2_woven", align_bytes=64, bufs=3)
             dst = z2_woven[:].rearrange("p (c i) t -> p c t i", i=4)
             src = z2_src.rearrange("p (c i) t -> p c t i", i=4)
             if (h, qs[0]) in ZW_S:
@@ -225,7 +243,7 @@ def tile_picked_grayscott_none_po_kernel(
 
         def weave1(h, qs):
             w = P * len(qs)
-            z_woven = ring.tile([P, w * PACK], BF16, name="z_woven", align_bytes=64)
+            z_woven = ring.tile([P, w * PACK], BF16, name="z_woven", align_bytes=64, bufs=3)
             z_words = z_woven[:].bitcast(F32).rearrange("p (q j u) -> p q j u", u=2, j=P)
             turned = word_banks[(h, qs[0])][:, qs[0] : qs[0] + len(qs)].rearrange("p q u j -> p q j u")
             if (h, qs[0]) in ZC_V:
@@ -241,8 +259,19 @@ def tile_picked_grayscott_none_po_kernel(
             z_c, z_s = made[("z", h, qs[0])]
             z2_c, z2_s = made[("z2", h, qs[0])]
             o_f32 = ring.tile([P, PACK, w], F32, name="o_f32", bufs=3)
+            if h == 0 and SPLIT0:
+                accs = [psum.tile([P, w], F32, name="bank") for r in range(PACK)]
+                for r in range(PACK):
+                    cols = slice(P * r, P * (r + 1))
+                    nc.tensor.matmul_mx(out=accs[r][:], lhsT=w4[:, cols].bitcast(FP8X4), lhsT_scale=s34[12:P, cols],
+                                        rhs=z2_c[:].bitcast(FP8X4), rhs_scale=z2_s[:], start=True, stop=False)
+                for r in range(PACK):
+                    cols = slice(P * r, P * (r + 1))
+                    nc.tensor.matmul_mx(out=accs[r][:], lhsT=w3[:, cols].bitcast(FP8X4), lhsT_scale=s34[8:P, cols],
+                                        rhs=z_c[:].bitcast(FP8X4), rhs_scale=z_s[:], start=False, stop=True)
+                    nc.scalar.copy(out=o_f32[:, r, :], in_=accs[r][:])
             per_bank = S // w
-            for b0 in range(0, PACK, per_bank):
+            for b0 in range(0, 0 if h == 0 and SPLIT0 else PACK, per_bank):
                 acc = psum.tile([P, per_bank, w], F32, name="bank")
                 for r in range(per_bank):
                     cols = slice(P * (b0 + r), P * (b0 + r + 1))
@@ -259,7 +288,7 @@ def tile_picked_grayscott_none_po_kernel(
             j0 = HALF * h + P * qs[0]
             js = slice(j0, j0 + w)
             o_f32 = made[("o", h, qs[0])]
-            o_woven = ring.tile([P, w, PACK], BF16, name="o_woven", align_bytes=64)
+            o_woven = ring.tile([P, w, PACK], BF16, name="o_woven", align_bytes=64, bufs=3)
             dst = o_woven[:].rearrange("p (c i) t -> p c t i", i=4)
             src = o_f32[:].rearrange("p t (c i) -> p c t i", i=4)
             if (h, qs[0]) in OW_S:
@@ -278,7 +307,7 @@ def tile_picked_grayscott_none_po_kernel(
         diffuse_y(0, 0)
         diffuse_e(1, 0)
         react(2)
-        s34 = deal(nc.vector, s_raw, U8, "s_dealt")
+        s34 = deal(nc.vector, s_raw, U8, "e_win0")
         diffuse_y(1, 0)
         diffuse_e(2, 0)
         react(3)

@@ -3,7 +3,7 @@ from contextlib import ExitStack
 import concourse.mybir as mybir
 from concourse.masks import make_identity
 
-K, T, S, N, H = 512, 2048, 512, 512, 512
+TABLE, CELLS, FEATURES = 2048, 512, 512
 FLOPS = 4 * 2 * 512 * 512 * 512
 
 F32 = mybir.dt.float32
@@ -17,25 +17,13 @@ ALU = mybir.AluOpType
 ACT = mybir.ActivationFunctionType
 
 P = 128
-PACK = 4
-HALF = 256
-LOGIT_V = 1
-OW_S = []
-ZW_S = [(0, 0)]
-DEALS = [(0, 1), (1, 4)]
-N_BUFS = 3
-EW_S = 0
-SPLIT0 = True
-FORCE = False
-REUSE = {(1, 0): (3, 0)}
-SHARE0 = True
-QUARTERS = [(0, 128), (128, 128), (256, 128), (384, 128)]
-ZC_V = []
-WHOLE = [(0, 512)]
-THIRDS = [(0, 256), (256, 128), (384, 128)]
-HALVES = [(0, 256), (256, 256)]
-Y_PIECES = [WHOLE, WHOLE, WHOLE, HALVES]
-E_PIECES = [WHOLE, WHOLE, WHOLE, HALVES]
+SLOTS = 4
+LAST = SLOTS - 1
+HALF = CELLS // 2
+LIST_ROWS = 16
+QUADRANTS = range(4)
+LINE = 4
+PARTS = 3
 
 
 def tile_picked_grayscott_none_po_kernel(
@@ -47,294 +35,268 @@ def tile_picked_grayscott_none_po_kernel(
     def words_of(dram):
         return dram[0].rearrange("p n t -> p (n t)").bitcast(I32)
 
-    def load_scale_rows(queues, plane, first_row, dram, quadrants=range(4)):
+    def load_scale_rows(queue, tile, first_row, dram, quadrants):
         for q in quadrants:
             r = 32 * q + first_row
-            queues[q].dma_start(out=plane[r : r + 4, :].bitcast(I32), in_=dram[0, 4 * q : 4 * q + 4, :].bitcast(I32))
+            queue.dma_start(out=tile[r : r + 4, :].bitcast(I32), in_=dram[0, 4 * q : 4 * q + 4, :].bitcast(I32))
 
     with ExitStack() as ctx:
         keep = ctx.enter_context(tc.tile_pool(name="keep", bufs=1))
         ring = ctx.enter_context(tc.tile_pool(name="ring", bufs=2))
         psum = ctx.enter_context(tc.psum_pool(name="psum", bufs=8))
 
-        offs_t = keep.tile([P, S // 16], U16, name="offs_t")
-        west_t = keep.tile([P, S // 16], U16, name="west_t")
-        east_t = keep.tile([P, S // 16], U16, name="east_t")
-        xw = keep.tile([P, T], I32, name="xw", align_bytes=64)
-        xs = keep.tile([P, T], U8, name="xs", align_bytes=64)
-        s_raw = keep.tile([P, H], U8, name="s_raw", align_bytes=64)
-        g1_t = keep.tile([P, PACK], F32, name="g1_t")
-        g2_t = keep.tile([P, PACK], F32, name="g2_t")
-        xs_rows = keep.tile([P, T], U8, name="xs_rows", align_bytes=64)
-        w_raw = [keep.tile([P, H], I32, name="w_raw%d" % i, align_bytes=64) for i in range(4)]
+        offs_t = keep.tile([P, CELLS // LIST_ROWS], U16, name="offs_t")
+        west_t = keep.tile([P, CELLS // LIST_ROWS], U16, name="west_t")
+        east_t = keep.tile([P, CELLS // LIST_ROWS], U16, name="east_t")
+        x_table = keep.tile([P, TABLE], I32, name="x_table", align_bytes=64)
+        x_scale_table = keep.tile([P, TABLE], U8, name="x_scale_table", align_bytes=64)
+        w_scales_raw = keep.tile([P, FEATURES], U8, name="w_scales_raw", align_bytes=64)
+        g1_t = keep.tile([P, SLOTS], F32, name="g1_t")
+        g2_t = keep.tile([P, SLOTS], F32, name="g2_t")
+        x_scale_rows = keep.tile([P, TABLE], U8, name="x_scale_rows", align_bytes=64)
+        w_raw = [keep.tile([P, FEATURES], I32, name="w_raw%d" % i, align_bytes=64) for i in range(4)]
         ident = keep.tile([P, P], F32, name="ident")
 
-        nc.gpsimd.memset(s_raw[:].bitcast(I32), 0)
-        nc.vector.memset(xs[:].bitcast(I32), 0)
+        nc.gpsimd.memset(w_scales_raw[:].bitcast(I32), 0)
+        nc.vector.memset(x_scale_table[:].bitcast(I32), 0)
 
         nc.sync.dma_start(offs_t[:], offs)
-        load_scale_rows([nc.sync] * 4, xs_rows, 0, x_scales)
-        load_scale_rows([nc.sync] * 2, s_raw, 0, w1_scales, [0, 1])
-        nc.sync.dma_start(out=xw[:], in_=words_of(x_words))
+        load_scale_rows(nc.sync, x_scale_rows, 0, x_scales, QUADRANTS)
+        load_scale_rows(nc.sync, w_scales_raw, 0, w1_scales, QUADRANTS[:2])
+        nc.sync.dma_start(out=x_table[:], in_=words_of(x_words))
         nc.sync.dma_start(out=w_raw[0][:], in_=words_of(w1_words))
         nc.sync.dma_start(out=w_raw[1][:], in_=words_of(w2_words))
-        load_scale_rows([nc.sync] * 4, s_raw, 0, w1_scales, [2, 3])
-        load_scale_rows([nc.sync] * 3 + [nc.gpsimd], s_raw, 4, w2_scales)
+        load_scale_rows(nc.sync, w_scales_raw, 0, w1_scales, QUADRANTS[2:])
+        load_scale_rows(nc.sync, w_scales_raw, 4, w2_scales, QUADRANTS[:3])
+        load_scale_rows(nc.gpsimd, w_scales_raw, 4, w2_scales, QUADRANTS[3:])
         make_identity(nc, ident[:])
-        nc.gpsimd.dma_start(out=g1_t[:], in_=g1.rearrange("(p t) o -> p (t o)", t=PACK))
+        nc.gpsimd.dma_start(out=g1_t[:], in_=g1.rearrange("(p t) o -> p (t o)", t=SLOTS))
         nc.sync.dma_start(out=w_raw[2][:], in_=words_of(w3_words))
         nc.sync.dma_start(out=w_raw[3][:], in_=words_of(w4_words))
-        nc.sync.dma_start(out=g2_t[:], in_=g2.rearrange("(p t) o -> p (t o)", t=PACK))
+        nc.sync.dma_start(out=g2_t[:], in_=g2.rearrange("(p t) o -> p (t o)", t=SLOTS))
         nc.sync.dma_start(west_t[:], west)
         nc.sync.dma_start(east_t[:], east)
-        for q in range(4):
+        for q in QUADRANTS:
             rows = slice(32 * q, 32 * q + 4)
-            nc.vector.tensor_copy(out=xs[rows, :].bitcast(I32), in_=xs_rows[rows, :].bitcast(I32))
+            nc.vector.tensor_copy(out=x_scale_table[rows, :].bitcast(I32), in_=x_scale_rows[rows, :].bitcast(I32))
 
-        def deal(engine, raw, dtype, name):
-            dealt = keep.tile([P, H], dtype, name=name, align_bytes=64)
-            engine.tensor_copy(
-                out=dealt[:].rearrange("p (t m) -> p m t", t=PACK), in_=raw[:].rearrange("p (m t) -> p m t", t=PACK)
+        def deal(dealt, raw, slots):
+            nc.vector.tensor_copy(
+                out=dealt[:].rearrange("p (t m) -> p m t", t=SLOTS)[:, :, slots],
+                in_=raw[:].rearrange("p (m t) -> p m t", t=SLOTS)[:, :, slots],
             )
-            return dealt
 
-        xs_g = keep.tile([P, S], U8, name="xs_g", align_bytes=64)
-        nc.vector.tensor_copy(out=xs_g[:], in_=xs[:].indirect(offs_t[:]))
-        xw_g = keep.tile([P, S], U32, name="xw_g", align_bytes=64)
-        nc.vector.tensor_copy(out=xw_g[:], in_=xw[:].bitcast(U32).indirect(offs_t[:]))
+        x_scale = keep.tile([P, CELLS], U8, name="x_scale", align_bytes=64)
+        nc.vector.tensor_copy(out=x_scale[:], in_=x_scale_table[:].indirect(offs_t[:]))
+        x_codes = keep.tile([P, CELLS], U32, name="x_codes", align_bytes=64)
+        nc.vector.tensor_copy(out=x_codes[:], in_=x_table[:].bitcast(U32).indirect(offs_t[:]))
 
-        s12 = keep.tile([P, H], U8, name="s_dealt", align_bytes=64)
-        w1 = keep.tile([P, H], I32, name="w1", align_bytes=64)
-        w2 = keep.tile([P, H], I32, name="w2", align_bytes=64)
-        for t0, t1 in DEALS:
-            for raw, dealt in ((s_raw, s12), (w_raw[0], w1), (w_raw[1], w2)):
-                nc.vector.tensor_copy(out=dealt[:].rearrange("p (t m) -> p m t", t=PACK)[:, :, t0:t1],
-                                      in_=raw[:].rearrange("p (m t) -> p m t", t=PACK)[:, :, t0:t1])
-        w3 = deal(nc.vector, w_raw[2], I32, "w3")
-        w4 = deal(nc.vector, w_raw[3], I32, "w4")
-        load_scale_rows([nc.sync] * 4, s_raw, 8, w3_scales)
-        load_scale_rows([nc.sync] * 4, s_raw, 12, w4_scales)
+        s12 = keep.tile([P, FEATURES], U8, name="s12", align_bytes=64)
+        w1 = keep.tile([P, FEATURES], I32, name="w1", align_bytes=64)
+        w2 = keep.tile([P, FEATURES], I32, name="w2", align_bytes=64)
+        for slots in (slice(0, 1), slice(1, SLOTS)):
+            deal(s12, w_scales_raw, slots)
+            deal(w1, w_raw[0], slots)
+            deal(w2, w_raw[1], slots)
+        all_slots = slice(0, SLOTS)
+        w3 = keep.tile([P, FEATURES], I32, name="w3", align_bytes=64)
+        deal(w3, w_raw[2], all_slots)
+        w4 = keep.tile([P, FEATURES], I32, name="w4", align_bytes=64)
+        deal(w4, w_raw[3], all_slots)
+        load_scale_rows(nc.sync, w_scales_raw, 8, w3_scales, QUADRANTS)
+        load_scale_rows(nc.sync, w_scales_raw, 12, w4_scales, QUADRANTS)
 
-        g_bank = psum.tile([P, 2, 2, P], F32, name="bank")
-        for t in range(PACK):
-            nc.tensor.transpose(g_bank[:, t // 2, t % 2, :], g1_t[:, t : t + 1].to_broadcast([P, P]), ident[:])
+        g1_bank = psum.tile([P, 2, 2, P], F32, name="bank")
+        for t in range(SLOTS):
+            nc.tensor.transpose(g1_bank[:, t // 2, t % 2, :], g1_t[:, t : t + 1].to_broadcast([P, P]), ident[:])
         g1_row = keep.tile([P, 2, P, 2], F32, name="g1_row")
-        nc.scalar.activation(out=g1_row[:], in_=g_bank[:].rearrange("j u e p -> j u p e"), func=ACT.Copy, scale=-0.25)
+        nc.scalar.activation(out=g1_row[:], in_=g1_bank[:].rearrange("j u r p -> j u p r"), func=ACT.Copy, scale=-0.25)
 
-        y_wins, e_wins, a_negs, bs = [], [], [], []
+        y_windows, v_windows, y_terms, v_terms = [], [], [], []
 
         def react(t):
             cols = slice(P * t, P * (t + 1))
-            acc_y = psum.tile([P, S], F32, name="bank")
+            acc_y = psum.tile([P, CELLS], F32, name="bank")
             nc.tensor.matmul_mx(out=acc_y[:], lhsT=w1[:, cols].bitcast(FP8X4), lhsT_scale=s12[:, cols],
-                                rhs=xw_g[:].bitcast(FP8X4), rhs_scale=xs_g[:], start=True, stop=True)
-            acc_e = psum.tile([P, S], F32, name="bank")
+                                rhs=x_codes[:].bitcast(FP8X4), rhs_scale=x_scale[:], start=True, stop=True)
+            acc_e = psum.tile([P, CELLS], F32, name="bank")
             nc.tensor.matmul_mx(out=acc_e[:], lhsT=w2[:, cols].bitcast(FP8X4), lhsT_scale=s12[4:P, cols],
-                                rhs=xw_g[:].bitcast(FP8X4), rhs_scale=xs_g[:], start=True, stop=True)
-            if min(w for j0, w in Y_PIECES[t]) >= HALF:
-                y_win = keep.tile([P, 2 * S], F32, name="y_win%d" % t)
-                logit, y = y_win[:, 0:S], y_win[:, S : 2 * S]
-            else:
-                y_win = keep.tile([P, S], F32, name="y_win%d" % t)
-                y_own = keep.tile([P, S], F32, name="y_own%d" % t)
-                logit, y = y_win[:], y_own[:]
-            if min(w for j0, w in E_PIECES[t]) >= HALF:
-                e_win = keep.tile([P, 2 * S], F32, name="e_win%d" % t, align_bytes=64)
-                ew, e = e_win[:, 0:S], e_win[:, S : 2 * S]
-            else:
-                e_win = keep.tile([P, S], F32, name="e_win%d" % t)
-                e_own = keep.tile([P, S], F32, name="e_own%d" % t)
-                ew, e = e_win[:], e_own[:]
-            q4 = ring.tile([P, S], F32, name="q4")
-            u8 = ring.tile([P, S], F32, name="u8")
-            a_neg = keep.tile([P, S], F32, name="a_neg%d" % t)
-            b = keep.tile([P, S], F32, name="b%d" % t)
+                                rhs=x_codes[:].bitcast(FP8X4), rhs_scale=x_scale[:], start=True, stop=True)
+            y_window = keep.tile([P, 2 * CELLS], F32, name="y_window%d" % t)
+            logit, y = y_window[:, 0:CELLS], y_window[:, CELLS : 2 * CELLS]
+            v_window = keep.tile([P, 2 * CELLS], F32, name="v_window%d" % t, align_bytes=64)
+            v, e = v_window[:, 0:CELLS], v_window[:, CELLS : 2 * CELLS]
+            ee4 = ring.tile([P, CELLS], F32, name="ee4")
+            ye8 = ring.tile([P, CELLS], F32, name="ye8")
+            y_term = keep.tile([P, CELLS], F32, name="y_term%d" % t)
+            v_term = keep.tile([P, CELLS], F32, name="v_term%d" % t)
             nc.scalar.activation(out=y, in_=acc_y[:], func=ACT.Sigmoid)
             nc.scalar.activation(out=e, in_=acc_e[:], func=ACT.Sigmoid)
-            if t < LOGIT_V:
+            if t == 0:
                 nc.vector.tensor_copy(out=logit, in_=acc_y[:])
-            if t < EW_S:
-                nc.scalar.activation(out=ew, in_=e, func=ACT.Copy, scale=g2_t[:, t : t + 1])
-            else:
-                nc.vector.tensor_scalar_mul(out=ew, in0=e, scalar1=g2_t[:, t : t + 1])
-            nc.scalar.activation(out=q4[:], in_=e, func=ACT.Square, scale=2.0)
-            if t >= LOGIT_V:
+            nc.vector.tensor_scalar_mul(out=v, in0=e, scalar1=g2_t[:, t : t + 1])
+            nc.scalar.activation(out=ee4[:], in_=e, func=ACT.Square, scale=2.0)
+            if t > 0:
                 nc.scalar.copy(out=logit, in_=acc_y[:])
-            nc.vector.scalar_tensor_tensor(out=u8[:], in0=y, scalar=8.0, in1=e, op0=ALU.mult, op1=ALU.mult)
-            nc.vector.scalar_tensor_tensor(out=b[:], in0=u8[:], scalar=4.0, in1=ew, op0=ALU.add, op1=ALU.mult)
-            nc.vector.scalar_tensor_tensor(out=a_neg[:], in0=q4[:], scalar=1.5, in1=y, op0=ALU.subtract, op1=ALU.mult)
-            y_wins.append(y_win)
-            e_wins.append(e_win)
-            a_negs.append(a_neg)
-            bs.append(b)
+            nc.vector.scalar_tensor_tensor(out=ye8[:], in0=y, scalar=8.0, in1=e, op0=ALU.mult, op1=ALU.mult)
+            nc.vector.scalar_tensor_tensor(out=v_term[:], in0=ye8[:], scalar=4.0, in1=v, op0=ALU.add, op1=ALU.mult)
+            nc.vector.scalar_tensor_tensor(out=y_term[:], in0=ee4[:], scalar=1.5, in1=y, op0=ALU.subtract, op1=ALU.mult)
+            y_windows.append(y_window)
+            v_windows.append(v_window)
+            y_terms.append(y_term)
+            v_terms.append(v_term)
 
-        scratch = {}
-        z2_rows = keep.tile([P, PACK * S], F32, name="z2_all")
+        z2_rows = keep.tile([P, SLOTS * CELLS], F32, name="z2_rows")
 
-        def diffuse_e(t, k):
-            j0, w = E_PIECES[t][k]
-            js = slice(j0, j0 + w)
-            ls = slice(j0 // 16, (j0 + w) // 16)
-            if j0 >= HALF and FORCE:
-                e1 = scratch[(t, 0)][:, j0 - HALF : j0 - HALF + w]
-            else:
-                e1_tile = ring.tile([P, w], F32, name="e1", bufs=3)
-                e1 = e1_tile[:]
-            scratch[(t, k)] = e1
-            nc.vector.tensor_tensor(e1, e_wins[t][:].indirect(west_t[:, ls]), bs[t][:, js], ALU.add)
-            nc.vector.tensor_tensor(z2_rows[:, S * t + j0 : S * t + j0 + w], e_wins[t][:].indirect(east_t[:, ls]), e1, ALU.add)
+        def diffuse_v(t, j0, width):
+            entries = slice(j0 // LIST_ROWS, (j0 + width) // LIST_ROWS)
+            partial = ring.tile([P, width], F32, name="partial", bufs=3)
+            nc.vector.tensor_tensor(partial[:], v_windows[t][:].indirect(west_t[:, entries]),
+                                    v_terms[t][:, j0 : j0 + width], ALU.add)
+            nc.vector.tensor_tensor(z2_rows[:, CELLS * t + j0 : CELLS * t + j0 + width],
+                                    v_windows[t][:].indirect(east_t[:, entries]), partial[:], ALU.add)
+            return partial
 
-        word_banks = {}
         sum_banks = {}
+        word_banks = {}
 
-        def diffuse_y(t, k):
-            j0, w = Y_PIECES[t][k]
-            u, r = t // 2, t % 2
-            ls = slice(j0 // 16, (j0 + w) // 16)
-            n_w = ring.tile([P, w], F32, name="n_w", bufs=N_BUFS)
-            n_e = ring.tile([P, w], F32, name="n_e", bufs=N_BUFS)
-            nc.scalar.activation(out=n_w[:], in_=y_wins[t][:].indirect(west_t[:, ls]), func=ACT.Sigmoid, scale=-1.0)
-            nc.scalar.activation(out=n_e[:], in_=y_wins[t][:].indirect(east_t[:, ls]), func=ACT.Sigmoid, scale=-1.0)
-            for c0 in range(0, w, P):
+        def diffuse_y(t, j0, width):
+            u, r = divmod(t, 2)
+            entries = slice(j0 // LIST_ROWS, (j0 + width) // LIST_ROWS)
+            n_west = ring.tile([P, width], F32, name="n_west", bufs=3)
+            n_east = ring.tile([P, width], F32, name="n_east", bufs=3)
+            nc.scalar.activation(out=n_west[:], in_=y_windows[t][:].indirect(west_t[:, entries]), func=ACT.Sigmoid, scale=-1.0)
+            nc.scalar.activation(out=n_east[:], in_=y_windows[t][:].indirect(east_t[:, entries]), func=ACT.Sigmoid, scale=-1.0)
+            for c0 in range(0, width, P):
                 h, q = divmod((j0 + c0) // P, 2)
                 if (u, h) not in sum_banks:
                     sum_banks[(u, h)] = psum.tile([P, 2, 2, P], F32, name="bank")
-                terms = (a_negs[t][:, j0 + c0 : j0 + c0 + P], n_w[:, c0 : c0 + P], n_e[:, c0 : c0 + P])
+                terms = (y_terms[t][:, j0 + c0 : j0 + c0 + P], n_west[:, c0 : c0 + P], n_east[:, c0 : c0 + P])
                 for i, term in enumerate(terms):
-                    nc.tensor.matmul(sum_banks[(u, h)][:, q, r, :], term, ident[:], is_transpose=True, start=(i == 0), stop=(i == 2))
+                    nc.tensor.matmul(sum_banks[(u, h)][:, q, r, :], term, ident[:], is_transpose=True,
+                                     start=(i == 0), stop=(i == len(terms) - 1))
 
-        def turn_back(u, h, q):
-            if (u, h) in REUSE:
-                words = bs[3][:, HALF + P * q : HALF + P * (q + 1)] if FORCE else scratch[REUSE[(u, h)]][:, P * q : P * (q + 1)]
-            else:
-                pairs = ring.tile([P, P], F32, name="pairs", bufs=8)
-                words = pairs[:]
-            nc.vector.scalar_tensor_tensor(out=words.bitcast(BF16).rearrange("j (p e) -> j p e", e=2), in0=sum_banks[(u, h)][:, q].rearrange("j e p -> j p e"), scalar=2.5,
-                                           in1=g1_row[:, u], op0=ALU.subtract, op1=ALU.mult)
-            if u == 0 and (h == 1 or q == 0 or not SHARE0):
+        def turn_back(u, h, q, words):
+            nc.vector.scalar_tensor_tensor(
+                out=words.bitcast(BF16).rearrange("j (p r) -> j p r", r=2),
+                in0=sum_banks[(u, h)][:, q].rearrange("j r p -> j p r"), scalar=2.5,
+                in1=g1_row[:, u], op0=ALU.subtract, op1=ALU.mult,
+            )
+            if (h, q) not in word_banks:
                 word_banks[(h, q)] = psum.tile([P, 2, 2, P], F32, name="bank")
-            if u == 0 and h == 0 and q == 1 and SHARE0:
-                word_banks[(h, q)] = word_banks[(h, 0)]
+                if h == 0:
+                    word_banks[(h, 1)] = word_banks[(h, q)]
             nc.tensor.transpose(word_banks[(h, q)][:, q, u, :], words, ident[:])
 
-        out_rows = out_0.rearrange("(p t) j -> p t j", t=PACK)
-        o_words = keep.tile([P, S], I32, name="o_words", align_bytes=64)
-        o_scales = keep.tile([P, S], U8, name="o_scales", align_bytes=64)
+        def fresh_words():
+            return ring.tile([P, P], F32, name="words", bufs=8)[:]
 
-        def quantise(woven, w, nm):
-            c = ring.tile([P, w], U32, name=nm + "_codes", align_bytes=64, bufs=3)
-            s = ring.tile([P, w], U8, name=nm + "_scales", align_bytes=64, bufs=3)
-            nc.vector.quantize_mx(out=c[:].bitcast(FP8X4), scales=s[:], in_=woven)
-            return c, s
+        out_rows = out_0.rearrange("(p t) j -> p t j", t=SLOTS)
+        out_codes = keep.tile([P, CELLS], I32, name="out_codes", align_bytes=64)
+        out_scale = keep.tile([P, CELLS], U8, name="out_scale", align_bytes=64)
 
-        made = {}
+        def quantise(woven, width, name):
+            codes = ring.tile([P, width], U32, name=name + "_codes", align_bytes=64, bufs=PARTS)
+            scale = ring.tile([P, width], U8, name=name + "_scale", align_bytes=64, bufs=PARTS)
+            nc.vector.quantize_mx(out=codes[:].bitcast(FP8X4), scales=scale[:], in_=woven)
+            return codes, scale
 
-        def weave2(h, qs):
-            w = P * len(qs)
-            z2_src = z2_rows[:].rearrange("p (t j) -> p j t", t=PACK)[:, HALF * h + P * qs[0] : HALF * h + P * qs[0] + w, :]
-            z2_woven = ring.tile([P, w, PACK], BF16, name="z2_woven", align_bytes=64, bufs=3)
-            dst = z2_woven[:].rearrange("p (c i) t -> p c t i", i=4)
-            src = z2_src.rearrange("p (c i) t -> p c t i", i=4)
-            if (h, qs[0]) in ZW_S:
+        def quantise_z2(j0, width):
+            rows = z2_rows[:].rearrange("p (t j) -> p j t", t=SLOTS)[:, j0 : j0 + width, :]
+            woven = ring.tile([P, width, SLOTS], BF16, name="z2_woven", align_bytes=64, bufs=PARTS)
+            dst = woven[:].rearrange("p (c i) t -> p c t i", i=LINE)
+            src = rows.rearrange("p (c i) t -> p c t i", i=LINE)
+            if j0 == 0:
                 nc.scalar.activation(out=dst, in_=src, func=ACT.Copy, scale=0.125)
             else:
                 nc.vector.tensor_scalar_mul(out=dst, in0=src, scalar1=0.125)
-            made[("z2", h, qs[0])] = quantise(z2_woven[:].rearrange("p j t -> p (j t)"), w, "z2")
+            return quantise(woven[:].rearrange("p j t -> p (j t)"), width, "z2")
 
-        def weave1(h, qs):
-            w = P * len(qs)
-            z_woven = ring.tile([P, w * PACK], BF16, name="z_woven", align_bytes=64, bufs=3)
-            z_words = z_woven[:].bitcast(F32).rearrange("p (q j u) -> p q j u", u=2, j=P)
-            turned = word_banks[(h, qs[0])][:, qs[0] : qs[0] + len(qs)].rearrange("p q u j -> p q j u")
-            if (h, qs[0]) in ZC_V:
-                nc.vector.tensor_copy(out=z_words, in_=turned)
-            else:
-                nc.scalar.copy(out=z_words, in_=turned)
-            made[("z", h, qs[0])] = quantise(z_woven[:], w, "z")
+        def quantise_z(j0, width):
+            h, q = divmod(j0 // P, 2)
+            woven = ring.tile([P, width * SLOTS], BF16, name="z_woven", align_bytes=64, bufs=PARTS)
+            nc.scalar.copy(
+                out=woven[:].bitcast(F32).rearrange("p (q j u) -> p q j u", u=2, j=P),
+                in_=word_banks[(h, q)][:, q : q + width // P].rearrange("p q u j -> p q j u"),
+            )
+            return quantise(woven[:], width, "z")
 
-        def project(h, qs):
-            w = P * len(qs)
-            j0 = HALF * h + P * qs[0]
-            js = slice(j0, j0 + w)
-            z_c, z_s = made[("z", h, qs[0])]
-            z2_c, z2_s = made[("z2", h, qs[0])]
-            o_f32 = ring.tile([P, PACK, w], F32, name="o_f32", bufs=3)
-            if h == 0 and SPLIT0:
-                accs = [psum.tile([P, w], F32, name="bank") for r in range(PACK)]
-                for r in range(PACK):
-                    cols = slice(P * r, P * (r + 1))
-                    nc.tensor.matmul_mx(out=accs[r][:], lhsT=w4[:, cols].bitcast(FP8X4), lhsT_scale=s34[12:P, cols],
-                                        rhs=z2_c[:].bitcast(FP8X4), rhs_scale=z2_s[:], start=True, stop=False)
-                for r in range(PACK):
-                    cols = slice(P * r, P * (r + 1))
-                    nc.tensor.matmul_mx(out=accs[r][:], lhsT=w3[:, cols].bitcast(FP8X4), lhsT_scale=s34[8:P, cols],
-                                        rhs=z_c[:].bitcast(FP8X4), rhs_scale=z_s[:], start=False, stop=True)
-                    nc.scalar.copy(out=o_f32[:, r, :], in_=accs[r][:])
-            per_bank = S // w
-            for b0 in range(0, 0 if h == 0 and SPLIT0 else PACK, per_bank):
-                acc = psum.tile([P, per_bank, w], F32, name="bank")
-                for r in range(per_bank):
-                    cols = slice(P * (b0 + r), P * (b0 + r + 1))
-                    nc.tensor.matmul_mx(out=acc[:, r, :], lhsT=w3[:, cols].bitcast(FP8X4), lhsT_scale=s34[8:P, cols],
-                                        rhs=z_c[:].bitcast(FP8X4), rhs_scale=z_s[:], start=True, stop=False)
-                    nc.tensor.matmul_mx(out=acc[:, r, :], lhsT=w4[:, cols].bitcast(FP8X4), lhsT_scale=s34[12:P, cols],
-                                        rhs=z2_c[:].bitcast(FP8X4), rhs_scale=z2_s[:], start=False, stop=True)
-                nc.scalar.copy(out=o_f32[:, b0 : b0 + per_bank, :], in_=acc[:])
-            nc.sync.dma_start(out=out_rows[:, :, js], in_=o_f32[:])
-            made[("o", h, qs[0])] = o_f32
+        def times_w3(acc, t, z, start):
+            cols = slice(P * t, P * (t + 1))
+            nc.tensor.matmul_mx(out=acc, lhsT=w3[:, cols].bitcast(FP8X4), lhsT_scale=s34[8:P, cols],
+                                rhs=z[0][:].bitcast(FP8X4), rhs_scale=z[1][:], start=start, stop=not start)
 
-        def planes(h, qs):
-            w = P * len(qs)
-            j0 = HALF * h + P * qs[0]
-            js = slice(j0, j0 + w)
-            o_f32 = made[("o", h, qs[0])]
-            o_woven = ring.tile([P, w, PACK], BF16, name="o_woven", align_bytes=64, bufs=3)
-            dst = o_woven[:].rearrange("p (c i) t -> p c t i", i=4)
-            src = o_f32[:].rearrange("p t (c i) -> p c t i", i=4)
-            if (h, qs[0]) in OW_S:
-                nc.scalar.copy(out=dst, in_=src)
-            else:
-                nc.vector.tensor_copy(out=dst, in_=src)
-            nc.vector.quantize_mx(out=o_words[:, js].bitcast(FP8X4), scales=o_scales[:, js],
-                                  in_=o_woven[:].rearrange("p j t -> p (j t)"))
-            if j0 + w in (HALF, S):
-                done = slice(HALF * h, HALF * (h + 1))
-                nc.sync.dma_start(out=words_of(out_1)[:, done], in_=o_words[:, done])
+        def times_w4(acc, t, z2, start):
+            cols = slice(P * t, P * (t + 1))
+            nc.tensor.matmul_mx(out=acc, lhsT=w4[:, cols].bitcast(FP8X4), lhsT_scale=s34[12:P, cols],
+                                rhs=z2[0][:].bitcast(FP8X4), rhs_scale=z2[1][:], start=start, stop=not start)
+
+        def project_first_half(z, z2):
+            result = ring.tile([P, SLOTS, HALF], F32, name="result", bufs=PARTS)
+            accs = [psum.tile([P, HALF], F32, name="bank") for t in range(SLOTS)]
+            for t in range(SLOTS):
+                times_w4(accs[t][:], t, z2, True)
+            for t in range(SLOTS):
+                times_w3(accs[t][:], t, z, False)
+                nc.scalar.copy(out=result[:, t, :], in_=accs[t][:])
+            nc.sync.dma_start(out=out_rows[:, :, 0:HALF], in_=result[:])
+            return result
+
+        def project_quarter(j0, z, z2):
+            result = ring.tile([P, SLOTS, P], F32, name="result", bufs=PARTS)
+            for u in range(2):
+                acc = psum.tile([P, 2, P], F32, name="bank")
+                for r in range(2):
+                    times_w3(acc[:, r, :], 2 * u + r, z, True)
+                    times_w4(acc[:, r, :], 2 * u + r, z2, False)
+                nc.scalar.copy(out=result[:, 2 * u : 2 * u + 2, :], in_=acc[:])
+            nc.sync.dma_start(out=out_rows[:, :, j0 : j0 + P], in_=result[:])
+            return result
+
+        def quantise_result(j0, width, result):
+            cells = slice(j0, j0 + width)
+            woven = ring.tile([P, width, SLOTS], BF16, name="out_woven", align_bytes=64, bufs=PARTS)
+            nc.vector.tensor_copy(out=woven[:].rearrange("p (c i) t -> p c t i", i=LINE),
+                                  in_=result[:].rearrange("p t (c i) -> p c t i", i=LINE))
+            nc.vector.quantize_mx(out=out_codes[:, cells].bitcast(FP8X4), scales=out_scale[:, cells],
+                                  in_=woven[:].rearrange("p j t -> p (j t)"))
+
+        def store_codes(cells):
+            nc.sync.dma_start(out=words_of(out_1)[:, cells], in_=out_codes[:, cells])
 
         react(0)
-        diffuse_e(0, 0)
-        react(1)
-        diffuse_y(0, 0)
-        diffuse_e(1, 0)
-        react(2)
-        s34 = deal(nc.vector, s_raw, U8, "e_win0")
-        diffuse_y(1, 0)
-        diffuse_e(2, 0)
-        react(3)
-        diffuse_y(2, 0)
-        turn_back(0, 0, 0)
-        turn_back(0, 0, 1)
-        turn_back(0, 1, 0)
-        turn_back(0, 1, 1)
-        diffuse_y(3, 0)
-        diffuse_y(3, 1)
-        diffuse_e(3, 0)
-        turn_back(1, 0, 0)
-        turn_back(1, 0, 1)
-        weave2(0, [0, 1])
-        weave1(0, [0, 1])
-        diffuse_e(3, 1)
-        turn_back(1, 1, 0)
-        turn_back(1, 1, 1)
-        project(0, [0, 1])
-        weave2(1, [0])
-        weave1(1, [0])
-        weave2(1, [1])
-        weave1(1, [1])
-        project(1, [0])
-        project(1, [1])
-        planes(0, [0, 1])
-        planes(1, [0])
-        planes(1, [1])
-        for q, queue in enumerate((nc.scalar, nc.scalar, nc.sync, nc.sync)):
-            queue.dma_start(out=out_2[0, 4 * q : 4 * q + 4, :].bitcast(I32), in_=o_scales[32 * q : 32 * q + 4, :].bitcast(I32))
+        for t in range(LAST):
+            diffuse_v(t, 0, CELLS)
+            react(t + 1)
+            if t == 1:
+                s34 = keep.tile([P, FEATURES], U8, name="v_window0", align_bytes=64)
+                deal(s34, w_scales_raw, all_slots)
+            diffuse_y(t, 0, CELLS)
+
+        diffuse_y(LAST, 0, HALF)
+        diffuse_y(LAST, HALF, HALF)
+        turn_back(0, 0, 0, fresh_words())
+        spent = diffuse_v(LAST, 0, HALF)
+        turn_back(0, 0, 1, fresh_words())
+        for q in range(2):
+            turn_back(1, 0, q, spent[:, P * q : P * (q + 1)])
+        z2_first = quantise_z2(0, HALF)
+        z_first = quantise_z(0, HALF)
+
+        for u in range(2):
+            for q in range(2):
+                turn_back(u, 1, q, fresh_words())
+        diffuse_v(LAST, HALF, HALF)
+        result_first = project_first_half(z_first, z2_first)
+        quarters = (HALF, HALF + P)
+        z_late = [quantise_z(j0, P) for j0 in quarters]
+        z2_late = [quantise_z2(j0, P) for j0 in quarters]
+        results_late = [project_quarter(j0, z, z2) for j0, z, z2 in zip(quarters, z_late, z2_late)]
+
+        quantise_result(0, HALF, result_first)
+        store_codes(slice(0, HALF))
+        for j0, result in zip(quarters, results_late):
+            quantise_result(j0, P, result)
+        store_codes(slice(HALF, CELLS))
+        for q, queue in zip(QUADRANTS, (nc.scalar, nc.scalar, nc.sync, nc.sync)):
+            queue.dma_start(out=out_2[0, 4 * q : 4 * q + 4, :].bitcast(I32), in_=out_scale[32 * q : 32 * q + 4, :].bitcast(I32))

@@ -43,7 +43,10 @@ def tile_picked_grayscott_none_po_kernel(
     with ExitStack() as ctx:
         keep = ctx.enter_context(tc.tile_pool(name="keep", bufs=1))
         ring = ctx.enter_context(tc.tile_pool(name="ring", bufs=2))
-        psum = ctx.enter_context(tc.psum_pool(name="psum", bufs=8))
+        psum = ctx.enter_context(tc.psum_pool(name="psum", bufs=1))
+
+        def bank(number, shape):
+            return psum.tile(shape, F32, name="bank%d" % number)
 
         offs_t = keep.tile([P, CELLS // LIST_ROWS], U16, name="offs_t")
         west_t = keep.tile([P, CELLS // LIST_ROWS], U16, name="west_t")
@@ -61,21 +64,22 @@ def tile_picked_grayscott_none_po_kernel(
         nc.vector.memset(x_scale_table[:].bitcast(I32), 0)
 
         nc.sync.dma_start(offs_t[:], offs)
-        load_scale_rows(nc.sync, x_scale_rows, 0, x_scales, QUADRANTS)
-        load_scale_rows(nc.sync, w_scales_raw, 0, w1_scales, QUADRANTS[:2])
+        load_scale_rows(nc.scalar, x_scale_rows, 0, x_scales, QUADRANTS[:2])
+        load_scale_rows(nc.sync, x_scale_rows, 0, x_scales, QUADRANTS[2:])
+        load_scale_rows(nc.scalar, w_scales_raw, 0, w1_scales, QUADRANTS[:1])
+        load_scale_rows(nc.sync, w_scales_raw, 0, w1_scales, QUADRANTS[1:2])
         nc.sync.dma_start(out=x_table[:], in_=words_of(x_words))
+        load_scale_rows(nc.sync, w_scales_raw, 0, w1_scales, QUADRANTS[2:])
+        load_scale_rows(nc.sync, w_scales_raw, 4, w2_scales, QUADRANTS)
         nc.sync.dma_start(out=w_raw[0][:], in_=words_of(w1_words))
         nc.sync.dma_start(out=w_raw[1][:], in_=words_of(w2_words))
-        load_scale_rows(nc.sync, w_scales_raw, 0, w1_scales, QUADRANTS[2:])
-        load_scale_rows(nc.sync, w_scales_raw, 4, w2_scales, QUADRANTS[:3])
-        load_scale_rows(nc.gpsimd, w_scales_raw, 4, w2_scales, QUADRANTS[3:])
         make_identity(nc, ident[:])
-        nc.gpsimd.dma_start(out=g1_t[:], in_=g1.rearrange("(p t) o -> p (t o)", t=SLOTS))
         nc.sync.dma_start(out=w_raw[2][:], in_=words_of(w3_words))
         nc.sync.dma_start(out=w_raw[3][:], in_=words_of(w4_words))
         nc.sync.dma_start(out=g2_t[:], in_=g2.rearrange("(p t) o -> p (t o)", t=SLOTS))
         nc.sync.dma_start(west_t[:], west)
         nc.sync.dma_start(east_t[:], east)
+        nc.sync.dma_start(out=g1_t[:], in_=g1.rearrange("(p t) o -> p (t o)", t=SLOTS))
         for q in QUADRANTS:
             rows = slice(32 * q, 32 * q + 4)
             nc.vector.tensor_copy(out=x_scale_table[rows, :].bitcast(I32), in_=x_scale_rows[rows, :].bitcast(I32))
@@ -88,108 +92,139 @@ def tile_picked_grayscott_none_po_kernel(
 
         x_scale = keep.tile([P, CELLS], U8, name="x_scale", align_bytes=64)
         nc.vector.tensor_copy(out=x_scale[:], in_=x_scale_table[:].indirect(offs_t[:]))
-        x_codes = keep.tile([P, CELLS], U32, name="x_codes", align_bytes=64)
-        nc.vector.tensor_copy(out=x_codes[:], in_=x_table[:].bitcast(U32).indirect(offs_t[:]))
+        x_codes = []
+
+        def pick(h, name):
+            entries = slice(HALF * h // LIST_ROWS, HALF * (h + 1) // LIST_ROWS)
+            x_codes.append(keep.tile([P, HALF], U32, name=name, align_bytes=64))
+            nc.vector.tensor_copy(out=x_codes[h][:], in_=x_table[:].bitcast(U32).indirect(offs_t[:, entries]))
 
         s12 = keep.tile([P, FEATURES], U8, name="s12", align_bytes=64)
         w1 = keep.tile([P, FEATURES], I32, name="w1", align_bytes=64)
         w2 = keep.tile([P, FEATURES], I32, name="w2", align_bytes=64)
-        for slots in (slice(0, 1), slice(1, SLOTS)):
-            deal(s12, w_scales_raw, slots)
-            deal(w1, w_raw[0], slots)
-            deal(w2, w_raw[1], slots)
-        all_slots = slice(0, SLOTS)
         w3 = keep.tile([P, FEATURES], I32, name="w3", align_bytes=64)
-        deal(w3, w_raw[2], all_slots)
         w4 = keep.tile([P, FEATURES], I32, name="w4", align_bytes=64)
+        first_slot, other_slots, all_slots = slice(0, 1), slice(1, SLOTS), slice(0, SLOTS)
+        pick(0, "x_codes_first")
+        deal(s12, w_scales_raw, first_slot)
+        deal(w1, w_raw[0], all_slots)
+        pick(1, "w_raw0")
+        deal(w2, w_raw[1], all_slots)
+        deal(s12, w_scales_raw, other_slots)
+        deal(w3, w_raw[2], all_slots)
         deal(w4, w_raw[3], all_slots)
         load_scale_rows(nc.sync, w_scales_raw, 8, w3_scales, QUADRANTS)
         load_scale_rows(nc.sync, w_scales_raw, 12, w4_scales, QUADRANTS)
 
-        g1_bank = psum.tile([P, 2, 2, P], F32, name="bank")
-        for t in range(SLOTS):
-            nc.tensor.transpose(g1_bank[:, t // 2, t % 2, :], g1_t[:, t : t + 1].to_broadcast([P, P]), ident[:])
-        g1_row = keep.tile([P, 2, P, 2], F32, name="g1_row")
-        nc.scalar.activation(out=g1_row[:], in_=g1_bank[:].rearrange("j u r p -> j u p r"), func=ACT.Copy, scale=-0.25)
+        def first_product(acc, w, first_row, t, j0, width):
+            cols = slice(P * t, P * (t + 1))
+            for c0 in range(0, width, HALF):
+                cells = slice(j0 + c0, j0 + c0 + HALF)
+                nc.tensor.matmul_mx(out=acc[:, c0 : c0 + HALF], lhsT=w[:, cols].bitcast(FP8X4), lhsT_scale=s12[first_row:P, cols],
+                                    rhs=x_codes[(j0 + c0) // HALF][:].bitcast(FP8X4), rhs_scale=x_scale[:, cells],
+                                    start=True, stop=True)
 
-        y_windows, v_windows, y_terms, v_terms = [], [], [], []
+        logit_windows, v_windows, ys, es = [], [], [], []
+        for t in range(SLOTS):
+            if t < LAST:
+                logit_windows.append(keep.tile([P, 2 * CELLS], F32, name="logit_window%d" % t))
+                v_windows.append(keep.tile([P, 2 * CELLS], F32, name="v_window%d" % t, align_bytes=64))
+                ys.append(logit_windows[t][:, CELLS:])
+                es.append(v_windows[t][:, CELLS:])
+            else:
+                logit_windows.append(keep.tile([P, CELLS], F32, name="logit_window%d" % t))
+                v_windows.append(keep.tile([P, CELLS], F32, name="v_window%d" % t, align_bytes=64))
+                ys.append(keep.tile([P, CELLS], F32, name="y_last")[:])
+                es.append(keep.tile([P, CELLS], F32, name="e_last")[:])
+        y_terms = [keep.tile([P, CELLS], F32, name="y_term%d" % t) for t in range(SLOTS)]
+        v_terms = [keep.tile([P, CELLS], F32, name="v_term%d" % t) for t in range(SLOTS)]
+        ee4s = [keep.tile([P, CELLS], F32, name="ee4_%d" % t) for t in range(SLOTS)]
+        ye8s = [keep.tile([P, CELLS], F32, name="ye8_%d" % t) for t in range(SLOTS)]
+
+        Y_BANKS, E_BANKS = (None, 3, 0, 2), (2, 4, 1, 3)
+
+        def concentrations(t):
+            if t == 0:
+                for h in range(2):
+                    cells = slice(HALF * h, HALF * (h + 1))
+                    acc_y = bank(h, [P, HALF])
+                    first_product(acc_y[:], w1, 0, t, HALF * h, HALF)
+                    nc.scalar.activation(out=ys[t][:, cells], in_=acc_y[:], func=ACT.Sigmoid)
+                    nc.scalar.copy(out=logit_windows[t][:, cells], in_=acc_y[:])
+            else:
+                acc_y = bank(Y_BANKS[t], [P, CELLS])
+                first_product(acc_y[:], w1, 0, t, 0, CELLS)
+            acc_e = bank(E_BANKS[t], [P, CELLS])
+            first_product(acc_e[:], w2, 4, t, 0, CELLS)
+            if t > 0:
+                nc.scalar.activation(out=ys[t], in_=acc_y[:], func=ACT.Sigmoid)
+            nc.scalar.activation(out=es[t], in_=acc_e[:], func=ACT.Sigmoid)
+            if t > 0:
+                nc.scalar.copy(out=logit_windows[t][:, 0:CELLS], in_=acc_y[:])
+            nc.scalar.activation(out=ee4s[t][:], in_=es[t], func=ACT.Square, scale=2.0)
+
+        def weigh(t):
+            nc.vector.tensor_scalar_mul(out=v_windows[t][:, 0:CELLS], in0=es[t], scalar1=g2_t[:, t : t + 1])
+            nc.vector.scalar_tensor_tensor(out=ye8s[t][:], in0=ys[t], scalar=8.0, in1=es[t], op0=ALU.mult, op1=ALU.mult)
 
         def react(t):
-            cols = slice(P * t, P * (t + 1))
-            acc_y = psum.tile([P, CELLS], F32, name="bank")
-            nc.tensor.matmul_mx(out=acc_y[:], lhsT=w1[:, cols].bitcast(FP8X4), lhsT_scale=s12[:, cols],
-                                rhs=x_codes[:].bitcast(FP8X4), rhs_scale=x_scale[:], start=True, stop=True)
-            acc_e = psum.tile([P, CELLS], F32, name="bank")
-            nc.tensor.matmul_mx(out=acc_e[:], lhsT=w2[:, cols].bitcast(FP8X4), lhsT_scale=s12[4:P, cols],
-                                rhs=x_codes[:].bitcast(FP8X4), rhs_scale=x_scale[:], start=True, stop=True)
-            y_window = keep.tile([P, 2 * CELLS], F32, name="y_window%d" % t)
-            logit, y = y_window[:, 0:CELLS], y_window[:, CELLS : 2 * CELLS]
-            v_window = keep.tile([P, 2 * CELLS], F32, name="v_window%d" % t, align_bytes=64)
-            v, e = v_window[:, 0:CELLS], v_window[:, CELLS : 2 * CELLS]
-            ee4 = ring.tile([P, CELLS], F32, name="ee4")
-            ye8 = ring.tile([P, CELLS], F32, name="ye8")
-            y_term = keep.tile([P, CELLS], F32, name="y_term%d" % t)
-            v_term = keep.tile([P, CELLS], F32, name="v_term%d" % t)
-            nc.scalar.activation(out=y, in_=acc_y[:], func=ACT.Sigmoid)
-            nc.scalar.activation(out=e, in_=acc_e[:], func=ACT.Sigmoid)
-            if t == 0:
-                nc.vector.tensor_copy(out=logit, in_=acc_y[:])
-            nc.vector.tensor_scalar_mul(out=v, in0=e, scalar1=g2_t[:, t : t + 1])
-            nc.scalar.activation(out=ee4[:], in_=e, func=ACT.Square, scale=2.0)
-            if t > 0:
-                nc.scalar.copy(out=logit, in_=acc_y[:])
-            nc.vector.scalar_tensor_tensor(out=ye8[:], in0=y, scalar=8.0, in1=e, op0=ALU.mult, op1=ALU.mult)
-            nc.vector.scalar_tensor_tensor(out=v_term[:], in0=ye8[:], scalar=4.0, in1=v, op0=ALU.add, op1=ALU.mult)
-            nc.vector.scalar_tensor_tensor(out=y_term[:], in0=ee4[:], scalar=1.5, in1=y, op0=ALU.subtract, op1=ALU.mult)
-            y_windows.append(y_window)
-            v_windows.append(v_window)
-            y_terms.append(y_term)
-            v_terms.append(v_term)
+            nc.vector.scalar_tensor_tensor(out=v_terms[t][:], in0=ye8s[t][:], scalar=4.0, in1=v_windows[t][:, 0:CELLS],
+                                           op0=ALU.add, op1=ALU.mult)
+            nc.vector.scalar_tensor_tensor(out=y_terms[t][:], in0=ee4s[t][:], scalar=1.5, in1=ys[t],
+                                           op0=ALU.subtract, op1=ALU.mult)
 
         z2_rows = keep.tile([P, SLOTS * CELLS], F32, name="z2_rows")
+        partials = [keep.tile([P, CELLS], F32, name="partial%d" % t) for t in range(SLOTS)]
 
-        def diffuse_v(t, j0, width):
+        def v_from_west(t, j0, width):
             entries = slice(j0 // LIST_ROWS, (j0 + width) // LIST_ROWS)
-            partial = ring.tile([P, width], F32, name="partial", bufs=3)
-            nc.vector.tensor_tensor(partial[:], v_windows[t][:].indirect(west_t[:, entries]),
+            nc.vector.tensor_tensor(partials[t][:, j0 : j0 + width], v_windows[t][:].indirect(west_t[:, entries]),
                                     v_terms[t][:, j0 : j0 + width], ALU.add)
-            nc.vector.tensor_tensor(z2_rows[:, CELLS * t + j0 : CELLS * t + j0 + width],
-                                    v_windows[t][:].indirect(east_t[:, entries]), partial[:], ALU.add)
-            return partial
 
-        sum_banks = {}
-        word_banks = {}
+        def v_from_east(t, j0, width):
+            entries = slice(j0 // LIST_ROWS, (j0 + width) // LIST_ROWS)
+            nc.vector.tensor_tensor(z2_rows[:, CELLS * t + j0 : CELLS * t + j0 + width],
+                                    v_windows[t][:].indirect(east_t[:, entries]), partials[t][:, j0 : j0 + width], ALU.add)
+
+        sums = {}
+
+        def open_sums(number, u, quarters):
+            tile = bank(number, [P, 2, len(quarters), P])
+            for i, c in enumerate(quarters):
+                sums[(u, c)] = (tile, i)
 
         def diffuse_y(t, j0, width):
             u, r = divmod(t, 2)
             entries = slice(j0 // LIST_ROWS, (j0 + width) // LIST_ROWS)
             n_west = ring.tile([P, width], F32, name="n_west", bufs=3)
             n_east = ring.tile([P, width], F32, name="n_east", bufs=3)
-            nc.scalar.activation(out=n_west[:], in_=y_windows[t][:].indirect(west_t[:, entries]), func=ACT.Sigmoid, scale=-1.0)
-            nc.scalar.activation(out=n_east[:], in_=y_windows[t][:].indirect(east_t[:, entries]), func=ACT.Sigmoid, scale=-1.0)
+            nc.scalar.activation(out=n_west[:], in_=logit_windows[t][:].indirect(west_t[:, entries]), func=ACT.Sigmoid, scale=-1.0)
+            nc.scalar.activation(out=n_east[:], in_=logit_windows[t][:].indirect(east_t[:, entries]), func=ACT.Sigmoid, scale=-1.0)
             for c0 in range(0, width, P):
-                h, q = divmod((j0 + c0) // P, 2)
-                if (u, h) not in sum_banks:
-                    sum_banks[(u, h)] = psum.tile([P, 2, 2, P], F32, name="bank")
+                tile, i = sums[(u, (j0 + c0) // P)]
                 terms = (y_terms[t][:, j0 + c0 : j0 + c0 + P], n_west[:, c0 : c0 + P], n_east[:, c0 : c0 + P])
-                for i, term in enumerate(terms):
-                    nc.tensor.matmul(sum_banks[(u, h)][:, q, r, :], term, ident[:], is_transpose=True,
-                                     start=(i == 0), stop=(i == len(terms) - 1))
+                for k, term in enumerate(terms):
+                    nc.tensor.matmul(tile[:, r, i, :], term, ident[:], is_transpose=True,
+                                     start=(k == 0), stop=(k == len(terms) - 1))
 
-        def turn_back(u, h, q, words):
+        turned = {}
+
+        def open_turned(number, quarters):
+            tile = bank(number, [P, len(quarters), 2, P])
+            for i, c in enumerate(quarters):
+                turned[c] = (tile, i)
+
+        def turn_back(u, c0, count):
+            tile, i = sums[(u, c0)]
+            words = ring.tile([P, count, P], F32, name="words", bufs=5)
             nc.vector.scalar_tensor_tensor(
-                out=words.bitcast(BF16).rearrange("j (p r) -> j p r", r=2),
-                in0=sum_banks[(u, h)][:, q].rearrange("j r p -> j p r"), scalar=2.5,
-                in1=g1_row[:, u], op0=ALU.subtract, op1=ALU.mult,
+                out=words[:].bitcast(BF16).rearrange("j c (p r) -> j c p r", r=2),
+                in0=tile[:, :, i : i + count, :].rearrange("j r c p -> j c p r"), scalar=2.5,
+                in1=g1_row[:, u : u + 1].to_broadcast([P, count, P, 2]), op0=ALU.subtract, op1=ALU.mult,
             )
-            if (h, q) not in word_banks:
-                word_banks[(h, q)] = psum.tile([P, 2, 2, P], F32, name="bank")
-                if h == 0:
-                    word_banks[(h, 1)] = word_banks[(h, q)]
-            nc.tensor.transpose(word_banks[(h, q)][:, q, u, :], words, ident[:])
-
-        def fresh_words():
-            return ring.tile([P, P], F32, name="words", bufs=8)[:]
+            for k in range(count):
+                back, place = turned[c0 + k]
+                nc.tensor.transpose(back[:, place, u, :], words[:, k, :], ident[:])
 
         out_rows = out_0.rearrange("(p t) j -> p t j", t=SLOTS)
         out_codes = keep.tile([P, CELLS], I32, name="out_codes", align_bytes=64)
@@ -201,56 +236,41 @@ def tile_picked_grayscott_none_po_kernel(
             nc.vector.quantize_mx(out=codes[:].bitcast(FP8X4), scales=scale[:], in_=woven)
             return codes, scale
 
-        def quantise_z2(j0, width):
+        def weave_z2(j0, width, on_scalar):
             rows = z2_rows[:].rearrange("p (t j) -> p j t", t=SLOTS)[:, j0 : j0 + width, :]
             woven = ring.tile([P, width, SLOTS], BF16, name="z2_woven", align_bytes=64, bufs=PARTS)
             dst = woven[:].rearrange("p (c i) t -> p c t i", i=LINE)
             src = rows.rearrange("p (c i) t -> p c t i", i=LINE)
-            if j0 == 0:
+            if on_scalar:
                 nc.scalar.activation(out=dst, in_=src, func=ACT.Copy, scale=0.125)
             else:
                 nc.vector.tensor_scalar_mul(out=dst, in0=src, scalar1=0.125)
-            return quantise(woven[:].rearrange("p j t -> p (j t)"), width, "z2")
+            return woven[:].rearrange("p j t -> p (j t)")
 
-        def quantise_z(j0, width):
-            h, q = divmod(j0 // P, 2)
-            woven = ring.tile([P, width * SLOTS], BF16, name="z_woven", align_bytes=64, bufs=PARTS)
+        def weave_z(c0, count):
+            back, place = turned[c0]
+            woven = ring.tile([P, count * P * SLOTS], BF16, name="z_woven", align_bytes=64, bufs=PARTS)
             nc.scalar.copy(
                 out=woven[:].bitcast(F32).rearrange("p (q j u) -> p q j u", u=2, j=P),
-                in_=word_banks[(h, q)][:, q : q + width // P].rearrange("p q u j -> p q j u"),
+                in_=back[:, place : place + count].rearrange("p q u j -> p q j u"),
             )
-            return quantise(woven[:], width, "z")
+            return woven[:]
 
-        def times_w3(acc, t, z, start):
-            cols = slice(P * t, P * (t + 1))
-            nc.tensor.matmul_mx(out=acc, lhsT=w3[:, cols].bitcast(FP8X4), lhsT_scale=s34[8:P, cols],
-                                rhs=z[0][:].bitcast(FP8X4), rhs_scale=z[1][:], start=start, stop=not start)
-
-        def times_w4(acc, t, z2, start):
-            cols = slice(P * t, P * (t + 1))
-            nc.tensor.matmul_mx(out=acc, lhsT=w4[:, cols].bitcast(FP8X4), lhsT_scale=s34[12:P, cols],
-                                rhs=z2[0][:].bitcast(FP8X4), rhs_scale=z2[1][:], start=start, stop=not start)
-
-        def project_first_half(z, z2):
-            result = ring.tile([P, SLOTS, HALF], F32, name="result", bufs=PARTS)
-            accs = [psum.tile([P, HALF], F32, name="bank") for t in range(SLOTS)]
+        def last_passes(accs, w, first_row, z, start):
+            per_bank = SLOTS // len(accs)
             for t in range(SLOTS):
-                times_w4(accs[t][:], t, z2, True)
-            for t in range(SLOTS):
-                times_w3(accs[t][:], t, z, False)
-                nc.scalar.copy(out=result[:, t, :], in_=accs[t][:])
-            nc.sync.dma_start(out=out_rows[:, :, 0:HALF], in_=result[:])
-            return result
+                cols = slice(P * t, P * (t + 1))
+                b, r = divmod(t, per_bank)
+                nc.tensor.matmul_mx(out=accs[b][:, r, :], lhsT=w[:, cols].bitcast(FP8X4), lhsT_scale=s34[first_row:P, cols],
+                                    rhs=z[0][:].bitcast(FP8X4), rhs_scale=z[1][:],
+                                    start=start and r == 0, stop=not start and r == per_bank - 1)
 
-        def project_quarter(j0, z, z2):
-            result = ring.tile([P, SLOTS, P], F32, name="result", bufs=PARTS)
-            for u in range(2):
-                acc = psum.tile([P, 2, P], F32, name="bank")
-                for r in range(2):
-                    times_w3(acc[:, r, :], 2 * u + r, z, True)
-                    times_w4(acc[:, r, :], 2 * u + r, z2, False)
-                nc.scalar.copy(out=result[:, 2 * u : 2 * u + 2, :], in_=acc[:])
-            nc.sync.dma_start(out=out_rows[:, :, j0 : j0 + P], in_=result[:])
+        def store_result(j0, width, accs):
+            result = ring.tile([P, SLOTS, width], F32, name="result", bufs=PARTS)
+            per_bank = SLOTS // len(accs)
+            for b, acc in enumerate(accs):
+                nc.scalar.copy(out=result[:, per_bank * b : per_bank * (b + 1), :], in_=acc[:])
+            nc.sync.dma_start(out=out_rows[:, :, j0 : j0 + width], in_=result[:])
             return result
 
         def quantise_result(j0, width, result):
@@ -264,34 +284,67 @@ def tile_picked_grayscott_none_po_kernel(
         def store_codes(cells):
             nc.sync.dma_start(out=words_of(out_1)[:, cells], in_=out_codes[:, cells])
 
+        concentrations(0)
+        weigh(0)
         react(0)
-        for t in range(LAST):
-            diffuse_v(t, 0, CELLS)
-            react(t + 1)
+        v_from_west(0, 0, CELLS)
+
+        g1_bank = bank(5, [P, 2, 2, P])
+        for t in range(SLOTS):
+            nc.tensor.transpose(g1_bank[:, t // 2, t % 2, :], g1_t[:, t : t + 1].to_broadcast([P, P]), ident[:])
+        g1_row = keep.tile([P, 2, P, 2], F32, name="g1_row")
+        nc.scalar.activation(out=g1_row[:], in_=g1_bank[:].rearrange("j u r p -> j u p r"), func=ACT.Copy, scale=-0.25)
+
+        open_sums(6, 0, (0, 1))
+        open_sums(7, 0, (2, 3))
+        for t in range(1, SLOTS):
+            concentrations(t)
+            weigh(t)
+            v_from_east(t - 1, 0, CELLS)
+            react(t)
             if t == 1:
                 s34 = keep.tile([P, FEATURES], U8, name="v_window0", align_bytes=64)
                 deal(s34, w_scales_raw, all_slots)
-            diffuse_y(t, 0, CELLS)
+            if t < LAST:
+                v_from_west(t, 0, CELLS)
+                diffuse_y(t - 1, 0, CELLS)
 
+        v_from_west(LAST, 0, HALF)
+        open_turned(0, (0, 1))
+        open_turned(1, (2,))
+        open_turned(2, (3,))
+        turn_back(0, 0, 2)
+        v_from_east(LAST, 0, HALF)
+        turn_back(0, 2, 2)
+        open_sums(4, 1, (0, 1))
+        open_sums(5, 1, (2,))
+        open_sums(6, 1, (3,))
+        diffuse_y(LAST - 1, 0, CELLS)
         diffuse_y(LAST, 0, HALF)
-        diffuse_y(LAST, HALF, HALF)
-        turn_back(0, 0, 0, fresh_words())
-        spent = diffuse_v(LAST, 0, HALF)
-        turn_back(0, 0, 1, fresh_words())
-        for q in range(2):
-            turn_back(1, 0, q, spent[:, P * q : P * (q + 1)])
-        z2_first = quantise_z2(0, HALF)
-        z_first = quantise_z(0, HALF)
+        diffuse_y(LAST, HALF, P)
+        diffuse_y(LAST, HALF + P, P)
 
-        for u in range(2):
-            for q in range(2):
-                turn_back(u, 1, q, fresh_words())
-        diffuse_v(LAST, HALF, HALF)
-        result_first = project_first_half(z_first, z2_first)
+        z2_first = quantise(weave_z2(0, HALF, False), HALF, "z2")
+        turn_back(1, 0, 2)
+        v_from_west(LAST, HALF, HALF)
+        first_accs = [bank(3, [P, 2, HALF]), bank(7, [P, 2, HALF])]
+        last_passes(first_accs, w4, 12, z2_first, True)
+        woven_first = weave_z(0, 2)
+        turn_back(1, 2, 1)
+        z_first = quantise(woven_first, HALF, "z")
+        last_passes(first_accs, w3, 8, z_first, False)
+        turn_back(1, 3, 1)
+        v_from_east(LAST, HALF, HALF)
+        woven_late = [weave_z(c, 1) for c in (2, 3)]
+        result_first = store_result(0, HALF, first_accs)
+        late_accs = [[bank(4, [P, SLOTS, P])], [bank(0, [P, SLOTS, P])]]
         quarters = (HALF, HALF + P)
-        z_late = [quantise_z(j0, P) for j0 in quarters]
-        z2_late = [quantise_z2(j0, P) for j0 in quarters]
-        results_late = [project_quarter(j0, z, z2) for j0, z, z2 in zip(quarters, z_late, z2_late)]
+        for i in range(2):
+            last_passes(late_accs[i], w3, 8, quantise(woven_late[i], P, "z"), True)
+        woven_z2 = [weave_z2(j0, P, False) for j0 in quarters]
+        for i in range(2):
+            last_passes(late_accs[i], w4, 12, quantise(woven_z2[i], P, "z2"), False)
+        results_late = [store_result(j0, P, accs) for j0, accs in zip(quarters, late_accs)]
 
         quantise_result(0, HALF, result_first)
         store_codes(slice(0, HALF))

@@ -99,18 +99,19 @@ def tile_picked_grayscott_none_po_kernel(
             x_codes.append(keep.tile([P, HALF], U32, name=name, align_bytes=64))
             nc.vector.tensor_copy(out=x_codes[h][:], in_=x_table[:].bitcast(U32).indirect(offs_t[:, entries]))
 
-        s12 = keep.tile([P, FEATURES], U8, name="s12", align_bytes=64)
+        s12_first = keep.tile([P, FEATURES], U8, name="s12_first", align_bytes=64)
         w1 = keep.tile([P, FEATURES], I32, name="w1", align_bytes=64)
         w2 = keep.tile([P, FEATURES], I32, name="w2", align_bytes=64)
         w3 = keep.tile([P, FEATURES], I32, name="w3", align_bytes=64)
         w4 = keep.tile([P, FEATURES], I32, name="w4", align_bytes=64)
         first_slot, other_slots, all_slots = slice(0, 1), slice(1, SLOTS), slice(0, SLOTS)
         pick(0, "x_codes_first")
-        deal(s12, w_scales_raw, first_slot)
+        deal(s12_first, w_scales_raw, first_slot)
         deal(w1, w_raw[0], all_slots)
         pick(1, "w_raw0")
         deal(w2, w_raw[1], all_slots)
-        deal(s12, w_scales_raw, other_slots)
+        s12_others = keep.tile([P, FEATURES], U8, name="w_raw1", align_bytes=64)
+        deal(s12_others, w_scales_raw, other_slots)
         deal(w3, w_raw[2], all_slots)
         deal(w4, w_raw[3], all_slots)
         load_scale_rows(nc.sync, w_scales_raw, 8, w3_scales, QUADRANTS)
@@ -118,6 +119,7 @@ def tile_picked_grayscott_none_po_kernel(
 
         def first_product(acc, w, first_row, t, j0, width):
             cols = slice(P * t, P * (t + 1))
+            s12 = s12_first if t == 0 else s12_others
             for c0 in range(0, width, HALF):
                 cells = slice(j0 + c0, j0 + c0 + HALF)
                 nc.tensor.matmul_mx(out=acc[:, c0 : c0 + HALF], lhsT=w[:, cols].bitcast(FP8X4), lhsT_scale=s12[first_row:P, cols],
@@ -136,76 +138,103 @@ def tile_picked_grayscott_none_po_kernel(
                 v_windows.append(keep.tile([P, CELLS], F32, name="v_window%d" % t, align_bytes=64))
                 ys.append(keep.tile([P, CELLS], F32, name="y_last")[:])
                 es.append(keep.tile([P, CELLS], F32, name="e_last")[:])
+        ees = [keep.tile([P, CELLS], F32, name="ee4_%d" % t)[:] for t in range(SLOTS)]
         y_terms = [keep.tile([P, CELLS], F32, name="y_term%d" % t) for t in range(SLOTS)]
         v_terms = [keep.tile([P, CELLS], F32, name="v_term%d" % t) for t in range(SLOTS)]
-        ee4s = [keep.tile([P, CELLS], F32, name="ee4_%d" % t) for t in range(SLOTS)]
         ye8s = [keep.tile([P, CELLS], F32, name="ye8_%d" % t) for t in range(SLOTS)]
 
-        Y_BANKS, E_BANKS = (None, 3, 0, 2), (2, 4, 1, 3)
+        Y_BANKS, E_BANKS = (None, 5, 0, 2), (None, 4, 3, 4)
+        V_ON_SCALAR = ()
 
         def concentrations(t):
             if t == 0:
+                halves_y = []
                 for h in range(2):
                     cells = slice(HALF * h, HALF * (h + 1))
-                    acc_y = bank(h, [P, HALF])
-                    first_product(acc_y[:], w1, 0, t, HALF * h, HALF)
-                    nc.scalar.activation(out=ys[t][:, cells], in_=acc_y[:], func=ACT.Sigmoid)
-                    nc.scalar.copy(out=logit_windows[t][:, cells], in_=acc_y[:])
-            else:
-                acc_y = bank(Y_BANKS[t], [P, CELLS])
-                first_product(acc_y[:], w1, 0, t, 0, CELLS)
+                    halves_y.append(bank(2 * h, [P, HALF]))
+                    first_product(halves_y[h][:], w1, 0, t, HALF * h, HALF)
+                    nc.scalar.activation(out=ys[t][:, cells], in_=halves_y[h][:], func=ACT.Sigmoid)
+                    half_e = bank(2 * h + 1, [P, HALF])
+                    first_product(half_e[:], w2, 4, t, HALF * h, HALF)
+                    nc.scalar.activation(out=es[t][:, cells], in_=half_e[:], func=ACT.Sigmoid)
+                nc.scalar.copy(out=logit_windows[t][:, 0:HALF], in_=halves_y[0][:])
+                nc.scalar.activation(out=ees[t], in_=es[t], func=ACT.Square, scale=2.0)
+                nc.scalar.copy(out=logit_windows[t][:, HALF:CELLS], in_=halves_y[1][:])
+                return
             acc_e = bank(E_BANKS[t], [P, CELLS])
             first_product(acc_e[:], w2, 4, t, 0, CELLS)
-            if t > 0:
-                nc.scalar.activation(out=ys[t], in_=acc_y[:], func=ACT.Sigmoid)
             nc.scalar.activation(out=es[t], in_=acc_e[:], func=ACT.Sigmoid)
+            acc_y = bank(Y_BANKS[t], [P, CELLS])
+            first_product(acc_y[:], w1, 0, t, 0, CELLS)
+            nc.scalar.activation(out=ys[t], in_=acc_y[:], func=ACT.Sigmoid)
+            if t in V_ON_SCALAR:
+                nc.scalar.activation(out=v_windows[t][:, 0:CELLS], in_=es[t], func=ACT.Copy, scale=g2_t[:, t : t + 1])
+            nc.scalar.activation(out=ees[t], in_=es[t], func=ACT.Square, scale=2.0)
             if t > 0:
                 nc.scalar.copy(out=logit_windows[t][:, 0:CELLS], in_=acc_y[:])
-            nc.scalar.activation(out=ee4s[t][:], in_=es[t], func=ACT.Square, scale=2.0)
 
-        def weigh(t):
-            nc.vector.tensor_scalar_mul(out=v_windows[t][:, 0:CELLS], in0=es[t], scalar1=g2_t[:, t : t + 1])
-            nc.vector.scalar_tensor_tensor(out=ye8s[t][:], in0=ys[t], scalar=8.0, in1=es[t], op0=ALU.mult, op1=ALU.mult)
+        def weigh(t, j0=0, width=CELLS):
+            if t not in V_ON_SCALAR:
+                cells = slice(j0, j0 + width)
+                nc.vector.tensor_scalar_mul(out=v_windows[t][:, cells], in0=es[t][:, cells], scalar1=g2_t[:, t : t + 1])
 
-        def react(t):
+        def product_term(t, j0=0, width=CELLS):
+            cells = slice(j0, j0 + width)
+            nc.vector.scalar_tensor_tensor(out=ye8s[t][:, cells], in0=ys[t][:, cells], scalar=8.0, in1=es[t][:, cells],
+                                           op0=ALU.mult, op1=ALU.mult)
+
+        def own_e_term(t):
             nc.vector.scalar_tensor_tensor(out=v_terms[t][:], in0=ye8s[t][:], scalar=4.0, in1=v_windows[t][:, 0:CELLS],
                                            op0=ALU.add, op1=ALU.mult)
-            nc.vector.scalar_tensor_tensor(out=y_terms[t][:], in0=ee4s[t][:], scalar=1.5, in1=ys[t],
-                                           op0=ALU.subtract, op1=ALU.mult)
+
+        def own_y_term(t):
+            nc.vector.scalar_tensor_tensor(out=y_terms[t][:], in0=ees[t], scalar=1.5, in1=ys[t], op0=ALU.subtract, op1=ALU.mult)
+
+        def by_halves(step, t):
+            step(t, 0, HALF)
+            step(t, HALF, HALF)
 
         z2_rows = keep.tile([P, SLOTS * CELLS], F32, name="z2_rows")
-        partials = [keep.tile([P, CELLS], F32, name="partial%d" % t) for t in range(SLOTS)]
+        partials = {}
 
         def v_from_west(t, j0, width):
             entries = slice(j0 // LIST_ROWS, (j0 + width) // LIST_ROWS)
-            nc.vector.tensor_tensor(partials[t][:, j0 : j0 + width], v_windows[t][:].indirect(west_t[:, entries]),
+            late = t == LAST and j0 == HALF
+            partials[(t, j0)] = keep.tile([P, width], F32, name="words1_2" if late else "partial%d_%d" % (t, j0), align_bytes=64)
+            nc.vector.tensor_tensor(partials[(t, j0)][:], v_windows[t][:].indirect(west_t[:, entries]),
                                     v_terms[t][:, j0 : j0 + width], ALU.add)
 
         def v_from_east(t, j0, width):
             entries = slice(j0 // LIST_ROWS, (j0 + width) // LIST_ROWS)
             nc.vector.tensor_tensor(z2_rows[:, CELLS * t + j0 : CELLS * t + j0 + width],
-                                    v_windows[t][:].indirect(east_t[:, entries]), partials[t][:, j0 : j0 + width], ALU.add)
+                                    v_windows[t][:].indirect(east_t[:, entries]), partials[(t, j0)][:], ALU.add)
 
         sums = {}
 
         def open_sums(number, u, quarters):
             tile = bank(number, [P, 2, len(quarters), P])
             for i, c in enumerate(quarters):
-                sums[(u, c)] = (tile, i)
+                sums[(u, c)] = (tile, i, len(quarters))
+
+        def add_terms(t, c, terms, first, last):
+            u, r = divmod(t, 2)
+            tile, i, count = sums[(u, c)]
+            for k, term in enumerate(terms):
+                nc.tensor.matmul(tile[:, r, i, :], term, ident[:], is_transpose=True,
+                                 start=(first and k == 0 and r == 0 and i == 0),
+                                 stop=(last and k == len(terms) - 1 and r == 1 and i == count - 1))
+
+        def local_terms(t):
+            for c in range(SLOTS):
+                add_terms(t, c, [y_terms[t][:, P * c : P * (c + 1)]], True, False)
 
         def diffuse_y(t, j0, width):
-            u, r = divmod(t, 2)
             entries = slice(j0 // LIST_ROWS, (j0 + width) // LIST_ROWS)
-            n_west = ring.tile([P, width], F32, name="n_west", bufs=3)
-            n_east = ring.tile([P, width], F32, name="n_east", bufs=3)
-            nc.scalar.activation(out=n_west[:], in_=logit_windows[t][:].indirect(west_t[:, entries]), func=ACT.Sigmoid, scale=-1.0)
-            nc.scalar.activation(out=n_east[:], in_=logit_windows[t][:].indirect(east_t[:, entries]), func=ACT.Sigmoid, scale=-1.0)
-            for c0 in range(0, width, P):
-                tile, i = sums[(u, (j0 + c0) // P)]
-                terms = (y_terms[t][:, j0 + c0 : j0 + c0 + P], n_west[:, c0 : c0 + P], n_east[:, c0 : c0 + P])
-                for k, term in enumerate(terms):
-                    nc.tensor.matmul(tile[:, r, i, :], term, ident[:], is_transpose=True,
-                                     start=(k == 0), stop=(k == len(terms) - 1))
+            for lists, last in ((west_t, False), (east_t, True)):
+                near = keep.tile([P, width], F32, name="near%d_%d_%d" % (t, j0, last), align_bytes=64)
+                nc.scalar.activation(out=near[:], in_=logit_windows[t][:].indirect(lists[:, entries]), func=ACT.Sigmoid, scale=-1.0)
+                for c0 in range(0, width, P):
+                    add_terms(t, (j0 + c0) // P, [near[:, c0 : c0 + P]], False, last)
 
         turned = {}
 
@@ -215,12 +244,12 @@ def tile_picked_grayscott_none_po_kernel(
                 turned[c] = (tile, i)
 
         def turn_back(u, c0, count):
-            tile, i = sums[(u, c0)]
-            words = ring.tile([P, count, P], F32, name="words", bufs=5)
+            tile, i, whole = sums[(u, c0)]
+            words = keep.tile([P, count, P], F32, name="words%d_%d" % (u, c0), align_bytes=64)
             nc.vector.scalar_tensor_tensor(
                 out=words[:].bitcast(BF16).rearrange("j c (p r) -> j c p r", r=2),
-                in0=tile[:, :, i : i + count, :].rearrange("j r c p -> j c p r"), scalar=2.5,
-                in1=g1_row[:, u : u + 1].to_broadcast([P, count, P, 2]), op0=ALU.subtract, op1=ALU.mult,
+                in0=tile[:, :, i : i + count, :].rearrange("j r c p -> j c p r"), scalar=-2.5,
+                in1=g1_row[:, u : u + 1].to_broadcast([P, count, P, 2]), op0=ALU.add, op1=ALU.mult,
             )
             for k in range(count):
                 back, place = turned[c0 + k]
@@ -230,8 +259,11 @@ def tile_picked_grayscott_none_po_kernel(
         out_codes = keep.tile([P, CELLS], I32, name="out_codes", align_bytes=64)
         out_scale = keep.tile([P, CELLS], U8, name="out_scale", align_bytes=64)
 
-        def quantise(woven, width, name):
-            codes = ring.tile([P, width], U32, name=name + "_codes", align_bytes=64, bufs=PARTS)
+        def quantise(woven, width, name, codes_name=None):
+            if codes_name:
+                codes = keep.tile([P, width], U32, name=codes_name, align_bytes=64)
+            else:
+                codes = ring.tile([P, width], U32, name=name + "_codes", align_bytes=64, bufs=PARTS)
             scale = ring.tile([P, width], U8, name=name + "_scale", align_bytes=64, bufs=PARTS)
             nc.vector.quantize_mx(out=codes[:].bitcast(FP8X4), scales=scale[:], in_=woven)
             return codes, scale
@@ -284,63 +316,80 @@ def tile_picked_grayscott_none_po_kernel(
         def store_codes(cells):
             nc.sync.dma_start(out=words_of(out_1)[:, cells], in_=out_codes[:, cells])
 
-        concentrations(0)
-        weigh(0)
-        react(0)
-        v_from_west(0, 0, CELLS)
+        def vector_work(t):
+            if t > 0:
+                weigh(t)
+                product_term(t)
+                v_from_east(t - 1, 0, CELLS)
+            else:
+                for j0 in (0, HALF):
+                    weigh(t, j0, HALF)
+                    product_term(t, j0, HALF)
+            own_e_term(t)
+            own_y_term(t)
+            v_from_west(t, 0, CELLS)
 
-        g1_bank = bank(5, [P, 2, 2, P])
+        open_sums(6, 0, (0, 1))
+        open_sums(7, 0, (2, 3))
+        for t in range(2):
+            concentrations(t)
+            vector_work(t)
+        local_terms(0)
+        g1_bank = bank(1, [P, 2, 2, P])
         for t in range(SLOTS):
             nc.tensor.transpose(g1_bank[:, t // 2, t % 2, :], g1_t[:, t : t + 1].to_broadcast([P, P]), ident[:])
         g1_row = keep.tile([P, 2, P, 2], F32, name="g1_row")
         nc.scalar.activation(out=g1_row[:], in_=g1_bank[:].rearrange("j u r p -> j u p r"), func=ACT.Copy, scale=-0.25)
+        s34 = keep.tile([P, FEATURES], U8, name="v_window0", align_bytes=64)
+        deal(s34, w_scales_raw, all_slots)
+        diffuse_y(0, 0, CELLS)
+        local_terms(1)
 
-        open_sums(6, 0, (0, 1))
-        open_sums(7, 0, (2, 3))
-        for t in range(1, SLOTS):
-            concentrations(t)
-            weigh(t)
-            v_from_east(t - 1, 0, CELLS)
-            react(t)
-            if t == 1:
-                s34 = keep.tile([P, FEATURES], U8, name="v_window0", align_bytes=64)
-                deal(s34, w_scales_raw, all_slots)
-            if t < LAST:
-                v_from_west(t, 0, CELLS)
-                diffuse_y(t - 1, 0, CELLS)
-
-        v_from_west(LAST, 0, HALF)
+        concentrations(2)
+        vector_work(2)
+        diffuse_y(1, 0, CELLS)
+        open_sums(5, 1, (0, 1))
+        open_sums(1, 1, (2,))
+        open_sums(3, 1, (3,))
+        local_terms(2)
+        concentrations(LAST)
         open_turned(0, (0, 1))
-        open_turned(1, (2,))
+        open_turned(4, (2,))
         open_turned(2, (3,))
+        weigh(LAST)
+        product_term(LAST)
         turn_back(0, 0, 2)
-        v_from_east(LAST, 0, HALF)
+        own_e_term(LAST)
+        own_y_term(LAST)
         turn_back(0, 2, 2)
-        open_sums(4, 1, (0, 1))
-        open_sums(5, 1, (2,))
-        open_sums(6, 1, (3,))
-        diffuse_y(LAST - 1, 0, CELLS)
+        v_from_east(2, 0, CELLS)
+        for step in (v_from_west, v_from_east):
+            step(LAST, 0, P)
+            step(LAST, P, P)
+        diffuse_y(2, 0, CELLS)
+        local_terms(LAST)
         diffuse_y(LAST, 0, HALF)
         diffuse_y(LAST, HALF, P)
         diffuse_y(LAST, HALF + P, P)
 
-        z2_first = quantise(weave_z2(0, HALF, False), HALF, "z2")
+        quarters = (HALF, HALF + P)
+        woven_z2_first = weave_z2(0, HALF, True)
         turn_back(1, 0, 2)
-        v_from_west(LAST, HALF, HALF)
-        first_accs = [bank(3, [P, 2, HALF]), bank(7, [P, 2, HALF])]
-        last_passes(first_accs, w4, 12, z2_first, True)
+        z2_first = quantise(woven_z2_first, HALF, "z2", "near3_384_1")
         woven_first = weave_z(0, 2)
         turn_back(1, 2, 1)
+        turn_back(1, 3, 1)
+        first_accs = [bank(6, [P, 2, HALF]), bank(7, [P, 2, HALF])]
+        last_passes(first_accs, w4, 12, z2_first, True)
+        v_from_west(LAST, HALF, HALF)
         z_first = quantise(woven_first, HALF, "z")
         last_passes(first_accs, w3, 8, z_first, False)
-        turn_back(1, 3, 1)
-        v_from_east(LAST, HALF, HALF)
         woven_late = [weave_z(c, 1) for c in (2, 3)]
+        late_accs = [[bank(5, [P, SLOTS, P])], [bank(1, [P, SLOTS, P])]]
+        last_passes(late_accs[0], w3, 8, quantise(woven_late[0], P, "z"), True)
+        v_from_east(LAST, HALF, HALF)
+        last_passes(late_accs[1], w3, 8, quantise(woven_late[1], P, "z"), True)
         result_first = store_result(0, HALF, first_accs)
-        late_accs = [[bank(4, [P, SLOTS, P])], [bank(0, [P, SLOTS, P])]]
-        quarters = (HALF, HALF + P)
-        for i in range(2):
-            last_passes(late_accs[i], w3, 8, quantise(woven_late[i], P, "z"), True)
         woven_z2 = [weave_z2(j0, P, False) for j0 in quarters]
         for i in range(2):
             last_passes(late_accs[i], w4, 12, quantise(woven_z2[i], P, "z2"), False)

@@ -109,7 +109,8 @@ def tile_picked_grayscott_none_po_kernel(
         deal(s12_first, w_scales_raw, first_slot)
         deal(w1, w_raw[0], all_slots)
         pick(1, "w_raw0")
-        deal(w2, w_raw[1], all_slots)
+        deal(w2, w_raw[1], first_slot)
+        deal(w2, w_raw[1], other_slots)
         s12_others = keep.tile([P, FEATURES], U8, name="w_raw1", align_bytes=64)
         deal(s12_others, w_scales_raw, other_slots)
         deal(w3, w_raw[2], all_slots)
@@ -138,7 +139,7 @@ def tile_picked_grayscott_none_po_kernel(
                 v_windows.append(keep.tile([P, CELLS], F32, name="v_window%d" % t, align_bytes=64))
                 ys.append(keep.tile([P, CELLS], F32, name="y_last")[:])
                 es.append(keep.tile([P, CELLS], F32, name="e_last")[:])
-        ees = [keep.tile([P, CELLS], F32, name="ee4_%d" % t)[:] for t in range(SLOTS)]
+        ees = [keep.tile([P, CELLS], F32, name="ee4_%d" % t, align_bytes=64)[:] for t in range(SLOTS)]
         y_terms = [keep.tile([P, CELLS], F32, name="y_term%d" % t) for t in range(SLOTS)]
         v_terms = [keep.tile([P, CELLS], F32, name="v_term%d" % t) for t in range(SLOTS)]
         ye8s = [keep.tile([P, CELLS], F32, name="ye8_%d" % t) for t in range(SLOTS)]
@@ -200,7 +201,7 @@ def tile_picked_grayscott_none_po_kernel(
         def v_from_west(t, j0, width):
             entries = slice(j0 // LIST_ROWS, (j0 + width) // LIST_ROWS)
             late = t == LAST and j0 == HALF
-            partials[(t, j0)] = keep.tile([P, width], F32, name="words1_2" if late else "partial%d_%d" % (t, j0), align_bytes=64)
+            partials[(t, j0)] = keep.tile([P, width], F32, name="near3_384_1" if late else "partial%d_%d" % (t, j0), align_bytes=64)
             nc.vector.tensor_tensor(partials[(t, j0)][:], v_windows[t][:].indirect(west_t[:, entries]),
                                     v_terms[t][:, j0 : j0 + width], ALU.add)
 
@@ -340,8 +341,6 @@ def tile_picked_grayscott_none_po_kernel(
             nc.tensor.transpose(g1_bank[:, t // 2, t % 2, :], g1_t[:, t : t + 1].to_broadcast([P, P]), ident[:])
         g1_row = keep.tile([P, 2, P, 2], F32, name="g1_row")
         nc.scalar.activation(out=g1_row[:], in_=g1_bank[:].rearrange("j u r p -> j u p r"), func=ACT.Copy, scale=-0.25)
-        s34 = keep.tile([P, FEATURES], U8, name="v_window0", align_bytes=64)
-        deal(s34, w_scales_raw, all_slots)
         diffuse_y(0, 0, CELLS)
         local_terms(1)
 
@@ -358,16 +357,19 @@ def tile_picked_grayscott_none_po_kernel(
         open_turned(2, (3,))
         weigh(LAST)
         product_term(LAST)
-        turn_back(0, 0, 2)
-        own_e_term(LAST)
         own_y_term(LAST)
+        s34 = keep.tile([P, FEATURES], U8, name="ee4_3", align_bytes=64)
+        nc.gpsimd.tensor_copy(out=s34[:].rearrange("p (t m) -> p t m", t=SLOTS),
+                              in_=w_scales_raw[:].rearrange("p (m t) -> p t m", t=SLOTS))
+        turn_back(0, 0, 2)
         turn_back(0, 2, 2)
+        own_e_term(LAST)
         v_from_east(2, 0, CELLS)
         for step in (v_from_west, v_from_east):
             step(LAST, 0, P)
             step(LAST, P, P)
-        diffuse_y(2, 0, CELLS)
         local_terms(LAST)
+        diffuse_y(2, 0, CELLS)
         diffuse_y(LAST, 0, HALF)
         diffuse_y(LAST, HALF, P)
         diffuse_y(LAST, HALF + P, P)
@@ -375,22 +377,23 @@ def tile_picked_grayscott_none_po_kernel(
         quarters = (HALF, HALF + P)
         woven_z2_first = weave_z2(0, HALF, True)
         turn_back(1, 0, 2)
-        z2_first = quantise(woven_z2_first, HALF, "z2", "near3_384_1")
         woven_first = weave_z(0, 2)
         turn_back(1, 2, 1)
         turn_back(1, 3, 1)
+        v_from_west(LAST, HALF, HALF)
+        z2_first = quantise(woven_z2_first, HALF, "z2")
         first_accs = [bank(6, [P, 2, HALF]), bank(7, [P, 2, HALF])]
         last_passes(first_accs, w4, 12, z2_first, True)
-        v_from_west(LAST, HALF, HALF)
+        v_from_east(LAST, HALF, HALF)
         z_first = quantise(woven_first, HALF, "z")
         last_passes(first_accs, w3, 8, z_first, False)
         woven_late = [weave_z(c, 1) for c in (2, 3)]
-        late_accs = [[bank(5, [P, SLOTS, P])], [bank(1, [P, SLOTS, P])]]
-        last_passes(late_accs[0], w3, 8, quantise(woven_late[0], P, "z"), True)
-        v_from_east(LAST, HALF, HALF)
-        last_passes(late_accs[1], w3, 8, quantise(woven_late[1], P, "z"), True)
         result_first = store_result(0, HALF, first_accs)
-        woven_z2 = [weave_z2(j0, P, False) for j0 in quarters]
+        late_accs = [[bank(5, [P, SLOTS, P])], [bank(1, [P, SLOTS, P])]]
+        woven_z2 = []
+        for i in range(2):
+            woven_z2.append(weave_z2(quarters[i], P, False))
+            last_passes(late_accs[i], w3, 8, quantise(woven_late[i], P, "z"), True)
         for i in range(2):
             last_passes(late_accs[i], w4, 12, quantise(woven_z2[i], P, "z2"), False)
         results_late = [store_result(j0, P, accs) for j0, accs in zip(quarters, late_accs)]

@@ -54,7 +54,7 @@ def tile_picked_grayscott_none_po_kernel(
         x_table = keep.tile([P, TABLE], I32, name="x_table", align_bytes=64)
         x_scale_table = keep.tile([P, TABLE], U8, name="x_scale_table", align_bytes=64)
         w_scales_raw = keep.tile([P, FEATURES], U8, name="w_scales_raw", align_bytes=64)
-        g1_t = keep.tile([P, SLOTS], F32, name="g1_t")
+        g1_all = keep.tile([P, FEATURES], F32, name="g1_all")
         g2_t = keep.tile([P, SLOTS], F32, name="g2_t")
         x_scale_rows = keep.tile([P, TABLE], U8, name="x_scale_rows", align_bytes=64)
         w_raw = [keep.tile([P, FEATURES], I32, name="w_raw%d" % i, align_bytes=64) for i in range(4)]
@@ -79,7 +79,6 @@ def tile_picked_grayscott_none_po_kernel(
         nc.sync.dma_start(out=g2_t[:], in_=g2.rearrange("(p t) o -> p (t o)", t=SLOTS))
         nc.sync.dma_start(west_t[:], west)
         nc.sync.dma_start(east_t[:], east)
-        nc.sync.dma_start(out=g1_t[:], in_=g1.rearrange("(p t) o -> p (t o)", t=SLOTS))
         for q in QUADRANTS:
             rows = slice(32 * q, 32 * q + 4)
             nc.vector.tensor_copy(out=x_scale_table[rows, :].bitcast(I32), in_=x_scale_rows[rows, :].bitcast(I32))
@@ -117,6 +116,7 @@ def tile_picked_grayscott_none_po_kernel(
         deal(w4, w_raw[3], all_slots)
         load_scale_rows(nc.sync, w_scales_raw, 8, w3_scales, QUADRANTS)
         load_scale_rows(nc.sync, w_scales_raw, 12, w4_scales, QUADRANTS)
+        nc.sync.dma_start(out=g1_all[:], in_=g1.rearrange("f o -> (f o)").partition_broadcast(P))
 
         def first_product(acc, w, first_row, t, j0, width):
             cols = slice(P * t, P * (t + 1))
@@ -336,11 +336,8 @@ def tile_picked_grayscott_none_po_kernel(
             concentrations(t)
             vector_work(t)
         local_terms(0)
-        g1_bank = bank(1, [P, 2, 2, P])
-        for t in range(SLOTS):
-            nc.tensor.transpose(g1_bank[:, t // 2, t % 2, :], g1_t[:, t : t + 1].to_broadcast([P, P]), ident[:])
         g1_row = keep.tile([P, 2, P, 2], F32, name="g1_row")
-        nc.scalar.activation(out=g1_row[:], in_=g1_bank[:].rearrange("j u r p -> j u p r"), func=ACT.Copy, scale=-0.25)
+        nc.vector.tensor_scalar_mul(out=g1_row[:], in0=g1_all[:].rearrange("j (p u r) -> j u p r", u=2, r=2), scalar1=-0.25)
         diffuse_y(0, 0, CELLS)
         local_terms(1)
 

@@ -127,57 +127,43 @@ def tile_picked_grayscott_none_po_kernel(
                                     rhs=x_codes[(j0 + c0) // HALF][:].bitcast(FP8X4), rhs_scale=x_scale[:, cells],
                                     start=True, stop=True)
 
-        logit_windows, v_windows, ys, es = [], [], [], []
+        y_windows = [keep.tile([P, 2 * CELLS], F32, name="y_window%d" % t) for t in range(SLOTS)]
+        ys = [window[:, 0:CELLS] for window in y_windows]
+        es = [y_windows[(t - 1) % SLOTS][:, CELLS:] for t in range(SLOTS)]
+        v_windows, ye8s = [], []
         for t in range(SLOTS):
-            if t < LAST:
-                logit_windows.append(keep.tile([P, 2 * CELLS], F32, name="logit_window%d" % t))
+            if t < 2:
                 v_windows.append(keep.tile([P, 2 * CELLS], F32, name="v_window%d" % t, align_bytes=64))
-                ys.append(logit_windows[t][:, CELLS:])
-                es.append(v_windows[t][:, CELLS:])
+                ye8s.append(v_windows[t][:, CELLS:])
             else:
-                logit_windows.append(keep.tile([P, CELLS], F32, name="logit_window%d" % t))
                 v_windows.append(keep.tile([P, CELLS], F32, name="v_window%d" % t, align_bytes=64))
-                ys.append(keep.tile([P, CELLS], F32, name="y_last")[:])
-                es.append(keep.tile([P, CELLS], F32, name="e_last")[:])
-        ees = [keep.tile([P, CELLS], F32, name="ee4_%d" % t, align_bytes=64)[:] for t in range(SLOTS)]
-        y_terms = [keep.tile([P, CELLS], F32, name="y_term%d" % t) for t in range(SLOTS)]
+                ye8s.append(keep.tile([P, CELLS], F32, name="ye8_%d" % t, align_bytes=64)[:])
+        y_terms = [keep.tile([P, CELLS], F32, name="y_term%d" % t, align_bytes=64) for t in range(SLOTS)]
         v_terms = [keep.tile([P, CELLS], F32, name="v_term%d" % t) for t in range(SLOTS)]
-        ye8s = [keep.tile([P, CELLS], F32, name="ye8_%d" % t) for t in range(SLOTS)]
 
-        Y_BANKS, E_BANKS = (None, 5, 0, 2), (None, 4, 3, 4)
-        V_ON_SCALAR = ()
+        Y_BANKS, E_BANKS = (None, 0, 2, 0), (None, 1, 3, 1)
 
         def concentrations(t):
             if t == 0:
-                halves_y = []
                 for h in range(2):
                     cells = slice(HALF * h, HALF * (h + 1))
-                    halves_y.append(bank(2 * h, [P, HALF]))
-                    first_product(halves_y[h][:], w1, 0, t, HALF * h, HALF)
-                    nc.scalar.activation(out=ys[t][:, cells], in_=halves_y[h][:], func=ACT.Sigmoid)
+                    half_y = bank(2 * h, [P, HALF])
+                    first_product(half_y[:], w1, 0, t, HALF * h, HALF)
+                    nc.scalar.activation(out=ys[t][:, cells], in_=half_y[:], func=ACT.Sigmoid)
                     half_e = bank(2 * h + 1, [P, HALF])
                     first_product(half_e[:], w2, 4, t, HALF * h, HALF)
                     nc.scalar.activation(out=es[t][:, cells], in_=half_e[:], func=ACT.Sigmoid)
-                nc.scalar.copy(out=logit_windows[t][:, 0:HALF], in_=halves_y[0][:])
-                nc.scalar.activation(out=ees[t], in_=es[t], func=ACT.Square, scale=2.0)
-                nc.scalar.copy(out=logit_windows[t][:, HALF:CELLS], in_=halves_y[1][:])
                 return
-            acc_e = bank(E_BANKS[t], [P, CELLS])
-            first_product(acc_e[:], w2, 4, t, 0, CELLS)
-            nc.scalar.activation(out=es[t], in_=acc_e[:], func=ACT.Sigmoid)
             acc_y = bank(Y_BANKS[t], [P, CELLS])
             first_product(acc_y[:], w1, 0, t, 0, CELLS)
             nc.scalar.activation(out=ys[t], in_=acc_y[:], func=ACT.Sigmoid)
-            if t in V_ON_SCALAR:
-                nc.scalar.activation(out=v_windows[t][:, 0:CELLS], in_=es[t], func=ACT.Copy, scale=g2_t[:, t : t + 1])
-            nc.scalar.activation(out=ees[t], in_=es[t], func=ACT.Square, scale=2.0)
-            if t > 0:
-                nc.scalar.copy(out=logit_windows[t][:, 0:CELLS], in_=acc_y[:])
+            acc_e = bank(E_BANKS[t], [P, CELLS])
+            first_product(acc_e[:], w2, 4, t, 0, CELLS)
+            nc.scalar.activation(out=es[t], in_=acc_e[:], func=ACT.Sigmoid)
 
         def weigh(t, j0=0, width=CELLS):
-            if t not in V_ON_SCALAR:
-                cells = slice(j0, j0 + width)
-                nc.vector.tensor_scalar_mul(out=v_windows[t][:, cells], in0=es[t][:, cells], scalar1=g2_t[:, t : t + 1])
+            cells = slice(j0, j0 + width)
+            nc.vector.tensor_scalar_mul(out=v_windows[t][:, cells], in0=es[t][:, cells], scalar1=g2_t[:, t : t + 1])
 
         def product_term(t, j0=0, width=CELLS):
             cells = slice(j0, j0 + width)
@@ -185,89 +171,80 @@ def tile_picked_grayscott_none_po_kernel(
                                            op0=ALU.mult, op1=ALU.mult)
 
         def own_e_term(t):
-            nc.vector.scalar_tensor_tensor(out=v_terms[t][:], in0=ye8s[t][:], scalar=4.0, in1=v_windows[t][:, 0:CELLS],
+            nc.vector.scalar_tensor_tensor(out=v_terms[t][:], in0=ye8s[t], scalar=4.0, in1=v_windows[t][:, 0:CELLS],
                                            op0=ALU.add, op1=ALU.mult)
 
         def own_y_term(t):
-            nc.vector.scalar_tensor_tensor(out=y_terms[t][:], in0=ees[t], scalar=1.5, in1=ys[t], op0=ALU.subtract, op1=ALU.mult)
-
-        def by_halves(step, t):
-            step(t, 0, HALF)
-            step(t, HALF, HALF)
+            nc.vector.scalar_tensor_tensor(out=y_terms[t][:], in0=ye8s[t], scalar=-1.0 / 3.0, in1=es[t], op0=ALU.mult, op1=ALU.mult)
 
         z2_rows = keep.tile([P, SLOTS * CELLS], F32, name="z2_rows")
         partials = {}
 
         def v_from_west(t, j0, width):
             entries = slice(j0 // LIST_ROWS, (j0 + width) // LIST_ROWS)
-            late = t == LAST and j0 == HALF
-            partials[(t, j0)] = keep.tile([P, width], F32, name="near3_384_1" if late else "partial%d_%d" % (t, j0), align_bytes=64)
-            nc.vector.tensor_tensor(partials[(t, j0)][:], v_windows[t][:].indirect(west_t[:, entries]),
+            partials[(t, j0)] = keep.tile([P, width], F32, name="partial%d_%d" % (t, j0), align_bytes=64)[:]
+            nc.vector.tensor_tensor(partials[(t, j0)], v_windows[t][:].indirect(west_t[:, entries]),
                                     v_terms[t][:, j0 : j0 + width], ALU.add)
+
+        def west_on_scalar(t, h, name):
+            near = keep.tile([P, HALF], F32, name=name, align_bytes=64)
+            entries = slice(HALF * h // LIST_ROWS, HALF * (h + 1) // LIST_ROWS)
+            nc.scalar.activation(out=near[:], in_=v_windows[t][:].indirect(west_t[:, entries]), func=ACT.Copy)
+            return near
+
+        def add_west(t, h, near, name):
+            j0 = HALF * h
+            partial = keep.tile([P, HALF], F32, name=name, align_bytes=64)
+            nc.vector.tensor_tensor(partial[:], near[:], v_terms[t][:, j0 : j0 + HALF], ALU.add)
+            partials[(t, j0)] = partial[:]
+            partials[(t, j0 + P)] = partial[:, P:]
 
         def v_from_east(t, j0, width):
             entries = slice(j0 // LIST_ROWS, (j0 + width) // LIST_ROWS)
             nc.vector.tensor_tensor(z2_rows[:, CELLS * t + j0 : CELLS * t + j0 + width],
-                                    v_windows[t][:].indirect(east_t[:, entries]), partials[(t, j0)][:], ALU.add)
+                                    v_windows[t][:].indirect(east_t[:, entries]), partials[(t, j0)][:, 0:width], ALU.add)
 
         sums = {}
 
-        def open_sums(number, u, quarters):
-            tile = bank(number, [P, 2, len(quarters), P])
-            for i, c in enumerate(quarters):
-                sums[(u, c)] = (tile, i, len(quarters))
+        def open_sums(u, numbers):
+            for h in range(2):
+                sums[(u, h)] = bank(numbers[h], [P, 2, 2, P])
 
-        def add_terms(t, c, terms, first, last):
+        def add_term(t, term, first=False, last=False):
             u, r = divmod(t, 2)
-            tile, i, count = sums[(u, c)]
-            for k, term in enumerate(terms):
-                nc.tensor.matmul(tile[:, r, i, :], term, ident[:], is_transpose=True,
-                                 start=(first and k == 0 and r == 0 and i == 0),
-                                 stop=(last and k == len(terms) - 1 and r == 1 and i == count - 1))
-
-        def local_terms(t):
             for c in range(SLOTS):
-                add_terms(t, c, [y_terms[t][:, P * c : P * (c + 1)]], True, False)
+                h, i = divmod(c, 2)
+                nc.tensor.matmul(sums[(u, h)][:, r, i, :], term[:, P * c : P * (c + 1)], ident[:], is_transpose=True,
+                                 start=(first and i == 0), stop=(last and i == 1))
 
-        def diffuse_y(t, j0, width):
-            entries = slice(j0 // LIST_ROWS, (j0 + width) // LIST_ROWS)
-            for lists, last in ((west_t, False), (east_t, True)):
-                near = keep.tile([P, width], F32, name="near%d_%d_%d" % (t, j0, last), align_bytes=64)
-                nc.scalar.activation(out=near[:], in_=logit_windows[t][:].indirect(lists[:, entries]), func=ACT.Sigmoid, scale=-1.0)
-                for c0 in range(0, width, P):
-                    add_terms(t, (j0 + c0) // P, [near[:, c0 : c0 + P]], False, last)
+        lists = {"west": west_t, "east": east_t}
+
+        def y_from(t, side, last=False):
+            near = keep.tile([P, CELLS], F32, name="near%d_%s" % (t, side), align_bytes=64)
+            nc.scalar.activation(out=near[:], in_=y_windows[t][:].indirect(lists[side][:]), func=ACT.Copy, scale=2.0 / 3.0)
+            add_term(t, near, last=last)
 
         turned = {}
 
-        def open_turned(number, quarters):
-            tile = bank(number, [P, len(quarters), 2, P])
-            for i, c in enumerate(quarters):
-                turned[c] = (tile, i)
-
-        def turn_back(u, c0, count):
-            tile, i, whole = sums[(u, c0)]
-            words = keep.tile([P, count, P], F32, name="words%d_%d" % (u, c0), align_bytes=64)
+        def turn_back(u, h):
+            words = keep.tile([P, 2, P], F32, name="words%d_%d" % (u, h), align_bytes=64)
             nc.vector.scalar_tensor_tensor(
                 out=words[:].bitcast(BF16).rearrange("j c (p r) -> j c p r", r=2),
-                in0=tile[:, :, i : i + count, :].rearrange("j r c p -> j c p r"), scalar=-2.5,
-                in1=g1_row[:, u : u + 1].to_broadcast([P, count, P, 2]), op0=ALU.add, op1=ALU.mult,
+                in0=sums[(u, h)][:].rearrange("j r c p -> j c p r"), scalar=1.0 / 3.0,
+                in1=g1_row[:, u : u + 1].to_broadcast([P, 2, P, 2]), op0=ALU.add, op1=ALU.mult,
             )
-            for k in range(count):
-                back, place = turned[c0 + k]
-                nc.tensor.transpose(back[:, place, u, :], words[:, k, :], ident[:])
+            for i in range(2):
+                nc.tensor.transpose(turned[h][:, i, u, :], words[:, i, :], ident[:])
 
         out_rows = out_0.rearrange("(p t) j -> p t j", t=SLOTS)
         out_codes = keep.tile([P, CELLS], I32, name="out_codes", align_bytes=64)
         out_scale = keep.tile([P, CELLS], U8, name="out_scale", align_bytes=64)
 
-        def quantise(woven, width, name, codes_name=None):
-            if codes_name:
-                codes = keep.tile([P, width], U32, name=codes_name, align_bytes=64)
-            else:
-                codes = ring.tile([P, width], U32, name=name + "_codes", align_bytes=64, bufs=PARTS)
+        def quantise(woven, width, name):
+            codes = ring.tile([P, width], U32, name=name + "_codes", align_bytes=64, bufs=PARTS)
             scale = ring.tile([P, width], U8, name=name + "_scale", align_bytes=64, bufs=PARTS)
             nc.vector.quantize_mx(out=codes[:].bitcast(FP8X4), scales=scale[:], in_=woven)
-            return codes, scale
+            return codes[:], scale[:]
 
         def weave_z2(j0, width, on_scalar):
             rows = z2_rows[:].rearrange("p (t j) -> p j t", t=SLOTS)[:, j0 : j0 + width, :]
@@ -280,22 +257,21 @@ def tile_picked_grayscott_none_po_kernel(
                 nc.vector.tensor_scalar_mul(out=dst, in0=src, scalar1=0.125)
             return woven[:].rearrange("p j t -> p (j t)")
 
-        def weave_z(c0, count):
-            back, place = turned[c0]
-            woven = ring.tile([P, count * P * SLOTS], BF16, name="z_woven", align_bytes=64, bufs=PARTS)
+        def weave_z(h):
+            woven = ring.tile([P, HALF * SLOTS], BF16, name="z_woven", align_bytes=64)
             nc.scalar.copy(
                 out=woven[:].bitcast(F32).rearrange("p (q j u) -> p q j u", u=2, j=P),
-                in_=back[:, place : place + count].rearrange("p q u j -> p q j u"),
+                in_=turned[h][:].rearrange("p q u j -> p q j u"),
             )
             return woven[:]
 
-        def last_passes(accs, w, first_row, z, start):
+        def last_passes(accs, w, first_row, codes, scale, start):
             per_bank = SLOTS // len(accs)
             for t in range(SLOTS):
                 cols = slice(P * t, P * (t + 1))
                 b, r = divmod(t, per_bank)
                 nc.tensor.matmul_mx(out=accs[b][:, r, :], lhsT=w[:, cols].bitcast(FP8X4), lhsT_scale=s34[first_row:P, cols],
-                                    rhs=z[0][:].bitcast(FP8X4), rhs_scale=z[1][:],
+                                    rhs=codes.bitcast(FP8X4), rhs_scale=scale,
                                     start=start and r == 0, stop=not start and r == per_bank - 1)
 
         def store_result(j0, width, accs):
@@ -306,99 +282,109 @@ def tile_picked_grayscott_none_po_kernel(
             nc.sync.dma_start(out=out_rows[:, :, j0 : j0 + width], in_=result[:])
             return result
 
-        def quantise_result(j0, width, result):
-            cells = slice(j0, j0 + width)
+        def weave_result(width, result):
             woven = ring.tile([P, width, SLOTS], BF16, name="out_woven", align_bytes=64, bufs=PARTS)
             nc.vector.tensor_copy(out=woven[:].rearrange("p (c i) t -> p c t i", i=LINE),
                                   in_=result[:].rearrange("p t (c i) -> p c t i", i=LINE))
-            nc.vector.quantize_mx(out=out_codes[:, cells].bitcast(FP8X4), scales=out_scale[:, cells],
-                                  in_=woven[:].rearrange("p j t -> p (j t)"))
+            return woven[:].rearrange("p j t -> p (j t)")
+
+        def quantise_result(j0, width, woven):
+            cells = slice(j0, j0 + width)
+            nc.vector.quantize_mx(out=out_codes[:, cells].bitcast(FP8X4), scales=out_scale[:, cells], in_=woven)
 
         def store_codes(cells):
             nc.sync.dma_start(out=words_of(out_1)[:, cells], in_=out_codes[:, cells])
 
-        def vector_work(t):
-            if t > 0:
-                weigh(t)
-                product_term(t)
-                v_from_east(t - 1, 0, CELLS)
-            else:
-                for j0 in (0, HALF):
-                    weigh(t, j0, HALF)
-                    product_term(t, j0, HALF)
-            own_e_term(t)
-            own_y_term(t)
-            v_from_west(t, 0, CELLS)
+        open_sums(0, (6, 7))
+        concentrations(0)
+        for j0 in (0, HALF):
+            weigh(0, j0, HALF)
+            product_term(0, j0, HALF)
+        concentrations(1)
+        add_term(0, ys[0], first=True)
+        add_term(1, ys[1])
+        own_e_term(0)
+        own_y_term(0)
+        add_term(0, y_terms[0])
+        v_from_west(0, 0, CELLS)
+        y_from(0, "west")
+        y_from(0, "east")
 
-        open_sums(6, 0, (0, 1))
-        open_sums(7, 0, (2, 3))
-        for t in range(2):
-            concentrations(t)
-            vector_work(t)
-        local_terms(0)
-        g1_row = keep.tile([P, 2, P, 2], F32, name="g1_row")
-        nc.vector.tensor_scalar_mul(out=g1_row[:], in0=g1_all[:].rearrange("j (p u r) -> j u p r", u=2, r=2), scalar1=-0.25)
-        diffuse_y(0, 0, CELLS)
-        local_terms(1)
-
+        open_sums(1, (4, 5))
         concentrations(2)
-        vector_work(2)
-        diffuse_y(1, 0, CELLS)
-        open_sums(5, 1, (0, 1))
-        open_sums(1, 1, (2,))
-        open_sums(3, 1, (3,))
-        local_terms(2)
+        add_term(2, ys[2], first=True)
+        weigh(1)
+        product_term(1)
+        v_from_east(0, 0, CELLS)
+        own_e_term(1)
+        own_y_term(1)
+        add_term(1, y_terms[1])
+        v_from_west(1, 0, CELLS)
+        y_from(1, "west")
+        y_from(1, "east", last=True)
+        g1_row = keep.tile([P, 2, P, 2], F32, name="y_term0", align_bytes=64)
+        nc.scalar.activation(out=g1_row[:], in_=g1_all[:].rearrange("j (p u r) -> j u p r", u=2, r=2), func=ACT.Copy, scale=0.375)
+
         concentrations(LAST)
-        open_turned(0, (0, 1))
-        open_turned(4, (2,))
-        open_turned(2, (3,))
-        weigh(LAST)
-        product_term(LAST)
-        own_y_term(LAST)
-        s34 = keep.tile([P, FEATURES], U8, name="ee4_3", align_bytes=64)
+        add_term(LAST, ys[LAST])
+        product_term(2)
+        weigh(2)
+        own_y_term(2)
+        add_term(2, y_terms[2])
+        v_from_east(1, 0, CELLS)
+        s34 = keep.tile([P, FEATURES], U8, name="partial1_0", align_bytes=64)
         nc.gpsimd.tensor_copy(out=s34[:].rearrange("p (t m) -> p t m", t=SLOTS),
                               in_=w_scales_raw[:].rearrange("p (m t) -> p t m", t=SLOTS))
-        turn_back(0, 0, 2)
-        turn_back(0, 2, 2)
+        for h in range(2):
+            turned[h] = bank(2 + h, [P, 2, 2, P])
+            turn_back(0, h)
+        y_from(2, "west")
+        y_from(2, "east")
+
+        product_term(LAST)
+        weigh(LAST)
+        own_y_term(LAST)
+        y_from(LAST, "west")
+        add_term(LAST, y_terms[LAST])
+        y_from(LAST, "east", last=True)
+        spent = ("near0_west", "near0_east", "near1_west", "near1_east")
+        west_v = {(t, h): west_on_scalar(t, h, spent[2 * h + t - 2]) for h in range(2) for t in (2, LAST)}
+        own_e_term(2)
         own_e_term(LAST)
-        v_from_east(2, 0, CELLS)
-        for step in (v_from_west, v_from_east):
-            step(LAST, 0, P)
-            step(LAST, P, P)
-        local_terms(LAST)
-        diffuse_y(2, 0, CELLS)
-        diffuse_y(LAST, 0, HALF)
-        diffuse_y(LAST, HALF, P)
-        diffuse_y(LAST, HALF + P, P)
+        woven_z = []
+        for h in range(2):
+            turn_back(1, h)
+            woven_z.append(weave_z(h))
+        add_west(2, 0, west_v[(2, 0)], "words1_0")
+        add_west(LAST, 0, west_v[(LAST, 0)], "y_term0")
+        v_from_east(2, 0, HALF)
+        v_from_east(LAST, 0, HALF)
+        woven_z2_first = weave_z2(0, HALF, True)
 
         quarters = (HALF, HALF + P)
-        woven_z2_first = weave_z2(0, HALF, True)
-        turn_back(1, 0, 2)
-        woven_first = weave_z(0, 2)
-        turn_back(1, 2, 1)
-        turn_back(1, 3, 1)
-        v_from_west(LAST, HALF, HALF)
-        z2_first = quantise(woven_z2_first, HALF, "z2")
         first_accs = [bank(6, [P, 2, HALF]), bank(7, [P, 2, HALF])]
-        last_passes(first_accs, w4, 12, z2_first, True)
-        v_from_east(LAST, HALF, HALF)
-        z_first = quantise(woven_first, HALF, "z")
-        last_passes(first_accs, w3, 8, z_first, False)
-        woven_late = [weave_z(c, 1) for c in (2, 3)]
+        late_accs = [[bank(0, [P, SLOTS, P])], [bank(1, [P, SLOTS, P])]]
+        last_passes(first_accs, w3, 8, *quantise(woven_z[0], HALF, "z"), True)
+        add_west(2, 1, west_v[(2, 1)], "near0_west")
+        add_west(LAST, 1, west_v[(LAST, 1)], "near0_east")
+        z_codes, z_scale = quantise(woven_z[1], HALF, "z")
+        for i in range(2):
+            last_passes(late_accs[i], w3, 8, z_codes[:, P * i : P * (i + 1)], z_scale[:, P * i : P * (i + 1)], True)
+        last_passes(first_accs, w4, 12, *quantise(woven_z2_first, HALF, "z2"), False)
         result_first = store_result(0, HALF, first_accs)
-        late_accs = [[bank(5, [P, SLOTS, P])], [bank(1, [P, SLOTS, P])]]
-        woven_z2 = []
+        v_from_east(2, HALF, HALF)
+        for j0 in quarters:
+            v_from_east(LAST, j0, P)
+        woven_z2 = [weave_z2(j0, P, False) for j0 in quarters]
         for i in range(2):
-            woven_z2.append(weave_z2(quarters[i], P, False))
-            last_passes(late_accs[i], w3, 8, quantise(woven_late[i], P, "z"), True)
-        for i in range(2):
-            last_passes(late_accs[i], w4, 12, quantise(woven_z2[i], P, "z2"), False)
+            last_passes(late_accs[i], w4, 12, *quantise(woven_z2[i], P, "z2"), False)
         results_late = [store_result(j0, P, accs) for j0, accs in zip(quarters, late_accs)]
 
-        quantise_result(0, HALF, result_first)
+        quantise_result(0, HALF, weave_result(HALF, result_first))
         store_codes(slice(0, HALF))
-        for j0, result in zip(quarters, results_late):
-            quantise_result(j0, P, result)
+        woven_late = [weave_result(P, result) for result in results_late]
+        for j0, woven in zip(quarters, woven_late):
+            quantise_result(j0, P, woven)
         store_codes(slice(HALF, CELLS))
         for q, queue in zip(QUADRANTS, (nc.scalar, nc.scalar, nc.sync, nc.sync)):
             queue.dma_start(out=out_2[0, 4 * q : 4 * q + 4, :].bitcast(I32), in_=out_scale[32 * q : 32 * q + 4, :].bitcast(I32))

@@ -101,8 +101,6 @@ def tile_picked_grayscott_none_po_kernel(
         s12_first = keep.tile([P, FEATURES], U8, name="s12_first", align_bytes=64)
         w1 = keep.tile([P, FEATURES], I32, name="w1", align_bytes=64)
         w2 = keep.tile([P, FEATURES], I32, name="w2", align_bytes=64)
-        w3 = keep.tile([P, FEATURES], I32, name="w3", align_bytes=64)
-        w4 = keep.tile([P, FEATURES], I32, name="w4", align_bytes=64)
         first_slot, other_slots, all_slots = slice(0, 1), slice(1, SLOTS), slice(0, SLOTS)
         pick(0, "x_codes_first")
         deal(s12_first, w_scales_raw, first_slot)
@@ -112,8 +110,6 @@ def tile_picked_grayscott_none_po_kernel(
         deal(w2, w_raw[1], other_slots)
         s12_others = keep.tile([P, FEATURES], U8, name="w_raw1", align_bytes=64)
         deal(s12_others, w_scales_raw, other_slots)
-        deal(w3, w_raw[2], all_slots)
-        deal(w4, w_raw[3], all_slots)
         load_scale_rows(nc.sync, w_scales_raw, 8, w3_scales, QUADRANTS)
         load_scale_rows(nc.sync, w_scales_raw, 12, w4_scales, QUADRANTS)
         nc.sync.dma_start(out=g1_all[:], in_=g1.rearrange("f o -> (f o)").partition_broadcast(P))
@@ -186,10 +182,10 @@ def tile_picked_grayscott_none_po_kernel(
             nc.vector.tensor_tensor(partials[(t, j0)], v_windows[t][:].indirect(west_t[:, entries]),
                                     v_terms[t][:, j0 : j0 + width], ALU.add)
 
-        def west_on_scalar(t, h, name):
+        def v_on_scalar(t, h, side, name):
             near = keep.tile([P, HALF], F32, name=name, align_bytes=64)
             entries = slice(HALF * h // LIST_ROWS, HALF * (h + 1) // LIST_ROWS)
-            nc.scalar.activation(out=near[:], in_=v_windows[t][:].indirect(west_t[:, entries]), func=ACT.Copy)
+            nc.scalar.activation(out=near[:], in_=v_windows[t][:].indirect(lists[side][:, entries]), func=ACT.Copy)
             return near
 
         def add_west(t, h, near, name):
@@ -197,44 +193,46 @@ def tile_picked_grayscott_none_po_kernel(
             partial = keep.tile([P, HALF], F32, name=name, align_bytes=64)
             nc.vector.tensor_tensor(partial[:], near[:], v_terms[t][:, j0 : j0 + HALF], ALU.add)
             partials[(t, j0)] = partial[:]
-            partials[(t, j0 + P)] = partial[:, P:]
+
+        def add_east(t, h, near):
+            j0 = HALF * h
+            nc.vector.tensor_tensor(z2_rows[:, CELLS * t + j0 : CELLS * t + j0 + HALF], near[:], partials[(t, j0)], ALU.add)
+
+        def deal_on_gpsimd(raw, dtype, name):
+            dealt = keep.tile([P, FEATURES], dtype, name=name, align_bytes=64)
+            nc.gpsimd.tensor_copy(out=dealt[:].rearrange("p (t m) -> p t m", t=SLOTS), in_=raw[:].rearrange("p (m t) -> p t m", t=SLOTS))
+            return dealt
 
         def v_from_east(t, j0, width):
             entries = slice(j0 // LIST_ROWS, (j0 + width) // LIST_ROWS)
             nc.vector.tensor_tensor(z2_rows[:, CELLS * t + j0 : CELLS * t + j0 + width],
                                     v_windows[t][:].indirect(east_t[:, entries]), partials[(t, j0)][:, 0:width], ALU.add)
 
-        sums = {}
-
-        def open_sums(u, numbers):
-            for h in range(2):
-                sums[(u, h)] = bank(numbers[h], [P, 2, 2, P])
+        sums = [bank(4 + c, [P, SLOTS, P]) for c in range(SLOTS)]
 
         def add_term(t, term, first=False, last=False):
-            u, r = divmod(t, 2)
             for c in range(SLOTS):
-                h, i = divmod(c, 2)
-                nc.tensor.matmul(sums[(u, h)][:, r, i, :], term[:, P * c : P * (c + 1)], ident[:], is_transpose=True,
-                                 start=(first and i == 0), stop=(last and i == 1))
+                nc.tensor.matmul(sums[c][:, t, :], term[:, P * c : P * (c + 1)], ident[:], is_transpose=True, start=first, stop=last)
 
         lists = {"west": west_t, "east": east_t}
 
         def y_from(t, side, last=False):
             near = keep.tile([P, CELLS], F32, name="near%d_%s" % (t, side), align_bytes=64)
-            nc.scalar.activation(out=near[:], in_=y_windows[t][:].indirect(lists[side][:]), func=ACT.Copy, scale=2.0 / 3.0)
+            nc.scalar.activation(out=near[:], in_=y_windows[t][:].indirect(lists[side][:]), func=ACT.Copy, scale=2.0 / 3.0, bias=1.0 / 6.0)
             add_term(t, near, last=last)
 
         turned = {}
 
-        def turn_back(u, h):
-            words = keep.tile([P, 2, P], F32, name="words%d_%d" % (u, h), align_bytes=64)
+        def turn_back(c):
+            words = keep.tile([P, FEATURES // 2], F32, name="words%d" % c, align_bytes=64)
             nc.vector.scalar_tensor_tensor(
-                out=words[:].bitcast(BF16).rearrange("j c (p r) -> j c p r", r=2),
-                in0=sums[(u, h)][:].rearrange("j r c p -> j c p r"), scalar=1.0 / 3.0,
-                in1=g1_row[:, u : u + 1].to_broadcast([P, 2, P, 2]), op0=ALU.add, op1=ALU.mult,
+                out=words[:].bitcast(BF16).rearrange("j (p t) -> j p t", t=SLOTS),
+                in0=sums[c][:].rearrange("j t p -> j p t"), scalar=0.375,
+                in1=g1_all[:].rearrange("j (p t) -> j p t", t=SLOTS), op0=ALU.mult, op1=ALU.mult,
             )
-            for i in range(2):
-                nc.tensor.transpose(turned[h][:, i, u, :], words[:, i, :], ident[:])
+            h, i = divmod(c, 2)
+            for u in range(2):
+                nc.tensor.transpose(turned[h][:, i, u, :], words[:, u::2], ident[:])
 
         out_rows = out_0.rearrange("(p t) j -> p t j", t=SLOTS)
         out_codes = keep.tile([P, CELLS], I32, name="out_codes", align_bytes=64)
@@ -248,7 +246,7 @@ def tile_picked_grayscott_none_po_kernel(
 
         def weave_z2(j0, width, on_scalar):
             rows = z2_rows[:].rearrange("p (t j) -> p j t", t=SLOTS)[:, j0 : j0 + width, :]
-            woven = ring.tile([P, width, SLOTS], BF16, name="z2_woven", align_bytes=64, bufs=PARTS)
+            woven = keep.tile([P, width, SLOTS], BF16, name="z2_woven%d" % j0, align_bytes=64)
             dst = woven[:].rearrange("p (c i) t -> p c t i", i=LINE)
             src = rows.rearrange("p (c i) t -> p c t i", i=LINE)
             if on_scalar:
@@ -282,10 +280,10 @@ def tile_picked_grayscott_none_po_kernel(
             nc.sync.dma_start(out=out_rows[:, :, j0 : j0 + width], in_=result[:])
             return result
 
-        def weave_result(width, result):
+        def weave_result(width, result, copy=nc.vector.tensor_copy):
             woven = ring.tile([P, width, SLOTS], BF16, name="out_woven", align_bytes=64, bufs=PARTS)
-            nc.vector.tensor_copy(out=woven[:].rearrange("p (c i) t -> p c t i", i=LINE),
-                                  in_=result[:].rearrange("p t (c i) -> p c t i", i=LINE))
+            copy(out=woven[:].rearrange("p (c i) t -> p c t i", i=LINE),
+                 in_=result[:].rearrange("p t (c i) -> p c t i", i=LINE))
             return woven[:].rearrange("p j t -> p (j t)")
 
         def quantise_result(j0, width, woven):
@@ -295,7 +293,6 @@ def tile_picked_grayscott_none_po_kernel(
         def store_codes(cells):
             nc.sync.dma_start(out=words_of(out_1)[:, cells], in_=out_codes[:, cells])
 
-        open_sums(0, (6, 7))
         concentrations(0)
         for j0 in (0, HALF):
             weigh(0, j0, HALF)
@@ -310,9 +307,8 @@ def tile_picked_grayscott_none_po_kernel(
         y_from(0, "west")
         y_from(0, "east")
 
-        open_sums(1, (4, 5))
         concentrations(2)
-        add_term(2, ys[2], first=True)
+        add_term(2, ys[2])
         weigh(1)
         product_term(1)
         v_from_east(0, 0, CELLS)
@@ -321,66 +317,64 @@ def tile_picked_grayscott_none_po_kernel(
         add_term(1, y_terms[1])
         v_from_west(1, 0, CELLS)
         y_from(1, "west")
-        y_from(1, "east", last=True)
-        g1_row = keep.tile([P, 2, P, 2], F32, name="y_term0", align_bytes=64)
-        nc.scalar.activation(out=g1_row[:], in_=g1_all[:].rearrange("j (p u r) -> j u p r", u=2, r=2), func=ACT.Copy, scale=0.375)
+        y_from(1, "east")
 
         concentrations(LAST)
         add_term(LAST, ys[LAST])
         product_term(2)
         weigh(2)
-        own_y_term(2)
-        add_term(2, y_terms[2])
+        product_term(LAST)
+        for t in (2, LAST):
+            own_y_term(t)
+            add_term(t, y_terms[t])
+        own_e_term(2)
         v_from_east(1, 0, CELLS)
-        s34 = keep.tile([P, FEATURES], U8, name="partial1_0", align_bytes=64)
-        nc.gpsimd.tensor_copy(out=s34[:].rearrange("p (t m) -> p t m", t=SLOTS),
-                              in_=w_scales_raw[:].rearrange("p (m t) -> p t m", t=SLOTS))
-        for h in range(2):
-            turned[h] = bank(2 + h, [P, 2, 2, P])
-            turn_back(0, h)
+        weigh(LAST)
+        v_from_west(2, 0, HALF)
+        own_e_term(LAST)
         y_from(2, "west")
         y_from(2, "east")
-
-        product_term(LAST)
-        weigh(LAST)
-        own_y_term(LAST)
         y_from(LAST, "west")
-        add_term(LAST, y_terms[LAST])
         y_from(LAST, "east", last=True)
-        spent = ("near0_west", "near0_east", "near1_west", "near1_east")
-        west_v = {(t, h): west_on_scalar(t, h, spent[2 * h + t - 2]) for h in range(2) for t in (2, LAST)}
-        own_e_term(2)
-        own_e_term(LAST)
-        woven_z = []
+        west_first = v_on_scalar(LAST, 0, "west", "near2_west")
+        west_second = [v_on_scalar(2, 1, "west", "near2_east"), v_on_scalar(LAST, 1, "west", "near3_west")]
+        east_second = [v_on_scalar(2, 1, "east", "near3_east"), v_on_scalar(LAST, 1, "east", "near1_east")]
+        s34 = deal_on_gpsimd(w_scales_raw, U8, "ye8_3")
+        w3 = deal_on_gpsimd(w_raw[2], I32, "w_scales_raw")
         for h in range(2):
-            turn_back(1, h)
-            woven_z.append(weave_z(h))
-        add_west(2, 0, west_v[(2, 0)], "words1_0")
-        add_west(LAST, 0, west_v[(LAST, 0)], "y_term0")
+            turned[h] = bank(2 + h, [P, 2, 2, P])
+        turn_back(0)
+        turn_back(1)
+        woven_z = [weave_z(0)]
+        add_west(LAST, 0, west_first, "words0")
         v_from_east(2, 0, HALF)
         v_from_east(LAST, 0, HALF)
+        w4 = deal_on_gpsimd(w_raw[3], I32, "words0")
         woven_z2_first = weave_z2(0, HALF, True)
+        turn_back(2)
+        turn_back(3)
+        woven_z.append(weave_z(1))
 
         quarters = (HALF, HALF + P)
-        first_accs = [bank(6, [P, 2, HALF]), bank(7, [P, 2, HALF])]
+        first_accs = [bank(4, [P, 2, HALF]), bank(5, [P, 2, HALF])]
         late_accs = [[bank(0, [P, SLOTS, P])], [bank(1, [P, SLOTS, P])]]
         last_passes(first_accs, w3, 8, *quantise(woven_z[0], HALF, "z"), True)
-        add_west(2, 1, west_v[(2, 1)], "near0_west")
-        add_west(LAST, 1, west_v[(LAST, 1)], "near0_east")
+        last_passes(first_accs, w4, 12, *quantise(woven_z2_first, HALF, "z2"), False)
+        result_first = store_result(0, HALF, first_accs)
+        add_west(2, 1, west_second[0], "words2")
+        add_west(LAST, 1, west_second[1], "words3")
+        add_east(2, 1, east_second[0])
+        add_east(LAST, 1, east_second[1])
         z_codes, z_scale = quantise(woven_z[1], HALF, "z")
         for i in range(2):
             last_passes(late_accs[i], w3, 8, z_codes[:, P * i : P * (i + 1)], z_scale[:, P * i : P * (i + 1)], True)
-        last_passes(first_accs, w4, 12, *quantise(woven_z2_first, HALF, "z2"), False)
-        result_first = store_result(0, HALF, first_accs)
-        v_from_east(2, HALF, HALF)
-        for j0 in quarters:
-            v_from_east(LAST, j0, P)
         woven_z2 = [weave_z2(j0, P, False) for j0 in quarters]
         for i in range(2):
             last_passes(late_accs[i], w4, 12, *quantise(woven_z2[i], P, "z2"), False)
+        woven_first = weave_result(HALF, result_first)
         results_late = [store_result(j0, P, accs) for j0, accs in zip(quarters, late_accs)]
 
-        quantise_result(0, HALF, weave_result(HALF, result_first))
+        quantise_result(0, HALF, woven_first)
         store_codes(slice(0, HALF))
         woven_late = [weave_result(P, result) for result in results_late]
         for j0, woven in zip(quarters, woven_late):

@@ -150,12 +150,17 @@ def tile_picked_grayscott_none_po_kernel(
                     first_product(half_e[:], w2, 4, t, HALF * h, HALF)
                     nc.scalar.activation(out=es[t][:, cells], in_=half_e[:], func=ACT.Sigmoid)
                 return
-            acc_y = bank(Y_BANKS[t], [P, CELLS])
-            first_product(acc_y[:], w1, 0, t, 0, CELLS)
-            nc.scalar.activation(out=ys[t], in_=acc_y[:], func=ACT.Sigmoid)
-            acc_e = bank(E_BANKS[t], [P, CELLS])
-            first_product(acc_e[:], w2, 4, t, 0, CELLS)
-            nc.scalar.activation(out=es[t], in_=acc_e[:], func=ACT.Sigmoid)
+            nc.scalar.activation(out=ys[t], in_=logits[t][0][:], func=ACT.Sigmoid)
+            nc.scalar.activation(out=es[t], in_=logits[t][1][:], func=ACT.Sigmoid)
+            if t < LAST:
+                nc.scalar.activation(out=v_windows[t][:, 0:CELLS], in_=es[t], func=ACT.Copy, scale=g2_t[:, t : t + 1])
+
+        logits = {}
+
+        def first_products(t):
+            logits[t] = (bank(Y_BANKS[t], [P, CELLS]), bank(E_BANKS[t], [P, CELLS]))
+            first_product(logits[t][0][:], w1, 0, t, 0, CELLS)
+            first_product(logits[t][1][:], w2, 4, t, 0, CELLS)
 
         def weigh(t, j0=0, width=CELLS):
             cells = slice(j0, j0 + width)
@@ -188,11 +193,10 @@ def tile_picked_grayscott_none_po_kernel(
             nc.scalar.activation(out=near[:], in_=v_windows[t][:].indirect(lists[side][:, entries]), func=ACT.Copy)
             return near
 
-        def add_west(t, h, near, name):
+        def add_west(t, h, near, partial):
             j0 = HALF * h
-            partial = keep.tile([P, HALF], F32, name=name, align_bytes=64)
-            nc.vector.tensor_tensor(partial[:], near[:], v_terms[t][:, j0 : j0 + HALF], ALU.add)
-            partials[(t, j0)] = partial[:]
+            nc.vector.tensor_tensor(partial, near[:], v_terms[t][:, j0 : j0 + HALF], ALU.add)
+            partials[(t, j0)] = partial
 
         def add_east(t, h, near):
             j0 = HALF * h
@@ -224,9 +228,9 @@ def tile_picked_grayscott_none_po_kernel(
         turned = {}
 
         def turn_back(c):
-            words = keep.tile([P, FEATURES // 2], F32, name="words%d" % c, align_bytes=64)
+            words = all_words[:, c, :]
             nc.vector.scalar_tensor_tensor(
-                out=words[:].bitcast(BF16).rearrange("j (p t) -> j p t", t=SLOTS),
+                out=words.bitcast(BF16).rearrange("j (p t) -> j p t", t=SLOTS),
                 in0=sums[c][:].rearrange("j t p -> j p t"), scalar=0.375,
                 in1=g1_all[:].rearrange("j (p t) -> j p t", t=SLOTS), op0=ALU.mult, op1=ALU.mult,
             )
@@ -297,7 +301,10 @@ def tile_picked_grayscott_none_po_kernel(
         for j0 in (0, HALF):
             weigh(0, j0, HALF)
             product_term(0, j0, HALF)
+        first_products(1)
         concentrations(1)
+        first_products(2)
+        first_products(LAST)
         add_term(0, ys[0], first=True)
         add_term(1, ys[1])
         own_e_term(0)
@@ -309,7 +316,6 @@ def tile_picked_grayscott_none_po_kernel(
 
         concentrations(2)
         add_term(2, ys[2])
-        weigh(1)
         product_term(1)
         v_from_east(0, 0, CELLS)
         own_e_term(1)
@@ -322,52 +328,47 @@ def tile_picked_grayscott_none_po_kernel(
         concentrations(LAST)
         add_term(LAST, ys[LAST])
         product_term(2)
-        weigh(2)
+        v_from_east(1, 0, CELLS)
         product_term(LAST)
+        weigh(LAST)
         for t in (2, LAST):
             own_y_term(t)
             add_term(t, y_terms[t])
-        own_e_term(2)
-        v_from_east(1, 0, CELLS)
-        weigh(LAST)
-        v_from_west(2, 0, HALF)
-        own_e_term(LAST)
+        for step in (own_e_term, lambda t: v_from_west(t, 0, HALF), lambda t: v_from_east(t, 0, HALF)):
+            step(2)
+            step(LAST)
         y_from(2, "west")
         y_from(2, "east")
         y_from(LAST, "west")
         y_from(LAST, "east", last=True)
-        west_first = v_on_scalar(LAST, 0, "west", "near2_west")
-        west_second = [v_on_scalar(2, 1, "west", "near2_east"), v_on_scalar(LAST, 1, "west", "near3_west")]
-        east_second = [v_on_scalar(2, 1, "east", "near3_east"), v_on_scalar(LAST, 1, "east", "near1_east")]
-        s34 = deal_on_gpsimd(w_scales_raw, U8, "ye8_3")
-        w3 = deal_on_gpsimd(w_raw[2], I32, "w_scales_raw")
+        west_second = [v_on_scalar(2, 1, "west", "near2_west"), v_on_scalar(LAST, 1, "west", "near2_east")]
+        woven_z2_first = weave_z2(0, HALF, True)
+        east_second = [v_on_scalar(2, 1, "east", "near3_west"), v_on_scalar(LAST, 1, "east", "near3_east")]
+        s34 = deal_on_gpsimd(w_scales_raw, U8, "partial3_0")
+        w4 = deal_on_gpsimd(w_raw[3], I32, "w_scales_raw")
+        w3 = deal_on_gpsimd(w_raw[2], I32, "w_raw3")
+        all_words = keep.tile([P, SLOTS, FEATURES // 2], F32, name="partial2_0", align_bytes=64)
+        woven_z = []
         for h in range(2):
             turned[h] = bank(2 + h, [P, 2, 2, P])
-        turn_back(0)
-        turn_back(1)
-        woven_z = [weave_z(0)]
-        add_west(LAST, 0, west_first, "words0")
-        v_from_east(2, 0, HALF)
-        v_from_east(LAST, 0, HALF)
-        w4 = deal_on_gpsimd(w_raw[3], I32, "words0")
-        woven_z2_first = weave_z2(0, HALF, True)
-        turn_back(2)
-        turn_back(3)
-        woven_z.append(weave_z(1))
+            turn_back(2 * h)
+            turn_back(2 * h + 1)
+            woven_z.append(weave_z(h))
 
         quarters = (HALF, HALF + P)
         first_accs = [bank(4, [P, 2, HALF]), bank(5, [P, 2, HALF])]
         late_accs = [[bank(0, [P, SLOTS, P])], [bank(1, [P, SLOTS, P])]]
-        last_passes(first_accs, w3, 8, *quantise(woven_z[0], HALF, "z"), True)
-        last_passes(first_accs, w4, 12, *quantise(woven_z2_first, HALF, "z2"), False)
+        last_passes(first_accs, w4, 12, *quantise(woven_z2_first, HALF, "z2"), True)
+        last_passes(first_accs, w3, 8, *quantise(woven_z[0], HALF, "z"), False)
         result_first = store_result(0, HALF, first_accs)
-        add_west(2, 1, west_second[0], "words2")
-        add_west(LAST, 1, west_second[1], "words3")
+        late_partials = keep.tile([P, 2, HALF], F32, name="g1_all")
+        add_west(2, 1, west_second[0], late_partials[:, 0, :])
+        add_west(LAST, 1, west_second[1], late_partials[:, 1, :])
         add_east(2, 1, east_second[0])
-        add_east(LAST, 1, east_second[1])
         z_codes, z_scale = quantise(woven_z[1], HALF, "z")
         for i in range(2):
             last_passes(late_accs[i], w3, 8, z_codes[:, P * i : P * (i + 1)], z_scale[:, P * i : P * (i + 1)], True)
+        add_east(LAST, 1, east_second[1])
         woven_z2 = [weave_z2(j0, P, False) for j0 in quarters]
         for i in range(2):
             last_passes(late_accs[i], w4, 12, *quantise(woven_z2[i], P, "z2"), False)

@@ -343,32 +343,33 @@ def tile_picked_grayscott_none_po_kernel(
         y_from(LAST, "east", last=True)
         west_second = [v_on_scalar(2, 1, "west", "near2_west"), v_on_scalar(LAST, 1, "west", "near2_east")]
         woven_z2_first = weave_z2(0, HALF, True)
-        east_second = [v_on_scalar(2, 1, "east", "near3_west"), v_on_scalar(LAST, 1, "east", "near3_east")]
+        east_last = v_on_scalar(LAST, 1, "east", "near3_east")
         s34 = deal_on_gpsimd(w_scales_raw, U8, "partial3_0")
         w4 = deal_on_gpsimd(w_raw[3], I32, "w_scales_raw")
         w3 = deal_on_gpsimd(w_raw[2], I32, "w_raw3")
         all_words = keep.tile([P, SLOTS, FEATURES // 2], F32, name="partial2_0", align_bytes=64)
-        woven_z = []
         for h in range(2):
             turned[h] = bank(2 + h, [P, 2, 2, P])
             turn_back(2 * h)
             turn_back(2 * h + 1)
-            woven_z.append(weave_z(h))
+        woven_z = [weave_z(0)]
 
         quarters = (HALF, HALF + P)
         first_accs = [bank(4, [P, 2, HALF]), bank(5, [P, 2, HALF])]
         late_accs = [[bank(0, [P, SLOTS, P])], [bank(1, [P, SLOTS, P])]]
         last_passes(first_accs, w4, 12, *quantise(woven_z2_first, HALF, "z2"), True)
+        east_third = v_on_scalar(2, 1, "east", "z2_woven0")
+        woven_z.append(weave_z(1))
         last_passes(first_accs, w3, 8, *quantise(woven_z[0], HALF, "z"), False)
         result_first = store_result(0, HALF, first_accs)
         late_partials = keep.tile([P, 2, HALF], F32, name="g1_all")
         add_west(2, 1, west_second[0], late_partials[:, 0, :])
         add_west(LAST, 1, west_second[1], late_partials[:, 1, :])
-        add_east(2, 1, east_second[0])
+        add_east(LAST, 1, east_last)
+        add_east(2, 1, east_third)
         z_codes, z_scale = quantise(woven_z[1], HALF, "z")
         for i in range(2):
             last_passes(late_accs[i], w3, 8, z_codes[:, P * i : P * (i + 1)], z_scale[:, P * i : P * (i + 1)], True)
-        add_east(LAST, 1, east_second[1])
         woven_z2 = [weave_z2(j0, P, False) for j0 in quarters]
         for i in range(2):
             last_passes(late_accs[i], w4, 12, *quantise(woven_z2[i], P, "z2"), False)

@@ -125,7 +125,7 @@ def tile_picked_grayscott_none_po_kernel(
 
         y_windows = [keep.tile([P, 2 * CELLS], F32, name="y_window%d" % t) for t in range(SLOTS)]
         ys = [window[:, 0:CELLS] for window in y_windows]
-        es = [y_windows[(t - 1) % SLOTS][:, CELLS:] for t in range(SLOTS)]
+        es = [y_windows[t][:, CELLS:] for t in (1, 0, 2, LAST)]
         v_windows, ye8s = [], []
         for t in range(SLOTS):
             if t < 2:
@@ -152,8 +152,9 @@ def tile_picked_grayscott_none_po_kernel(
                 return
             nc.scalar.activation(out=ys[t], in_=logits[t][0][:], func=ACT.Sigmoid)
             nc.scalar.activation(out=es[t], in_=logits[t][1][:], func=ACT.Sigmoid)
-            if t < LAST:
-                nc.scalar.activation(out=v_windows[t][:, 0:CELLS], in_=es[t], func=ACT.Copy, scale=g2_t[:, t : t + 1])
+
+        def weigh_on_scalar(t):
+            nc.scalar.activation(out=v_windows[t][:, 0:CELLS], in_=es[t], func=ACT.Copy, scale=g2_t[:, t : t + 1])
 
         logits = {}
 
@@ -171,8 +172,9 @@ def tile_picked_grayscott_none_po_kernel(
             nc.vector.scalar_tensor_tensor(out=ye8s[t][:, cells], in0=ys[t][:, cells], scalar=8.0, in1=es[t][:, cells],
                                            op0=ALU.mult, op1=ALU.mult)
 
-        def own_e_term(t):
-            nc.vector.scalar_tensor_tensor(out=v_terms[t][:], in0=ye8s[t], scalar=4.0, in1=v_windows[t][:, 0:CELLS],
+        def own_e_term(t, j0=0, width=CELLS):
+            cells = slice(j0, j0 + width)
+            nc.vector.scalar_tensor_tensor(out=v_terms[t][:, cells], in0=ye8s[t][:, cells], scalar=4.0, in1=v_windows[t][:, cells],
                                            op0=ALU.add, op1=ALU.mult)
 
         def own_y_term(t):
@@ -276,11 +278,11 @@ def tile_picked_grayscott_none_po_kernel(
                                     rhs=codes.bitcast(FP8X4), rhs_scale=scale,
                                     start=start and r == 0, stop=not start and r == per_bank - 1)
 
-        def store_result(j0, width, accs):
+        def store_result(j0, width, accs, copies=(nc.scalar.copy, nc.scalar.copy)):
             result = ring.tile([P, SLOTS, width], F32, name="result", bufs=PARTS)
             per_bank = SLOTS // len(accs)
             for b, acc in enumerate(accs):
-                nc.scalar.copy(out=result[:, per_bank * b : per_bank * (b + 1), :], in_=acc[:])
+                copies[b](out=result[:, per_bank * b : per_bank * (b + 1), :], in_=acc[:])
             nc.sync.dma_start(out=out_rows[:, :, j0 : j0 + width], in_=result[:])
             return result
 
@@ -303,11 +305,13 @@ def tile_picked_grayscott_none_po_kernel(
             product_term(0, j0, HALF)
         first_products(1)
         concentrations(1)
+        weigh_on_scalar(1)
         first_products(2)
         first_products(LAST)
         add_term(0, ys[0], first=True)
         add_term(1, ys[1])
-        own_e_term(0)
+        own_e_term(0, 0, HALF)
+        own_e_term(0, HALF, HALF)
         own_y_term(0)
         add_term(0, y_terms[0])
         v_from_west(0, 0, CELLS)
@@ -323,6 +327,7 @@ def tile_picked_grayscott_none_po_kernel(
         add_term(1, y_terms[1])
         v_from_west(1, 0, CELLS)
         y_from(1, "west")
+        weigh_on_scalar(2)
         y_from(1, "east")
 
         concentrations(LAST)
@@ -363,8 +368,8 @@ def tile_picked_grayscott_none_po_kernel(
         last_passes(first_accs, w3, 8, *quantise(woven_z[0], HALF, "z"), False)
         result_first = store_result(0, HALF, first_accs)
         late_partials = keep.tile([P, 2, HALF], F32, name="g1_all")
-        add_west(2, 1, west_second[0], late_partials[:, 0, :])
         add_west(LAST, 1, west_second[1], late_partials[:, 1, :])
+        add_west(2, 1, west_second[0], late_partials[:, 0, :])
         add_east(LAST, 1, east_last)
         add_east(2, 1, east_third)
         z_codes, z_scale = quantise(woven_z[1], HALF, "z")

@@ -361,7 +361,7 @@ def tile_picked_grayscott_none_po_kernel(
 
         quarters = (HALF, HALF + P)
         first_accs = [bank(4, [P, 2, HALF]), bank(5, [P, 2, HALF])]
-        late_accs = [[bank(0, [P, SLOTS, P])], [bank(1, [P, SLOTS, P])]]
+        late_accs = [[bank(0, [P, SLOTS, P])], [bank(1, [P, 2, P]), bank(6, [P, 2, P])]]
         last_passes(first_accs, w4, 12, *quantise(woven_z2_first, HALF, "z2"), True)
         east_third = v_on_scalar(2, 1, "east", "z2_woven0")
         woven_z.append(weave_z(1))
@@ -379,10 +379,10 @@ def tile_picked_grayscott_none_po_kernel(
         for i in range(2):
             last_passes(late_accs[i], w4, 12, *quantise(woven_z2[i], P, "z2"), False)
         woven_first = weave_result(HALF, result_first)
-        results_late = [store_result(j0, P, accs) for j0, accs in zip(quarters, late_accs)]
-
         quantise_result(0, HALF, woven_first)
         store_codes(slice(0, HALF))
+        results_late = [store_result(quarters[0], P, late_accs[0]),
+                        store_result(quarters[1], P, late_accs[1], (nc.vector.tensor_copy, nc.scalar.copy))]
         woven_late = [weave_result(P, result) for result in results_late]
         for j0, woven in zip(quarters, woven_late):
             quantise_result(j0, P, woven)

@@ -338,12 +338,12 @@ def tile_picked_grayscott_none_po_kernel(
         weigh(LAST)
         for t in (2, LAST):
             own_y_term(t)
-            add_term(t, y_terms[t])
         for step in (own_e_term, lambda t: v_from_west(t, 0, HALF), lambda t: v_from_east(t, 0, HALF)):
             step(2)
             step(LAST)
-        y_from(2, "west")
-        y_from(2, "east")
+        for t, side in ((2, "west"), (LAST, "east")):
+            y_from(2, side)
+            add_term(t, y_terms[t])
         y_from(LAST, "west")
         y_from(LAST, "east", last=True)
         west_second = [v_on_scalar(2, 1, "west", "near2_west"), v_on_scalar(LAST, 1, "west", "near2_east")]

@@ -204,9 +204,10 @@ def tile_picked_grayscott_none_po_kernel(
             j0 = HALF * h
             nc.vector.tensor_tensor(z2_rows[:, CELLS * t + j0 : CELLS * t + j0 + HALF], near[:], partials[(t, j0)], ALU.add)
 
-        def deal_on_gpsimd(raw, dtype, name):
+        def deal_on_gpsimd(raw, dtype, name, run):
             dealt = keep.tile([P, FEATURES], dtype, name=name, align_bytes=64)
-            nc.gpsimd.tensor_copy(out=dealt[:].rearrange("p (t m) -> p t m", t=SLOTS), in_=raw[:].rearrange("p (m t) -> p t m", t=SLOTS))
+            nc.gpsimd.tensor_copy(out=dealt[:].rearrange("p (t c i) -> p c t i", t=SLOTS, i=run),
+                                  in_=raw[:].rearrange("p (c i t) -> p c t i", t=SLOTS, i=run))
             return dealt
 
         def v_from_east(t, j0, width):
@@ -349,9 +350,9 @@ def tile_picked_grayscott_none_po_kernel(
         west_second = [v_on_scalar(2, 1, "west", "near2_west"), v_on_scalar(LAST, 1, "west", "near2_east")]
         woven_z2_first = weave_z2(0, HALF, True)
         east_last = v_on_scalar(LAST, 1, "east", "near3_east")
-        s34 = deal_on_gpsimd(w_scales_raw, U8, "partial3_0")
-        w4 = deal_on_gpsimd(w_raw[3], I32, "w_scales_raw")
-        w3 = deal_on_gpsimd(w_raw[2], I32, "w_raw3")
+        s34 = deal_on_gpsimd(w_scales_raw, U8, "partial3_0", 16)
+        w4 = deal_on_gpsimd(w_raw[3], I32, "w_scales_raw", 4)
+        w3 = deal_on_gpsimd(w_raw[2], I32, "w_raw3", 4)
         all_words = keep.tile([P, SLOTS, FEATURES // 2], F32, name="partial2_0", align_bytes=64)
         for h in range(2):
             turned[h] = bank(2 + h, [P, 2, 2, P])

@@ -350,10 +350,11 @@ def tile_picked_grayscott_none_po_kernel(
         west_second = [v_on_scalar(2, 1, "west", "near2_west"), v_on_scalar(LAST, 1, "west", "near2_east")]
         woven_z2_first = weave_z2(0, HALF, True)
         east_last = v_on_scalar(LAST, 1, "east", "near3_east")
-        s34 = deal_on_gpsimd(w_scales_raw, U8, "partial3_0", 16)
-        w4 = deal_on_gpsimd(w_raw[3], I32, "w_scales_raw", 4)
-        w3 = deal_on_gpsimd(w_raw[2], I32, "w_raw3", 4)
-        all_words = keep.tile([P, SLOTS, FEATURES // 2], F32, name="partial2_0", align_bytes=64)
+        w4 = keep.tile([P, FEATURES], I32, name="partial2_0", align_bytes=64)
+        deal(w4, w_raw[3], all_slots)
+        s34 = deal_on_gpsimd(w_scales_raw, U8, "w_raw3", 16)
+        w3 = deal_on_gpsimd(w_raw[2], I32, "w_scales_raw", 4)
+        all_words = keep.tile([P, SLOTS, FEATURES // 2], F32, name="partial3_0", align_bytes=64)
         for h in range(2):
             turned[h] = bank(2 + h, [P, 2, 2, P])
             turn_back(2 * h)

@@ -217,16 +217,20 @@ def tile_picked_grayscott_none_po_kernel(
 
         sums = [bank(4 + c, [P, SLOTS, P]) for c in range(SLOTS)]
 
-        def add_term(t, term, first=False, last=False):
-            for c in range(SLOTS):
+        def add_term(t, term, first=False, last=False, quarters=range(SLOTS)):
+            for c in quarters:
                 nc.tensor.matmul(sums[c][:, t, :], term[:, P * c : P * (c + 1)], ident[:], is_transpose=True, start=first, stop=last)
 
         lists = {"west": west_t, "east": east_t}
 
         def y_from(t, side, last=False):
             near = keep.tile([P, CELLS], F32, name="near%d_%s" % (t, side), align_bytes=64)
-            nc.scalar.activation(out=near[:], in_=y_windows[t][:].indirect(lists[side][:]), func=ACT.Copy, scale=2.0 / 3.0, bias=1.0 / 6.0)
-            add_term(t, near, last=last)
+            pieces = 2 if last else 1
+            for piece in range(pieces):
+                j0, j1 = CELLS * piece // pieces, CELLS * (piece + 1) // pieces
+                nc.scalar.activation(out=near[:, j0:j1], in_=y_windows[t][:].indirect(lists[side][:, j0 // LIST_ROWS : j1 // LIST_ROWS]),
+                                     func=ACT.Copy, scale=2.0 / 3.0, bias=1.0 / 6.0)
+                add_term(t, near, last=last, quarters=range(j0 // P, j1 // P))
 
         turned = {}
 

@@ -23,6 +23,7 @@ HALF = CELLS // 2
 LIST_ROWS = 16
 QUADRANTS = range(4)
 LINE = 4
+WORD_RUN, BYTE_RUN = 4, 16
 PARTS = 3
 
 
@@ -83,10 +84,10 @@ def tile_picked_grayscott_none_po_kernel(
             rows = slice(32 * q, 32 * q + 4)
             nc.vector.tensor_copy(out=x_scale_table[rows, :].bitcast(I32), in_=x_scale_rows[rows, :].bitcast(I32))
 
-        def deal(dealt, raw, slots):
-            nc.vector.tensor_copy(
-                out=dealt[:].rearrange("p (t m) -> p m t", t=SLOTS)[:, :, slots],
-                in_=raw[:].rearrange("p (m t) -> p m t", t=SLOTS)[:, :, slots],
+        def deal(dealt, raw, slots, run, copy=nc.vector.tensor_copy):
+            copy(
+                out=dealt[:].rearrange("p (t c i) -> p c t i", t=SLOTS, i=run)[:, :, slots, :],
+                in_=raw[:].rearrange("p (c i t) -> p c t i", t=SLOTS, i=run)[:, :, slots, :],
             )
 
         x_scale = keep.tile([P, CELLS], U8, name="x_scale", align_bytes=64)
@@ -103,13 +104,13 @@ def tile_picked_grayscott_none_po_kernel(
         w2 = keep.tile([P, FEATURES], I32, name="w2", align_bytes=64)
         first_slot, other_slots, all_slots = slice(0, 1), slice(1, SLOTS), slice(0, SLOTS)
         pick(0, "x_codes_first")
-        deal(s12_first, w_scales_raw, first_slot)
-        deal(w1, w_raw[0], all_slots)
+        deal(s12_first, w_scales_raw, first_slot, BYTE_RUN)
+        deal(w1, w_raw[0], all_slots, WORD_RUN)
         pick(1, "w_raw0")
-        deal(w2, w_raw[1], first_slot)
-        deal(w2, w_raw[1], other_slots)
+        deal(w2, w_raw[1], first_slot, WORD_RUN)
+        deal(w2, w_raw[1], other_slots, WORD_RUN)
         s12_others = keep.tile([P, FEATURES], U8, name="w_raw1", align_bytes=64)
-        deal(s12_others, w_scales_raw, other_slots)
+        deal(s12_others, w_scales_raw, other_slots, BYTE_RUN)
         load_scale_rows(nc.sync, w_scales_raw, 8, w3_scales, QUADRANTS)
         load_scale_rows(nc.sync, w_scales_raw, 12, w4_scales, QUADRANTS)
         nc.sync.dma_start(out=g1_all[:], in_=g1.rearrange("f o -> (f o)").partition_broadcast(P))
@@ -203,12 +204,6 @@ def tile_picked_grayscott_none_po_kernel(
         def add_east(t, h, near):
             j0 = HALF * h
             nc.vector.tensor_tensor(z2_rows[:, CELLS * t + j0 : CELLS * t + j0 + HALF], near[:], partials[(t, j0)], ALU.add)
-
-        def deal_on_gpsimd(raw, dtype, name, run):
-            dealt = keep.tile([P, FEATURES], dtype, name=name, align_bytes=64)
-            nc.gpsimd.tensor_copy(out=dealt[:].rearrange("p (t c i) -> p c t i", t=SLOTS, i=run),
-                                  in_=raw[:].rearrange("p (c i t) -> p c t i", t=SLOTS, i=run))
-            return dealt
 
         def v_from_east(t, j0, width):
             entries = slice(j0 // LIST_ROWS, (j0 + width) // LIST_ROWS)
@@ -355,9 +350,11 @@ def tile_picked_grayscott_none_po_kernel(
         woven_z2_first = weave_z2(0, HALF, True)
         east_last = v_on_scalar(LAST, 1, "east", "near3_east")
         w4 = keep.tile([P, FEATURES], I32, name="partial2_0", align_bytes=64)
-        deal(w4, w_raw[3], all_slots)
-        s34 = deal_on_gpsimd(w_scales_raw, U8, "w_raw3", 16)
-        w3 = deal_on_gpsimd(w_raw[2], I32, "w_scales_raw", 4)
+        deal(w4, w_raw[3], all_slots, WORD_RUN)
+        s34 = keep.tile([P, FEATURES], U8, name="w_raw3", align_bytes=64)
+        deal(s34, w_scales_raw, all_slots, BYTE_RUN, nc.gpsimd.tensor_copy)
+        w3 = keep.tile([P, FEATURES], I32, name="w_scales_raw", align_bytes=64)
+        deal(w3, w_raw[2], all_slots, WORD_RUN, nc.gpsimd.tensor_copy)
         all_words = keep.tile([P, SLOTS, FEATURES // 2], F32, name="partial3_0", align_bytes=64)
         for h in range(2):
             turned[h] = bank(2 + h, [P, 2, 2, P])

from contextlib import ExitStack

import concourse.mybir as mybir
from concourse.masks import make_identity

TABLE, CELLS, FEATURES = 2048, 512, 512
FLOPS = 4 * 2 * 512 * 512 * 512

F32 = mybir.dt.float32
BF16 = mybir.dt.bfloat16
I32 = mybir.dt.int32
U32 = mybir.dt.uint32
U16 = mybir.dt.uint16
U8 = mybir.dt.uint8
FP8X4 = mybir.dt.float8_e4m3fn_x4
ALU = mybir.AluOpType
ACT = mybir.ActivationFunctionType

P = 128
SLOTS = 4
LAST = SLOTS - 1
HALF = CELLS // 2
LIST_ROWS = 16
QUADRANTS = range(4)
LINE = 4
WORD_RUN, BYTE_RUN = 4, 16
PARTS = 3


def tile_picked_grayscott_none_po_kernel(
    tc, x_words, x_scales, w1_words, w1_scales, w2_words, w2_scales, g1, g2,
    w3_words, w3_scales, w4_words, w4_scales, offs, west, east, out_0, out_1, out_2,
):
    nc = tc.nc

    def words_of(dram):
        return dram[0].rearrange("p n t -> p (n t)").bitcast(I32)

    def load_scale_rows(queue, tile, first_row, dram, quadrants):
        for q in quadrants:
            r = 32 * q + first_row
            queue.dma_start(out=tile[r : r + 4, :].bitcast(I32), in_=dram[0, 4 * q : 4 * q + 4, :].bitcast(I32))

    with ExitStack() as ctx:
        keep = ctx.enter_context(tc.tile_pool(name="keep", bufs=1))
        ring = ctx.enter_context(tc.tile_pool(name="ring", bufs=2))
        psum = ctx.enter_context(tc.psum_pool(name="psum", bufs=1))

        def bank(number, shape):
            return psum.tile(shape, F32, name="bank%d" % number)

        offs_t = keep.tile([P, CELLS // LIST_ROWS], U16, name="offs_t")
        west_t = keep.tile([P, CELLS // LIST_ROWS], U16, name="west_t")
        east_t = keep.tile([P, CELLS // LIST_ROWS], U16, name="east_t")
        x_table = keep.tile([P, TABLE], I32, name="x_table", align_bytes=64)
        x_scale_table = keep.tile([P, TABLE], U8, name="x_scale_table", align_bytes=64)
        w_scales_raw = keep.tile([P, FEATURES], U8, name="w_scales_raw", align_bytes=64)
        g1_all = keep.tile([P, FEATURES], F32, name="g1_all")
        g2_t = keep.tile([P, SLOTS], F32, name="g2_t")
        x_scale_rows = keep.tile([P, TABLE], U8, name="x_scale_rows", align_bytes=64)
        w_raw = [keep.tile([P, FEATURES], I32, name="w_raw%d" % i, align_bytes=64) for i in range(4)]
        ident = keep.tile([P, P], F32, name="ident")

        nc.gpsimd.memset(w_scales_raw[:].bitcast(I32), 0)
        nc.vector.memset(x_scale_table[:].bitcast(I32), 0)

        nc.sync.dma_start(offs_t[:], offs)
        load_scale_rows(nc.scalar, x_scale_rows, 0, x_scales, QUADRANTS[:2])
        load_scale_rows(nc.sync, x_scale_rows, 0, x_scales, QUADRANTS[2:])
        load_scale_rows(nc.scalar, w_scales_raw, 0, w1_scales, QUADRANTS[:1])
        load_scale_rows(nc.sync, w_scales_raw, 0, w1_scales, QUADRANTS[1:2])
        nc.sync.dma_start(out=x_table[:], in_=words_of(x_words))
        load_scale_rows(nc.sync, w_scales_raw, 0, w1_scales, QUADRANTS[2:])
        load_scale_rows(nc.sync, w_scales_raw, 4, w2_scales, QUADRANTS)
        nc.sync.dma_start(out=w_raw[0][:], in_=words_of(w1_words))
        nc.sync.dma_start(out=w_raw[1][:], in_=words_of(w2_words))
        make_identity(nc, ident[:])
        nc.sync.dma_start(out=w_raw[2][:], in_=words_of(w3_words))
        nc.sync.dma_start(out=w_raw[3][:], in_=words_of(w4_words))
        nc.sync.dma_start(out=g2_t[:], in_=g2.rearrange("(p t) o -> p (t o)", t=SLOTS))
        nc.sync.dma_start(west_t[:], west)
        nc.sync.dma_start(east_t[:], east)
        for q in QUADRANTS:
            rows = slice(32 * q, 32 * q + 4)
            nc.vector.tensor_copy(out=x_scale_table[rows, :].bitcast(I32), in_=x_scale_rows[rows, :].bitcast(I32))

        def deal(dealt, raw, slots, run, copy=nc.vector.tensor_copy):
            copy(
                out=dealt[:].rearrange("p (t c i) -> p c t i", t=SLOTS, i=run)[:, :, slots, :],
                in_=raw[:].rearrange("p (c i t) -> p c t i", t=SLOTS, i=run)[:, :, slots, :],
            )

        x_scale = keep.tile([P, CELLS], U8, name="x_scale", align_bytes=64)
        nc.vector.tensor_copy(out=x_scale[:], in_=x_scale_table[:].indirect(offs_t[:]))
        x_codes = []

        def pick(h, name):
            entries = slice(HALF * h // LIST_ROWS, HALF * (h + 1) // LIST_ROWS)
            x_codes.append(keep.tile([P, HALF], U32, name=name, align_bytes=64))
            nc.vector.tensor_copy(out=x_codes[h][:], in_=x_table[:].bitcast(U32).indirect(offs_t[:, entries]))

        s12_first = keep.tile([P, FEATURES], U8, name="s12_first", align_bytes=64)
        w1 = keep.tile([P, FEATURES], I32, name="w1", align_bytes=64)
        w2 = keep.tile([P, FEATURES], I32, name="w2", align_bytes=64)
        first_slot, other_slots, all_slots = slice(0, 1), slice(1, SLOTS), slice(0, SLOTS)
        pick(0, "x_codes_first")
        deal(s12_first, w_scales_raw, first_slot, BYTE_RUN)
        deal(w1, w_raw[0], all_slots, WORD_RUN)
        pick(1, "w_raw0")
        deal(w2, w_raw[1], first_slot, WORD_RUN)
        deal(w2, w_raw[1], other_slots, WORD_RUN)
        s12_others = keep.tile([P, FEATURES], U8, name="w_raw1", align_bytes=64)
        deal(s12_others, w_scales_raw, other_slots, BYTE_RUN)
        load_scale_rows(nc.sync, w_scales_raw, 8, w3_scales, QUADRANTS)
        load_scale_rows(nc.sync, w_scales_raw, 12, w4_scales, QUADRANTS)
        nc.sync.dma_start(out=g1_all[:], in_=g1.rearrange("f o -> (f o)").partition_broadcast(P))

        def first_product(acc, w, first_row, t, j0, width):
            cols = slice(P * t, P * (t + 1))
            s12 = s12_first if t == 0 else s12_others
            for c0 in range(0, width, HALF):
                cells = slice(j0 + c0, j0 + c0 + HALF)
                nc.tensor.matmul_mx(out=acc[:, c0 : c0 + HALF], lhsT=w[:, cols].bitcast(FP8X4), lhsT_scale=s12[first_row:P, cols],
                                    rhs=x_codes[(j0 + c0) // HALF][:].bitcast(FP8X4), rhs_scale=x_scale[:, cells],
                                    start=True, stop=True)

        y_windows = [keep.tile([P, 2 * CELLS], F32, name="y_window%d" % t) for t in range(SLOTS)]
        ys = [window[:, 0:CELLS] for window in y_windows]
        es = [y_windows[t][:, CELLS:] for t in (1, 0, 2, LAST)]
        v_windows, ye8s = [], []
        for t in range(SLOTS):
            if t < 2:
                v_windows.append(keep.tile([P, 2 * CELLS], F32, name="v_window%d" % t, align_bytes=64))
                ye8s.append(v_windows[t][:, CELLS:])
            else:
                v_windows.append(keep.tile([P, CELLS], F32, name="v_window%d" % t, align_bytes=64))
                ye8s.append(keep.tile([P, CELLS], F32, name="ye8_%d" % t, align_bytes=64)[:])
        y_terms = [keep.tile([P, CELLS], F32, name="y_term%d" % t, align_bytes=64) for t in range(SLOTS)]
        v_terms = [keep.tile([P, CELLS], F32, name="v_term%d" % t) for t in range(SLOTS)]

        Y_BANKS, E_BANKS = (None, 0, 2, 0), (None, 1, 3, 1)

        def concentrations(t):
            if t == 0:
                for h in range(2):
                    cells = slice(HALF * h, HALF * (h + 1))
                    half_y = bank(2 * h, [P, HALF])
                    first_product(half_y[:], w1, 0, t, HALF * h, HALF)
                    nc.scalar.activation(out=ys[t][:, cells], in_=half_y[:], func=ACT.Sigmoid)
                    half_e = bank(2 * h + 1, [P, HALF])
                    first_product(half_e[:], w2, 4, t, HALF * h, HALF)
                    nc.scalar.activation(out=es[t][:, cells], in_=half_e[:], func=ACT.Sigmoid)
                return
            nc.scalar.activation(out=ys[t], in_=logits[t][0][:], func=ACT.Sigmoid)
            nc.scalar.activation(out=es[t], in_=logits[t][1][:], func=ACT.Sigmoid)

        def weigh_on_scalar(t):
            nc.scalar.activation(out=v_windows[t][:, 0:CELLS], in_=es[t], func=ACT.Copy, scale=g2_t[:, t : t + 1])

        logits = {}

        def first_products(t):
            logits[t] = (bank(Y_BANKS[t], [P, CELLS]), bank(E_BANKS[t], [P, CELLS]))
            first_product(logits[t][0][:], w1, 0, t, 0, CELLS)
            first_product(logits[t][1][:], w2, 4, t, 0, CELLS)

        def weigh(t, j0=0, width=CELLS):
            cells = slice(j0, j0 + width)
            nc.vector.tensor_scalar_mul(out=v_windows[t][:, cells], in0=es[t][:, cells], scalar1=g2_t[:, t : t + 1])

        def product_term(t, j0=0, width=CELLS):
            cells = slice(j0, j0 + width)
            nc.vector.scalar_tensor_tensor(out=ye8s[t][:, cells], in0=ys[t][:, cells], scalar=8.0, in1=es[t][:, cells],
                                           op0=ALU.mult, op1=ALU.mult)

        def own_e_term(t, j0=0, width=CELLS):
            cells = slice(j0, j0 + width)
            nc.vector.scalar_tensor_tensor(out=v_terms[t][:, cells], in0=ye8s[t][:, cells], scalar=4.0, in1=v_windows[t][:, cells],
                                           op0=ALU.add, op1=ALU.mult)

        def own_y_term(t):
            nc.vector.scalar_tensor_tensor(out=y_terms[t][:], in0=ye8s[t], scalar=-1.0 / 3.0, in1=es[t], op0=ALU.mult, op1=ALU.mult)

        z2_rows = keep.tile([P, SLOTS * CELLS], F32, name="z2_rows")
        partials = {}

        def v_from_west(t, j0, width):
            entries = slice(j0 // LIST_ROWS, (j0 + width) // LIST_ROWS)
            partials[(t, j0)] = keep.tile([P, width], F32, name="partial%d_%d" % (t, j0), align_bytes=64)[:]
            nc.vector.tensor_tensor(partials[(t, j0)], v_windows[t][:].indirect(west_t[:, entries]),
                                    v_terms[t][:, j0 : j0 + width], ALU.add)

        def v_on_scalar(t, h, side, name):
            near = keep.tile([P, HALF], F32, name=name, align_bytes=64)
            entries = slice(HALF * h // LIST_ROWS, HALF * (h + 1) // LIST_ROWS)
            nc.scalar.activation(out=near[:], in_=v_windows[t][:].indirect(lists[side][:, entries]), func=ACT.Copy)
            return near

        def add_west(t, h, near, partial):
            j0 = HALF * h
            nc.vector.tensor_tensor(partial, near[:], v_terms[t][:, j0 : j0 + HALF], ALU.add)
            partials[(t, j0)] = partial

        def add_east(t, h, near):
            j0 = HALF * h
            nc.vector.tensor_tensor(z2_rows[:, CELLS * t + j0 : CELLS * t + j0 + HALF], near[:], partials[(t, j0)], ALU.add)

        def v_from_east(t, j0, width):
            entries = slice(j0 // LIST_ROWS, (j0 + width) // LIST_ROWS)
            nc.vector.tensor_tensor(z2_rows[:, CELLS * t + j0 : CELLS * t + j0 + width],
                                    v_windows[t][:].indirect(east_t[:, entries]), partials[(t, j0)][:, 0:width], ALU.add)

        sums = [bank(4 + c, [P, SLOTS, P]) for c in range(SLOTS)]

        def add_term(t, term, first=False, last=False, quarters=range(SLOTS)):
            for c in quarters:
                nc.tensor.matmul(sums[c][:, t, :], term[:, P * c : P * (c + 1)], ident[:], is_transpose=True, start=first, stop=last)

        lists = {"west": west_t, "east": east_t}

        def y_from(t, side, last=False):
            near = keep.tile([P, CELLS], F32, name="near%d_%s" % (t, side), align_bytes=64)
            pieces = 2 if last else 1
            for piece in range(pieces):
                j0, j1 = CELLS * piece // pieces, CELLS * (piece + 1) // pieces
                nc.scalar.activation(out=near[:, j0:j1], in_=y_windows[t][:].indirect(lists[side][:, j0 // LIST_ROWS : j1 // LIST_ROWS]),
                                     func=ACT.Copy, scale=2.0 / 3.0, bias=1.0 / 6.0)
                add_term(t, near, last=last, quarters=range(j0 // P, j1 // P))

        turned = {}

        def turn_back(c):
            words = all_words[:, c, :]
            nc.vector.scalar_tensor_tensor(
                out=words.bitcast(BF16).rearrange("j (p t) -> j p t", t=SLOTS),
                in0=sums[c][:].rearrange("j t p -> j p t"), scalar=0.375,
                in1=g1_all[:].rearrange("j (p t) -> j p t", t=SLOTS), op0=ALU.mult, op1=ALU.mult,
            )
            h, i = divmod(c, 2)
            for u in range(2):
                nc.tensor.transpose(turned[h][:, i, u, :], words[:, u::2], ident[:])

        out_rows = out_0.rearrange("(p t) j -> p t j", t=SLOTS)
        out_codes = keep.tile([P, CELLS], I32, name="out_codes", align_bytes=64)
        out_scale = keep.tile([P, CELLS], U8, name="out_scale", align_bytes=64)

        def quantise(woven, width, name):
            codes = ring.tile([P, width], U32, name=name + "_codes", align_bytes=64, bufs=PARTS)
            scale = ring.tile([P, width], U8, name=name + "_scale", align_bytes=64, bufs=PARTS)
            nc.vector.quantize_mx(out=codes[:].bitcast(FP8X4), scales=scale[:], in_=woven)
            return codes[:], scale[:]

        def weave_z2(j0, width, on_scalar):
            rows = z2_rows[:].rearrange("p (t j) -> p j t", t=SLOTS)[:, j0 : j0 + width, :]
            woven = keep.tile([P, width, SLOTS], BF16, name="z2_woven%d" % j0, align_bytes=64)
            dst = woven[:].rearrange("p (c i) t -> p c t i", i=LINE)
            src = rows.rearrange("p (c i) t -> p c t i", i=LINE)
            if on_scalar:
                nc.scalar.activation(out=dst, in_=src, func=ACT.Copy, scale=0.125)
            else:
                nc.vector.tensor_scalar_mul(out=dst, in0=src, scalar1=0.125)
            return woven[:].rearrange("p j t -> p (j t)")

        def weave_z(h):
            woven = ring.tile([P, HALF * SLOTS], BF16, name="z_woven", align_bytes=64)
            nc.scalar.copy(
                out=woven[:].bitcast(F32).rearrange("p (q j u) -> p q j u", u=2, j=P),
                in_=turned[h][:].rearrange("p q u j -> p q j u"),
            )
            return woven[:]

        def last_passes(accs, w, first_row, codes, scale, start):
            per_bank = SLOTS // len(accs)
            for t in range(SLOTS):
                cols = slice(P * t, P * (t + 1))
                b, r = divmod(t, per_bank)
                nc.tensor.matmul_mx(out=accs[b][:, r, :], lhsT=w[:, cols].bitcast(FP8X4), lhsT_scale=s34[first_row:P, cols],
                                    rhs=codes.bitcast(FP8X4), rhs_scale=scale,
                                    start=start and r == 0, stop=not start and r == per_bank - 1)

        def store_result(j0, width, accs, copies=(nc.scalar.copy, nc.scalar.copy)):
            result = ring.tile([P, SLOTS, width], F32, name="result", bufs=PARTS)
            per_bank = SLOTS // len(accs)
            for b, acc in enumerate(accs):
                copies[b](out=result[:, per_bank * b : per_bank * (b + 1), :], in_=acc[:])
            nc.sync.dma_start(out=out_rows[:, :, j0 : j0 + width], in_=result[:])
            return result

        def weave_result(width, result, copy=nc.vector.tensor_copy):
            woven = ring.tile([P, width, SLOTS], BF16, name="out_woven", align_bytes=64, bufs=PARTS)
            copy(out=woven[:].rearrange("p (c i) t -> p c t i", i=LINE),
                 in_=result[:].rearrange("p t (c i) -> p c t i", i=LINE))
            return woven[:].rearrange("p j t -> p (j t)")

        def quantise_result(j0, width, woven):
            cells = slice(j0, j0 + width)
            nc.vector.quantize_mx(out=out_codes[:, cells].bitcast(FP8X4), scales=out_scale[:, cells], in_=woven)

        def store_codes(cells):
            nc.sync.dma_start(out=words_of(out_1)[:, cells], in_=out_codes[:, cells])

        concentrations(0)
        for j0 in (0, HALF):
            weigh(0, j0, HALF)
            product_term(0, j0, HALF)
        first_products(1)
        concentrations(1)
        weigh_on_scalar(1)
        first_products(2)
        first_products(LAST)
        add_term(0, ys[0], first=True)
        add_term(1, ys[1])
        own_e_term(0, 0, HALF)
        own_e_term(0, HALF, HALF)
        own_y_term(0)
        add_term(0, y_terms[0])
        v_from_west(0, 0, CELLS)
        y_from(0, "west")
        y_from(0, "east")

        concentrations(2)
        add_term(2, ys[2])
        product_term(1)
        v_from_east(0, 0, CELLS)
        own_e_term(1)
        own_y_term(1)
        add_term(1, y_terms[1])
        v_from_west(1, 0, CELLS)
        y_from(1, "west")
        weigh_on_scalar(2)
        y_from(1, "east")

        concentrations(LAST)
        add_term(LAST, ys[LAST])
        product_term(2)
        v_from_east(1, 0, CELLS)
        product_term(LAST)
        weigh(LAST)
        for t in (2, LAST):
            own_y_term(t)
        for step in (own_e_term, lambda t: v_from_west(t, 0, HALF), lambda t: v_from_east(t, 0, HALF)):
            step(2)
            step(LAST)
        for t, side in ((2, "west"), (LAST, "east")):
            y_from(2, side)
            add_term(t, y_terms[t])
        y_from(LAST, "west")
        y_from(LAST, "east", last=True)
        west_second = [v_on_scalar(2, 1, "west", "near2_west"), v_on_scalar(LAST, 1, "west", "near2_east")]
        woven_z2_first = weave_z2(0, HALF, True)
        east_last = v_on_scalar(LAST, 1, "east", "near3_east")
        w4 = keep.tile([P, FEATURES], I32, name="partial2_0", align_bytes=64)
        deal(w4, w_raw[3], all_slots, WORD_RUN)
        s34 = keep.tile([P, FEATURES], U8, name="w_raw3", align_bytes=64)
        deal(s34, w_scales_raw, all_slots, BYTE_RUN, nc.gpsimd.tensor_copy)
        w3 = keep.tile([P, FEATURES], I32, name="w_scales_raw", align_bytes=64)
        deal(w3, w_raw[2], all_slots, WORD_RUN, nc.gpsimd.tensor_copy)
        all_words = keep.tile([P, SLOTS, FEATURES // 2], F32, name="partial3_0", align_bytes=64)
        for h in range(2):
            turned[h] = bank(2 + h, [P, 2, 2, P])
            turn_back(2 * h)
            turn_back(2 * h + 1)
        woven_z = [weave_z(0)]

        quarters = (HALF, HALF + P)
        first_accs = [bank(4, [P, 2, HALF]), bank(5, [P, 2, HALF])]
        late_accs = [[bank(0, [P, SLOTS, P])], [bank(1, [P, 2, P]), bank(6, [P, 2, P])]]
        last_passes(first_accs, w4, 12, *quantise(woven_z2_first, HALF, "z2"), True)
        east_third = v_on_scalar(2, 1, "east", "z2_woven0")
        woven_z.append(weave_z(1))
        last_passes(first_accs, w3, 8, *quantise(woven_z[0], HALF, "z"), False)
        result_first = store_result(0, HALF, first_accs)
        late_partials = keep.tile([P, 2, HALF], F32, name="g1_all")
        add_west(LAST, 1, west_second[1], late_partials[:, 1, :])
        add_west(2, 1, west_second[0], late_partials[:, 0, :])
        add_east(LAST, 1, east_last)
        add_east(2, 1, east_third)
        z_codes, z_scale = quantise(woven_z[1], HALF, "z")
        for i in range(2):
            last_passes(late_accs[i], w3, 8, z_codes[:, P * i : P * (i + 1)], z_scale[:, P * i : P * (i + 1)], True)
        woven_z2 = [weave_z2(j0, P, False) for j0 in quarters]
        for i in range(2):
            last_passes(late_accs[i], w4, 12, *quantise(woven_z2[i], P, "z2"), False)
        woven_first = weave_result(HALF, result_first)
        quantise_result(0, HALF, woven_first)
        store_codes(slice(0, HALF))
        results_late = [store_result(quarters[0], P, late_accs[0]),
                        store_result(quarters[1], P, late_accs[1], (nc.vector.tensor_copy, nc.scalar.copy))]
        woven_late = [weave_result(P, result) for result in results_late]
        for j0, woven in zip(quarters, woven_late):
            quantise_result(j0, P, woven)
        store_codes(slice(HALF, CELLS))
        for q, queue in zip(QUADRANTS, (nc.scalar, nc.scalar, nc.sync, nc.sync)):
            queue.dma_start(out=out_2[0, 4 * q : 4 * q + 4, :].bitcast(I32), in_=out_scale[32 * q : 32 * q + 4, :].bitcast(I32))
